import numpy as np
import ml_dtypes


def mxq(x, axis, fmt="e4m3"):
    dtype, down = {"e4m3": (ml_dtypes.float8_e4m3fn, 7), "e5m2": (ml_dtypes.float8_e5m2, 14)}[fmt]
    v = np.moveaxis(np.asarray(x, np.float32).astype(ml_dtypes.bfloat16).astype(np.float64), axis, -1)
    blocks = v.reshape(v.shape[:-1] + (-1, 32))
    amax = np.abs(blocks).max(-1, keepdims=True)
    byte = np.maximum(np.where(amax > 0, np.frexp(amax)[1] - 1 + 127, 0) - down, 1)
    scale = np.exp2(byte - 127.0)
    codes = (blocks / scale).astype(np.float32).astype(dtype).astype(np.float64)
    return np.moveaxis((codes * scale).reshape(v.shape), -1, axis)


WIDE = False


def mx_kscale(k):
    if not WIDE:
        return np.ones(k)
    levels = np.array([10, -10, 5, -5, 0])
    if k % 512:
        return np.exp2(np.random.permutation(np.resize(levels, k // 32))).repeat(32)
    a = np.empty((k // 512, 16))
    for p in range(k // 512):
        a[p, :8] = np.random.permutation(np.resize(levels, 8))
        for g in range(8):
            far = levels[np.abs(levels - a[p, g]) >= 10]
            a[p, g + 8] = far[np.random.randint(len(far))]
    return np.exp2(a.ravel()).repeat(32)


def f64(x):
    return np.asarray(x).astype(np.float64)


def striped(idx):
    return np.tile(idx.reshape(-1, 16).T, (8, 1)).astype(np.uint16)


def unstriped(offs):
    return offs[:16].T.reshape(-1).astype(np.int64)


E2M1 = np.array([0.0, 0.5, 1.0, 1.5, 2.0, 3.0, 4.0, 6.0, -0.0, -0.5, -1.0, -1.5, -2.0, -3.0, -4.0, -6.0])


def pack_weight(w, fmt):
    k, n = w.shape
    w = f64(np.asarray(w, np.float32).astype(ml_dtypes.bfloat16)).reshape(k // 32, 32, n)
    amax = np.abs(w).max(1)
    if fmt == "e4m3":
        byte = np.frexp(amax)[1] - 1 + 127 - 7
    else:
        mant, ex = np.frexp(amax / 6.0)
        byte = np.where(mant > 0.5, ex, ex - 1) + 127
    byte = np.clip(np.where(amax > 0, byte, 1), 1, 254)
    scaled = (w * np.exp2(127.0 - byte)[:, None, :]).reshape(k, n).astype(np.float32)
    by_word = np.ascontiguousarray(scaled.reshape(k // 512, 128, 4, n).transpose(0, 1, 3, 2))
    if fmt == "e4m3":
        words = by_word.astype(ml_dtypes.float8_e4m3fn).view(np.uint8)
    else:
        c = by_word.astype(ml_dtypes.float4_e2m1fn).view(np.uint8) & 0xF
        words = (c[..., 0::2] | (c[..., 1::2] << 4)).reshape(k // 512, 128, 2 * n)
    return np.ascontiguousarray(words), np.ascontiguousarray(byte.astype(np.uint8).reshape(k // 512, 16, n))


def unpack_weight(words, scales, fmt):
    g, _, n = scales.shape
    words = np.ascontiguousarray(words).reshape(g, 128, n, -1)
    if fmt == "e4m3":
        vals = words.view(ml_dtypes.float8_e4m3fn).astype(np.float64)
    else:
        nib = np.empty((g, 128, n, 4), np.uint8)
        nib[..., 0::2] = words & 0xF
        nib[..., 1::2] = words >> 4
        vals = E2M1[nib]
    vals = vals * np.repeat(np.exp2(scales.astype(np.float64) - 127.0), 8, axis=1)[..., None]
    return vals.transpose(0, 1, 3, 2).reshape(g * 512, n)


def gelu(v):
    return 0.5 * v * (1.0 + np.tanh(np.sqrt(2.0 / np.pi) * (v + 0.044715 * v**3)))


def bf(x):
    return np.asarray(x, np.float32).astype(ml_dtypes.bfloat16)

def planes(Y):
    n, m = Y.shape
    b = f64(bf(Y)).reshape(n // 32, 32, m)
    amax = np.abs(b).max(1)
    byte = np.clip(np.where(amax > 0, np.frexp(amax)[1] - 1 + 127 - 7, 1), 1, 254)
    codes = (b * np.exp2(127.0 - byte)[:, None, :]).reshape(n, m).astype(np.float32).astype(ml_dtypes.float8_e4m3fn).view(np.uint8)
    words = codes.reshape(n // 512, 128, 4, m).transpose(0, 1, 3, 2)
    return np.ascontiguousarray(words), np.ascontiguousarray(byte.astype(np.uint8).reshape(n // 512, 16, m))


K, T, S, H, N = 512, 2048, 1024, 1024, 512

def setup_inputs():
    n = np.random.standard_normal
    s = mx_kscale(K)[:, None]
    u = mx_kscale(H)[:, None]
    spread = np.exp(0.8 * n(N))
    tab_words, tab_scales = pack_weight(n((K, T)) * s, "e4m3")
    w2_words, w2_scales = pack_weight(n((K, H)) / np.sqrt(K) / s, "e2m1")
    w3_words, w3_scales = pack_weight(n((K, H)) / np.sqrt(K) / s, "e4m3")
    return {
        "tab_words": tab_words, "tab_scales": tab_scales,
        "offs": striped(np.random.permutation(T)[:S]),
        "offs2": striped(np.random.permutation(T)[:S]),
        "offs3": striped(np.random.permutation(T)[:S]),
        "w1": (n((K, H)) / np.sqrt(K) / s).astype(np.float32),
        "w2_words": w2_words, "w2_scales": w2_scales,
        "w3_words": w3_words, "w3_scales": w3_scales,
        "gain": (np.exp(0.3 * n(H)) * u[:, 0]).astype(np.float32),
        "wf": (n((H, N)) / np.sqrt(H) * spread / u).astype(np.float32),
        "bf": (0.5 * n(N) * spread).astype(np.float32),
    }

def reference(tab_words, tab_scales, offs, offs2, offs3, w1, w2_words, w2_scales, w3_words, w3_scales, gain, wf, bf):
    v = unpack_weight(tab_words, tab_scales, "e4m3")[:, unstriped(offs)]
    vb = unpack_weight(tab_words, tab_scales, "e4m3")[:, unstriped(offs2)]
    vc = unpack_weight(tab_words, tab_scales, "e4m3")[:, unstriped(offs3)]
    a = mxq(f64(w1), 0, "e4m3").T @ v
    b = unpack_weight(w2_words, w2_scales, "e2m1").T @ vb
    c = unpack_weight(w3_words, w3_scales, "e4m3").T @ vc
    m = np.maximum(np.maximum(a, b), c)
    h = m / (1.0 + np.exp(-m)) * f64(gain)[:, None]
    y = (mxq(f64(wf), 0, "e4m3").T @ mxq(h, 0, "e4m3")) + f64(bf)[:, None]
    words, scales = planes(y)
    return y, words, scales

@@ -1,0 +1,238 @@
+from contextlib import ExitStack
+
+import concourse.mybir as mybir
+
+K, T, S, H, N = 512, 2048, 1024, 1024, 512
+FLOPS = 2 * S * (3 * K * H + H * N)
+
+F32 = mybir.dt.float32
+BF16 = mybir.dt.bfloat16
+I32 = mybir.dt.int32
+U32 = mybir.dt.uint32
+U16 = mybir.dt.uint16
+U8 = mybir.dt.uint8
+FP8X4 = mybir.dt.float8_e4m3fn_x4
+FP4X4 = mybir.dt.float4_e2m1fn_x4
+ACT = mybir.ActivationFunctionType
+ALU = mybir.AluOpType
+
+P = 128
+PACK = 4
+PASS = P * PACK
+GROUPS = H // PASS
+QUADS = 4
+CHUNK = 256
+UNIT = 128
+ALIGN = 64
+
+
+def tile_list_opcode_trigram_families_kernel(
+    tc, tab_words, tab_scales, offs, offs2, offs3, w1, w2_words, w2_scales, w3_words, w3_scales, gain, wf, bf,
+    out_0, out_1, out_2,
+):
+    nc = tc.nc
+    with ExitStack() as ctx:
+        held = ctx.enter_context(tc.tile_pool(name="held", bufs=1))
+        picked = ctx.enter_context(tc.tile_pool(name="picked", bufs=2))
+        work = ctx.enter_context(tc.tile_pool(name="work", bufs=3))
+        psum = ctx.enter_context(tc.psum_pool(name="psum", bufs=2))
+
+        table_scales = held.tile([P, T], U8, name="table_scales", align_bytes=ALIGN)
+        nc.vector.memset(table_scales[:].bitcast(I32), 0)
+        raw_scales = held.tile([P, 2 * H], U8, name="raw_scales", align_bytes=ALIGN)
+        nc.vector.memset(raw_scales[:].bitcast(I32), 0)
+
+        def load_scale_rows(dst, rows):
+            for q in range(QUADS):
+                nc.scalar.dma_start(out=dst[32 * q : 32 * q + 4, :].bitcast(I32), in_=rows[4 * q : 4 * q + 4, :].bitcast(I32))
+
+        lists = [held.tile([P, S // 16], U16, name=f"list{i}") for i in range(3)]
+        nc.sync.dma_start(lists[0][:], offs)
+        load_scale_rows(table_scales[:], tab_scales[0])
+        table_words = held.tile([P, T], I32, name="table_words", align_bytes=ALIGN)
+        nc.sync.dma_start(out=table_words[:], in_=tab_words[0].rearrange("p t i -> p (t i)").bitcast(I32))
+        nc.sync.dma_start(lists[1][:], offs2)
+        nc.sync.dma_start(lists[2][:], offs3)
+
+        w1_rows = w1.rearrange("(p j) r -> p j r", j=PACK)
+        w1_raw = [held.tile([P, PACK, PASS], F32, name=f"w1_raw{g}") for g in range(GROUPS)]
+        w2_raw = held.tile([P, H // 2], I32, name="w2_raw")
+        w3_raw = held.tile([P, H], I32, name="w3_raw")
+        load_scale_rows(raw_scales[:, :H], w2_scales[0])
+        nc.sync.dma_start(out=w1_raw[0][:], in_=w1_rows[:, :, 0:PASS])
+        nc.sync.dma_start(out=w2_raw[:], in_=w2_words[0].bitcast(I32))
+        nc.sync.dma_start(out=w3_raw[:], in_=w3_words[0].rearrange("p e i -> p (e i)").bitcast(I32))
+        load_scale_rows(raw_scales[:, H:], w3_scales[0])
+        nc.sync.dma_start(out=w1_raw[1][:], in_=w1_rows[:, :, PASS : 2 * PASS])
+
+        gains = held.tile([P, GROUPS, 16], F32, name="gains")
+        gain_runs = gain.rearrange("(g u e) -> u g e", g=GROUPS, e=16)
+        for v in range(4):
+            nc.sync.dma_start(out=gains[v:P:4, :, 0:13], in_=gain_runs[:, :, v : v + 13])
+        wf_rows = wf.rearrange("(g u t v) n -> g v u t n", g=GROUPS, t=PACK, v=4)
+        wf_raw = [held.tile([P, PACK, N], F32, name=f"wf_raw{g}") for g in range(GROUPS)]
+        for g in range(GROUPS):
+            for v in range(4):
+                nc.sync.dma_start(out=wf_raw[g][v:P:4, :, :], in_=wf_rows[g, v])
+        bias = held.tile([P, PACK], F32, name="bias")
+        nc.sync.dma_start(out=bias[:], in_=bf.rearrange("(p s) -> p s", s=PACK))
+
+        def gather(c):
+            cols = slice(c * CHUNK // 16, (c + 1) * CHUNK // 16)
+            got = []
+            for i in range(3):
+                scales = picked.tile([P, CHUNK], U8, name=f"picked_scales{i}", align_bytes=ALIGN)
+                nc.vector.tensor_copy(scales[:], table_scales[:].indirect(lists[i][:, cols]))
+                words = picked.tile([P, CHUNK], U32, name=f"picked_words{i}", align_bytes=ALIGN)
+                nc.vector.tensor_copy(words[:], table_words[:].bitcast(U32).indirect(lists[i][:, cols]))
+                got.append((words, scales))
+            return got
+
+        def quantize_w1(g):
+            rounded = held.tile([P, PASS * PACK], BF16, name=f"w1_rounded{g}", align_bytes=ALIGN)
+            nc.scalar.copy(
+                out=rounded[:].rearrange("p (t u v j) -> p t u j v", t=PACK, v=4, j=PACK),
+                in_=w1_raw[g][:].rearrange("p j (u t v) -> p t u j v", t=PACK, v=4),
+            )
+            codes = held.tile([P, PASS], U32, name=f"w1_codes{g}", align_bytes=ALIGN)
+            scales = held.tile([P, PASS], U8, name=f"w1_scales{g}", align_bytes=ALIGN)
+            nc.vector.quantize_mx(out=codes[:].bitcast(FP8X4), scales=scales[:], in_=rounded[:])
+            return codes, scales
+
+        def quantize_wf(g):
+            rounded = held.tile([P, N * PACK], BF16, name=f"wf_rounded{g}", align_bytes=ALIGN)
+            nc.scalar.copy(
+                out=rounded[:].rearrange("p (s m t) -> p m t s", s=PACK, t=PACK),
+                in_=wf_raw[g][:].rearrange("p t (m s) -> p m t s", s=PACK),
+            )
+            codes = held.tile([P, N], U32, name=f"wf_codes{g}", align_bytes=ALIGN)
+            scales = held.tile([P, N], U8, name=f"wf_scales{g}", align_bytes=ALIGN)
+            nc.vector.quantize_mx(out=codes[:].bitcast(FP8X4), scales=scales[:], in_=rounded[:])
+            return codes, scales
+
+        def deal(dst, src, words_per_run):
+            nc.vector.tensor_copy(
+                out=dst.rearrange("p (x t u e) -> p x t u e", t=PACK, u=32, e=words_per_run),
+                in_=src.rearrange("p (x u t e) -> p x t u e", t=PACK, u=32, e=words_per_run),
+            )
+
+        first = gather(0)
+        w1_q = [quantize_w1(0)]
+        w2_codes = held.tile([P, 2 * H], U8, name="w2_codes", align_bytes=ALIGN)
+        deal(w2_codes[:].bitcast(I32), w2_raw[:], 2)
+        w3_codes = held.tile([P, H], U32, name="w3_codes", align_bytes=ALIGN)
+        deal(w3_codes[:].bitcast(I32), w3_raw[:], 4)
+        w23_scales = held.tile([P, 2 * H], U8, name="w23_scales", align_bytes=ALIGN)
+        deal(w23_scales[:].bitcast(I32), raw_scales[:].bitcast(I32), 1)
+        w1_q.append(quantize_w1(1))
+        wf_q = []
+
+        gain_tiles = []
+        for g in range(GROUPS):
+            spread = held.tile([P, UNIT * PACK], F32, name=f"gain_tile{g}")
+            nc.scalar.copy(
+                out=spread[:].rearrange("p (c t) -> p c t", t=PACK),
+                in_=gains[:, g, 0:13:4].unsqueeze(1).to_broadcast([P, UNIT, PACK]),
+            )
+            gain_tiles.append(spread)
+
+        def stationary(i, g, t):
+            c0 = g * PASS + t * P
+            if i == 0:
+                return w1_q[g][0][:, t * P : (t + 1) * P].bitcast(FP8X4), w1_q[g][1][:, t * P : (t + 1) * P]
+            if i == 1:
+                return w2_codes[:, 2 * c0 : 2 * (c0 + P)].bitcast(FP4X4), w23_scales[:, c0 : c0 + P]
+            return w3_codes[:, c0 : c0 + P].bitcast(FP8X4), w23_scales[:, H + c0 : H + c0 + P]
+
+        def pairs_of_bank(bank):
+            return bank[:].rearrange("p t (c i) -> p c t i", i=2)
+
+        def pairs(tile):
+            return tile[:].rearrange("p (c t i) -> p c t i", t=PACK, i=2)
+
+        def unit(got, g, half, rounded, engine):
+            cols = slice(half * UNIT, (half + 1) * UNIT)
+            banks = []
+            for i in range(3):
+                bank = psum.tile([P, PACK, UNIT], F32, name=f"first{i}")
+                for t in range(PACK):
+                    codes, scales = stationary(i, g, t)
+                    nc.tensor.matmul_mx(
+                        out=bank[:, t, :], lhsT=codes, lhsT_scale=scales,
+                        rhs=got[i][0][:, cols].bitcast(FP8X4), rhs_scale=got[i][1][:, cols],
+                        start=True, stop=True,
+                    )
+                banks.append(bank)
+            a = work.tile([P, PACK * UNIT], F32, name="a")
+            nc.scalar.copy(out=pairs(a), in_=pairs_of_bank(banks[0]))
+            ab = work.tile([P, PACK * UNIT], F32, name="ab")
+            nc.vector.tensor_tensor(out=pairs(ab), in0=pairs_of_bank(banks[1]), in1=pairs(a), op=ALU.max)
+            abc = work.tile([P, PACK * UNIT], F32, name="abc")
+            nc.vector.tensor_tensor(out=abc[:].rearrange("p (c i t) -> p c t i", t=PACK, i=2), in0=pairs_of_bank(banks[2]), in1=pairs(ab), op=ALU.max)
+            silu = work.tile([P, PACK * UNIT], F32, name="silu")
+            nc.scalar.activation(out=silu[:], in_=abc[:], func=ACT.Silu)
+            engine.tensor_tensor(out=rounded, in0=silu[:], in1=gain_tiles[g][:], op=ALU.mult)
+
+        y_scales = held.tile([P, S], U8, name="y_scales", align_bytes=ALIGN)
+        y_rows = out_0.rearrange("(p s) j -> p s j", s=PACK)
+        y_words = out_1[0].rearrange("p m t -> p (m t)").bitcast(I32)
+
+        def second(start, width, h_q):
+            cols = slice(start, start + width)
+            per_bank = PASS // width
+            y = work.tile([P, PACK, width], F32, name="y")
+            for b in range(PACK // per_bank):
+                bank = psum.tile([P, per_bank, width], F32, name="logits")
+                for e in range(per_bank):
+                    s = per_bank * b + e
+                    for g in range(GROUPS):
+                        nc.tensor.matmul_mx(
+                            out=bank[:, e, :],
+                            lhsT=wf_q[g][0][:, s * P : (s + 1) * P].bitcast(FP8X4), lhsT_scale=wf_q[g][1][:, s * P : (s + 1) * P],
+                            rhs=h_q[g][0][:].bitcast(FP8X4), rhs_scale=h_q[g][1][:],
+                            start=(g == 0), stop=(g == GROUPS - 1),
+                        )
+                for e in range(per_bank):
+                    s = per_bank * b + e
+                    nc.scalar.activation(out=y[:, s, :], in_=bank[:, e, :], func=ACT.Identity, bias=bias[:, s : s + 1])
+            nc.sync.dma_start(out=y_rows[:, :, cols], in_=y[:])
+            rounded = work.tile([P, width * PACK], BF16, name="y_rounded", align_bytes=ALIGN)
+            nc.scalar.copy(
+                out=rounded[:].rearrange("p (c i s) -> p c s i", s=PACK, i=4),
+                in_=y[:].rearrange("p s (c i) -> p c s i", i=4),
+            )
+            codes = work.tile([P, width], U32, name="y_codes", align_bytes=ALIGN)
+            nc.vector.quantize_mx(out=codes[:].bitcast(FP8X4), scales=y_scales[:, cols], in_=rounded[:])
+            nc.sync.dma_start(out=y_words[:, cols], in_=codes[:].bitcast(I32))
+
+        def stretch(got, c, halves):
+            width = UNIT * len(halves)
+            h_q = []
+            for g in range(GROUPS):
+                rounded = work.tile([P, width * PACK], BF16, name="h_rounded", align_bytes=ALIGN)
+                for n, half in enumerate(halves):
+                    index = (c * 2 + half) * 2 + g
+                    engine = nc.vector
+                    unit(got, g, half, rounded[:, n * UNIT * PACK : (n + 1) * UNIT * PACK], engine)
+                codes = work.tile([P, width], U32, name="h_codes", align_bytes=ALIGN)
+                scales = work.tile([P, width], U8, name="h_scales", align_bytes=ALIGN)
+                nc.vector.quantize_mx(out=codes[:].bitcast(FP8X4), scales=scales[:], in_=rounded[:])
+                h_q.append((codes, scales))
+                if c == 0:
+                    wf_q.append(quantize_wf(g))
+            second(c * CHUNK + halves[0] * UNIT, width, h_q)
+
+        got = first
+        chunks = S // CHUNK
+        for c in range(chunks):
+            if c + 1 < chunks:
+                ahead = gather(c + 1)
+                stretch(got, c, [0, 1])
+                got = ahead
+            else:
+                stretch(got, c, [0])
+                stretch(got, c, [1])
+        for q in range(QUADS):
+            nc.sync.dma_start(
+                out=out_2[0, 4 * q : 4 * q + 4, :].bitcast(I32), in_=y_scales[32 * q : 32 * q + 4, :].bitcast(I32)
+            )

@@ -21,9 +21,11 @@ PACK = 4
 PASS = P * PACK
 GROUPS = H // PASS
 QUADS = 4
-CHUNK = 256
 UNIT = 128
 ALIGN = 64
+CHUNK = 256
+AHEAD = 2
+STRETCHES = (256, 256, 256, 128)
 
 
 def tile_list_opcode_trigram_families_kernel(
@@ -44,71 +46,97 @@ def tile_list_opcode_trigram_families_kernel(
 
         def load_scale_rows(dst, rows):
             for q in range(QUADS):
-                nc.scalar.dma_start(out=dst[32 * q : 32 * q + 4, :].bitcast(I32), in_=rows[4 * q : 4 * q + 4, :].bitcast(I32))
+                nc.sync.dma_start(out=dst[32 * q : 32 * q + 4, :].bitcast(I32), in_=rows[4 * q : 4 * q + 4, :].bitcast(I32))
 
         lists = [held.tile([P, S // 16], U16, name=f"list{i}") for i in range(3)]
-        nc.sync.dma_start(lists[0][:], offs)
-        load_scale_rows(table_scales[:], tab_scales[0])
         table_words = held.tile([P, T], I32, name="table_words", align_bytes=ALIGN)
-        nc.sync.dma_start(out=table_words[:], in_=tab_words[0].rearrange("p t i -> p (t i)").bitcast(I32))
-        nc.sync.dma_start(lists[1][:], offs2)
-        nc.sync.dma_start(lists[2][:], offs3)
-
         w1_rows = w1.rearrange("(p j) r -> p j r", j=PACK)
         w1_raw = [held.tile([P, PACK, PASS], F32, name=f"w1_raw{g}") for g in range(GROUPS)]
         w2_raw = held.tile([P, H // 2], I32, name="w2_raw")
         w3_raw = held.tile([P, H], I32, name="w3_raw")
-        load_scale_rows(raw_scales[:, :H], w2_scales[0])
-        nc.sync.dma_start(out=w1_raw[0][:], in_=w1_rows[:, :, 0:PASS])
-        nc.sync.dma_start(out=w2_raw[:], in_=w2_words[0].bitcast(I32))
-        nc.sync.dma_start(out=w3_raw[:], in_=w3_words[0].rearrange("p e i -> p (e i)").bitcast(I32))
-        load_scale_rows(raw_scales[:, H:], w3_scales[0])
-        nc.sync.dma_start(out=w1_raw[1][:], in_=w1_rows[:, :, PASS : 2 * PASS])
-
         gains = held.tile([P, GROUPS, 16], F32, name="gains")
         gain_runs = gain.rearrange("(g u e) -> u g e", g=GROUPS, e=16)
-        for v in range(4):
-            nc.sync.dma_start(out=gains[v:P:4, :, 0:13], in_=gain_runs[:, :, v : v + 13])
         wf_rows = wf.rearrange("(g u t v) n -> g v u t n", g=GROUPS, t=PACK, v=4)
         wf_raw = [held.tile([P, PACK, N], F32, name=f"wf_raw{g}") for g in range(GROUPS)]
-        for g in range(GROUPS):
+        bias = held.tile([P, PACK], F32, name="bias")
+
+        def load_table():
+            nc.sync.dma_start(out=table_words[:], in_=tab_words[0].rearrange("p t i -> p (t i)").bitcast(I32))
+
+        def load_w1(g):
+            nc.sync.dma_start(out=w1_raw[g][:], in_=w1_rows[:, :, g * PASS : (g + 1) * PASS])
+
+        def load_wf(g):
             for v in range(4):
                 nc.sync.dma_start(out=wf_raw[g][v:P:4, :, :], in_=wf_rows[g, v])
-        bias = held.tile([P, PACK], F32, name="bias")
-        nc.sync.dma_start(out=bias[:], in_=bf.rearrange("(p s) -> p s", s=PACK))
 
-        def gather(c):
-            cols = slice(c * CHUNK // 16, (c + 1) * CHUNK // 16)
-            got = []
-            for i in range(3):
-                scales = picked.tile([P, CHUNK], U8, name=f"picked_scales{i}", align_bytes=ALIGN)
-                nc.vector.tensor_copy(scales[:], table_scales[:].indirect(lists[i][:, cols]))
-                words = picked.tile([P, CHUNK], U32, name=f"picked_words{i}", align_bytes=ALIGN)
-                nc.vector.tensor_copy(words[:], table_words[:].bitcast(U32).indirect(lists[i][:, cols]))
-                got.append((words, scales))
-            return got
+        def load_gains():
+            for v in range(4):
+                nc.sync.dma_start(out=gains[v:P:4, :, 0:13], in_=gain_runs[:, :, v : v + 13])
 
-        def quantize_w1(g):
+        def load_bias():
+            nc.sync.dma_start(out=bias[:], in_=bf.rearrange("(p s) -> p s", s=PACK))
+
+        def load_w23():
+            nc.sync.dma_start(out=w2_raw[:], in_=w2_words[0].bitcast(I32))
+            nc.sync.dma_start(out=w3_raw[:], in_=w3_words[0].rearrange("p e i -> p (e i)").bitcast(I32))
+
+        nc.sync.dma_start(lists[0][:], offs)
+        load_scale_rows(table_scales[:], tab_scales[0])
+        nc.sync.dma_start(lists[1][:], offs2)
+        nc.sync.dma_start(lists[2][:], offs3)
+        load_bias()
+        load_w1(0)
+        load_table()
+        load_w1(1)
+        load_gains()
+        load_wf(0)
+        load_wf(1)
+        load_scale_rows(raw_scales[:, :H], w2_scales[0])
+        load_scale_rows(raw_scales[:, H:], w3_scales[0])
+        nc.sync.dma_start(out=w2_raw[:], in_=w2_words[0].bitcast(I32))
+        nc.sync.dma_start(out=w3_raw[:], in_=w3_words[0].rearrange("p e i -> p (e i)").bitcast(I32))
+
+        picked_scales = [held.tile([P, S], U8, name=f"picked_scales{i}", align_bytes=ALIGN) for i in range(3)]
+        for i in range(3):
+            nc.vector.tensor_copy(picked_scales[i][:], table_scales[:].indirect(lists[i][:]))
+
+        picked_words = {}
+
+        def gather_words(chunk, i):
+            words = picked.tile([P, CHUNK], U32, name=f"picked_words{i}", align_bytes=ALIGN)
+            nc.vector.tensor_copy(
+                words[:], table_words[:].bitcast(U32).indirect(lists[i][:, chunk * CHUNK // 16 : (chunk + 1) * CHUNK // 16])
+            )
+            picked_words[chunk, i] = words
+
+        for chunk in range(AHEAD):
+            for i in (2, 1, 0):
+                gather_words(chunk, i)
+
+        def quantize(rounded, name):
+            codes = held.tile([P, PASS], U32, name=f"{name}_codes", align_bytes=ALIGN)
+            scales = held.tile([P, PASS], U8, name=f"{name}_scales", align_bytes=ALIGN)
+            nc.vector.quantize_mx(out=codes[:].bitcast(FP8X4), scales=scales[:], in_=rounded[:])
+            return codes, scales
+
+        w1_q, wf_q = [], []
+        for g in range(GROUPS):
             rounded = held.tile([P, PASS * PACK], BF16, name=f"w1_rounded{g}", align_bytes=ALIGN)
             nc.scalar.copy(
                 out=rounded[:].rearrange("p (t u v j) -> p t u j v", t=PACK, v=4, j=PACK),
                 in_=w1_raw[g][:].rearrange("p j (u t v) -> p t u j v", t=PACK, v=4),
             )
-            codes = held.tile([P, PASS], U32, name=f"w1_codes{g}", align_bytes=ALIGN)
-            scales = held.tile([P, PASS], U8, name=f"w1_scales{g}", align_bytes=ALIGN)
-            nc.vector.quantize_mx(out=codes[:].bitcast(FP8X4), scales=scales[:], in_=rounded[:])
-            return codes, scales
-
-        def quantize_wf(g):
+            w1_q.append(quantize(rounded, f"w1_{g}"))
+        for g in range(GROUPS):
             rounded = held.tile([P, N * PACK], BF16, name=f"wf_rounded{g}", align_bytes=ALIGN)
             nc.scalar.copy(
                 out=rounded[:].rearrange("p (s m t) -> p m t s", s=PACK, t=PACK),
                 in_=wf_raw[g][:].rearrange("p t (m s) -> p m t s", s=PACK),
             )
-            codes = held.tile([P, N], U32, name=f"wf_codes{g}", align_bytes=ALIGN)
-            scales = held.tile([P, N], U8, name=f"wf_scales{g}", align_bytes=ALIGN)
-            nc.vector.quantize_mx(out=codes[:].bitcast(FP8X4), scales=scales[:], in_=rounded[:])
-            return codes, scales
+            wf_q.append(quantize(rounded, f"wf_{g}"))
+        gain_cols = held.tile([P, GROUPS, PACK], F32, name="gain_cols")
+        nc.vector.tensor_copy(out=gain_cols[:], in_=gains[:, :, 0:13:4])
 
         def deal(dst, src, words_per_run):
             nc.vector.tensor_copy(
@@ -116,25 +144,12 @@ def tile_list_opcode_trigram_families_kernel(
                 in_=src.rearrange("p (x u t e) -> p x t u e", t=PACK, u=32, e=words_per_run),
             )
 
-        first = gather(0)
-        w1_q = [quantize_w1(0)]
-        w2_codes = held.tile([P, 2 * H], U8, name="w2_codes", align_bytes=ALIGN)
-        deal(w2_codes[:].bitcast(I32), w2_raw[:], 2)
-        w3_codes = held.tile([P, H], U32, name="w3_codes", align_bytes=ALIGN)
-        deal(w3_codes[:].bitcast(I32), w3_raw[:], 4)
         w23_scales = held.tile([P, 2 * H], U8, name="w23_scales", align_bytes=ALIGN)
         deal(w23_scales[:].bitcast(I32), raw_scales[:].bitcast(I32), 1)
-        w1_q.append(quantize_w1(1))
-        wf_q = []
-
-        gain_tiles = []
-        for g in range(GROUPS):
-            spread = held.tile([P, UNIT * PACK], F32, name=f"gain_tile{g}")
-            nc.scalar.copy(
-                out=spread[:].rearrange("p (c t) -> p c t", t=PACK),
-                in_=gains[:, g, 0:13:4].unsqueeze(1).to_broadcast([P, UNIT, PACK]),
-            )
-            gain_tiles.append(spread)
+        w3_codes = held.tile([P, H], U32, name="w3_codes", align_bytes=ALIGN)
+        deal(w3_codes[:].bitcast(I32), w3_raw[:], 4)
+        w2_codes = held.tile([P, 2 * H], U8, name="w2_codes", align_bytes=ALIGN)
+        deal(w2_codes[:].bitcast(I32), w2_raw[:], 2)
 
         def stationary(i, g, t):
             c0 = g * PASS + t * P
@@ -150,34 +165,42 @@ def tile_list_opcode_trigram_families_kernel(
         def pairs(tile):
             return tile[:].rearrange("p (c t i) -> p c t i", t=PACK, i=2)
 
-        def unit(got, g, half, rounded, engine):
-            cols = slice(half * UNIT, (half + 1) * UNIT)
-            banks = []
-            for i in range(3):
+        def unit(start, g, rounded, engine):
+            cols = slice(start, start + UNIT)
+            banks = {}
+            for i in (2, 1, 0):
                 bank = psum.tile([P, PACK, UNIT], F32, name=f"first{i}")
                 for t in range(PACK):
                     codes, scales = stationary(i, g, t)
                     nc.tensor.matmul_mx(
                         out=bank[:, t, :], lhsT=codes, lhsT_scale=scales,
-                        rhs=got[i][0][:, cols].bitcast(FP8X4), rhs_scale=got[i][1][:, cols],
+                        rhs=picked_words[start // CHUNK, i][:, start % CHUNK : start % CHUNK + UNIT].bitcast(FP8X4), rhs_scale=picked_scales[i][:, cols],
                         start=True, stop=True,
                     )
-                banks.append(bank)
-            a = work.tile([P, PACK * UNIT], F32, name="a")
-            nc.scalar.copy(out=pairs(a), in_=pairs_of_bank(banks[0]))
-            ab = work.tile([P, PACK * UNIT], F32, name="ab")
-            nc.vector.tensor_tensor(out=pairs(ab), in0=pairs_of_bank(banks[1]), in1=pairs(a), op=ALU.max)
+                banks[i] = bank
+            c = work.tile([P, PACK * UNIT], F32, name="c")
+            nc.scalar.copy(out=pairs(c), in_=pairs_of_bank(banks[2]))
+            bc = work.tile([P, PACK * UNIT], F32, name="bc")
+            nc.vector.tensor_tensor(out=pairs(bc), in0=pairs_of_bank(banks[1]), in1=pairs(c), op=ALU.max)
             abc = work.tile([P, PACK * UNIT], F32, name="abc")
-            nc.vector.tensor_tensor(out=abc[:].rearrange("p (c i t) -> p c t i", t=PACK, i=2), in0=pairs_of_bank(banks[2]), in1=pairs(ab), op=ALU.max)
+            nc.vector.tensor_tensor(
+                out=abc[:].rearrange("p (c i t) -> p c t i", t=PACK, i=2),
+                in0=pairs_of_bank(banks[0]), in1=pairs(bc), op=ALU.max,
+            )
             silu = work.tile([P, PACK * UNIT], F32, name="silu")
             nc.scalar.activation(out=silu[:], in_=abc[:], func=ACT.Silu)
-            engine.tensor_tensor(out=rounded, in0=silu[:], in1=gain_tiles[g][:], op=ALU.mult)
+            engine.tensor_tensor(
+                out=rounded.rearrange("p (c t) -> p c t", t=PACK),
+                in0=silu[:].rearrange("p (c t) -> p c t", t=PACK),
+                in1=gain_cols[:, g, :].unsqueeze(1).to_broadcast([P, UNIT, PACK]),
+                op=ALU.mult,
+            )
 
         y_scales = held.tile([P, S], U8, name="y_scales", align_bytes=ALIGN)
         y_rows = out_0.rearrange("(p s) j -> p s j", s=PACK)
         y_words = out_1[0].rearrange("p m t -> p (m t)").bitcast(I32)
 
-        def second(start, width, h_q):
+        def second(start, width, h_codes, h_scales, rounder):
             cols = slice(start, start + width)
             per_bank = PASS // width
             y = work.tile([P, PACK, width], F32, name="y")
@@ -189,7 +212,8 @@ def tile_list_opcode_trigram_families_kernel(
                         nc.tensor.matmul_mx(
                             out=bank[:, e, :],
                             lhsT=wf_q[g][0][:, s * P : (s + 1) * P].bitcast(FP8X4), lhsT_scale=wf_q[g][1][:, s * P : (s + 1) * P],
-                            rhs=h_q[g][0][:].bitcast(FP8X4), rhs_scale=h_q[g][1][:],
+                            rhs=h_codes[:, g * width : (g + 1) * width].bitcast(FP8X4),
+                            rhs_scale=h_scales[:, g * width : (g + 1) * width],
                             start=(g == 0), stop=(g == GROUPS - 1),
                         )
                 for e in range(per_bank):
@@ -197,7 +221,7 @@ def tile_list_opcode_trigram_families_kernel(
                     nc.scalar.activation(out=y[:, s, :], in_=bank[:, e, :], func=ACT.Identity, bias=bias[:, s : s + 1])
             nc.sync.dma_start(out=y_rows[:, :, cols], in_=y[:])
             rounded = work.tile([P, width * PACK], BF16, name="y_rounded", align_bytes=ALIGN)
-            nc.scalar.copy(
+            rounder(
                 out=rounded[:].rearrange("p (c i s) -> p c s i", s=PACK, i=4),
                 in_=y[:].rearrange("p s (c i) -> p c s i", i=4),
             )
@@ -205,34 +229,58 @@ def tile_list_opcode_trigram_families_kernel(
             nc.vector.quantize_mx(out=codes[:].bitcast(FP8X4), scales=y_scales[:, cols], in_=rounded[:])
             nc.sync.dma_start(out=y_words[:, cols], in_=codes[:].bitcast(I32))
 
-        def stretch(got, c, halves):
-            width = UNIT * len(halves)
-            h_q = []
+        def last_stretch(start):
+            cols = slice(start, start + UNIT)
+            banks = [psum.tile([P, 2, UNIT], F32, name="logits") for b in range(2)]
             for g in range(GROUPS):
-                rounded = work.tile([P, width * PACK], BF16, name="h_rounded", align_bytes=ALIGN)
-                for n, half in enumerate(halves):
-                    index = (c * 2 + half) * 2 + g
-                    engine = nc.vector
-                    unit(got, g, half, rounded[:, n * UNIT * PACK : (n + 1) * UNIT * PACK], engine)
-                codes = work.tile([P, width], U32, name="h_codes", align_bytes=ALIGN)
-                scales = work.tile([P, width], U8, name="h_scales", align_bytes=ALIGN)
-                nc.vector.quantize_mx(out=codes[:].bitcast(FP8X4), scales=scales[:], in_=rounded[:])
-                h_q.append((codes, scales))
-                if c == 0:
-                    wf_q.append(quantize_wf(g))
-            second(c * CHUNK + halves[0] * UNIT, width, h_q)
+                rounded = work.tile([P, UNIT * PACK], BF16, name="h_rounded", align_bytes=ALIGN)
+                unit(start, g, rounded[:], nc.gpsimd if g == 0 else nc.vector)
+                h_codes = work.tile([P, UNIT], U32, name="h_codes", align_bytes=ALIGN)
+                h_scales = work.tile([P, UNIT], U8, name="h_scales", align_bytes=ALIGN)
+                nc.vector.quantize_mx(out=h_codes[:].bitcast(FP8X4), scales=h_scales[:], in_=rounded[:])
+                for s in range(PACK):
+                    nc.tensor.matmul_mx(
+                        out=banks[s // 2][:, s % 2, :],
+                        lhsT=wf_q[g][0][:, s * P : (s + 1) * P].bitcast(FP8X4), lhsT_scale=wf_q[g][1][:, s * P : (s + 1) * P],
+                        rhs=h_codes[:].bitcast(FP8X4), rhs_scale=h_scales[:],
+                        start=(g == 0 and s % 2 == 0), stop=(g == GROUPS - 1 and s % 2 == 1),
+                    )
+            y = work.tile([P, PACK, UNIT], F32, name="y")
+            for s in range(PACK):
+                if s < 2:
+                    nc.scalar.activation(out=y[:, s, :], in_=banks[0][:, s, :], func=ACT.Identity, bias=bias[:, s : s + 1])
+                else:
+                    nc.vector.tensor_scalar(
+                        out=y[:, s, :], in0=banks[1][:, s - 2, :], scalar1=bias[:, s : s + 1], scalar2=None, op0=ALU.add
+                    )
+            nc.scalar.dma_start(out=y_rows[:, :, cols], in_=y[:])
+            rounded = work.tile([P, UNIT * PACK], BF16, name="y_rounded", align_bytes=ALIGN)
+            nc.vector.tensor_copy(
+                out=rounded[:].rearrange("p (c i s) -> p c s i", s=PACK, i=4),
+                in_=y[:].rearrange("p s (c i) -> p c s i", i=4),
+            )
+            codes = work.tile([P, UNIT], U32, name="y_codes", align_bytes=ALIGN)
+            nc.vector.quantize_mx(out=codes[:].bitcast(FP8X4), scales=y_scales[:, cols], in_=rounded[:])
+            nc.sync.dma_start(out=y_words[:, cols], in_=codes[:].bitcast(I32))
 
-        got = first
-        chunks = S // CHUNK
-        for c in range(chunks):
-            if c + 1 < chunks:
-                ahead = gather(c + 1)
-                stretch(got, c, [0, 1])
-                got = ahead
-            else:
-                stretch(got, c, [0])
-                stretch(got, c, [1])
+        start = 0
+        for n, width in enumerate(STRETCHES):
+            rounded = work.tile([P, GROUPS * width * PACK], BF16, name="h_rounded", align_bytes=ALIGN)
+            for g in range(GROUPS):
+                for offset in range(0, width, UNIT):
+                    first = (g * width + offset) * PACK
+                    engine = nc.gpsimd
+                    unit(start + offset, g, rounded[:, first : first + UNIT * PACK], engine)
+            if n + AHEAD < S // CHUNK:
+                for i in (2, 1, 0):
+                    gather_words(n + AHEAD, i)
+            h_codes = work.tile([P, GROUPS * width], U32, name="h_codes", align_bytes=ALIGN)
+            h_scales = work.tile([P, GROUPS * width], U8, name="h_scales", align_bytes=ALIGN)
+            nc.vector.quantize_mx(out=h_codes[:].bitcast(FP8X4), scales=h_scales[:], in_=rounded[:])
+            second(start, width, h_codes, h_scales, nc.scalar.copy)
+            start = start + width
+        last_stretch(start)
         for q in range(QUADS):
-            nc.sync.dma_start(
+            (nc.scalar if q % 2 == 0 else nc.sync).dma_start(
                 out=out_2[0, 4 * q : 4 * q + 4, :].bitcast(I32), in_=y_scales[32 * q : 32 * q + 4, :].bitcast(I32)
             )

@@ -23,8 +23,7 @@ GROUPS = H // PASS
 QUADS = 4
 UNIT = 128
 ALIGN = 64
-CHUNK = 256
-AHEAD = 2
+CHUNK = 512
 STRETCHES = (256, 256, 256, 128)
 
 
@@ -35,7 +34,7 @@ def tile_list_opcode_trigram_families_kernel(
     nc = tc.nc
     with ExitStack() as ctx:
         held = ctx.enter_context(tc.tile_pool(name="held", bufs=1))
-        picked = ctx.enter_context(tc.tile_pool(name="picked", bufs=2))
+        picked = ctx.enter_context(tc.tile_pool(name="picked", bufs=1))
         work = ctx.enter_context(tc.tile_pool(name="work", bufs=3))
         psum = ctx.enter_context(tc.psum_pool(name="psum", bufs=2))
 
@@ -53,7 +52,7 @@ def tile_list_opcode_trigram_families_kernel(
         w1_rows = w1.rearrange("(p j) r -> p j r", j=PACK)
         w1_raw = [held.tile([P, PACK, PASS], F32, name=f"w1_raw{g}") for g in range(GROUPS)]
         w2_raw = held.tile([P, H // 2], I32, name="w2_raw")
-        w3_raw = held.tile([P, H], I32, name="w3_raw")
+        w3_raw = picked.tile([P, H], I32, name="w3_raw", offset=3 * CHUNK * 4 + CHUNK * 2)
         gains = held.tile([P, GROUPS, 16], F32, name="gains")
         gain_runs = gain.rearrange("(g u e) -> u g e", g=GROUPS, e=16)
         wf_rows = wf.rearrange("(g u t v) n -> g v u t n", g=GROUPS, t=PACK, v=4)
@@ -89,12 +88,12 @@ def tile_list_opcode_trigram_families_kernel(
         load_w1(0)
         load_table()
         load_w1(1)
-        load_gains()
-        load_wf(0)
-        load_wf(1)
-        load_scale_rows(raw_scales[:, :H], w2_scales[0])
-        load_scale_rows(raw_scales[:, H:], w3_scales[0])
         nc.sync.dma_start(out=w2_raw[:], in_=w2_words[0].bitcast(I32))
+        load_wf(0)
+        load_scale_rows(raw_scales[:, :H], w2_scales[0])
+        load_wf(1)
+        load_scale_rows(raw_scales[:, H:], w3_scales[0])
+        load_gains()
         nc.sync.dma_start(out=w3_raw[:], in_=w3_words[0].rearrange("p e i -> p (e i)").bitcast(I32))
 
         picked_scales = [held.tile([P, S], U8, name=f"picked_scales{i}", align_bytes=ALIGN) for i in range(3)]
@@ -104,15 +103,14 @@ def tile_list_opcode_trigram_families_kernel(
         picked_words = {}
 
         def gather_words(chunk, i):
-            words = picked.tile([P, CHUNK], U32, name=f"picked_words{i}", align_bytes=ALIGN)
+            words = picked.tile([P, CHUNK], U32, name=f"picked_words{chunk}{i}", align_bytes=ALIGN, offset=(3 * chunk + i) * CHUNK * 4)
             nc.vector.tensor_copy(
                 words[:], table_words[:].bitcast(U32).indirect(lists[i][:, chunk * CHUNK // 16 : (chunk + 1) * CHUNK // 16])
             )
             picked_words[chunk, i] = words
 
-        for chunk in range(AHEAD):
-            for i in (2, 1, 0):
-                gather_words(chunk, i)
+        for i in (2, 1, 0):
+            gather_words(0, i)
 
         def quantize(rounded, name):
             codes = held.tile([P, PASS], U32, name=f"{name}_codes", align_bytes=ALIGN)
@@ -136,7 +134,7 @@ def tile_list_opcode_trigram_families_kernel(
             )
             wf_q.append(quantize(rounded, f"wf_{g}"))
         gain_cols = held.tile([P, GROUPS, PACK], F32, name="gain_cols")
-        nc.vector.tensor_copy(out=gain_cols[:], in_=gains[:, :, 0:13:4])
+        nc.gpsimd.tensor_copy(out=gain_cols[:], in_=gains[:, :, 0:13:4])
 
         def deal(dst, src, words_per_run):
             nc.vector.tensor_copy(
@@ -145,11 +143,15 @@ def tile_list_opcode_trigram_families_kernel(
             )
 
         w23_scales = held.tile([P, 2 * H], U8, name="w23_scales", align_bytes=ALIGN)
-        deal(w23_scales[:].bitcast(I32), raw_scales[:].bitcast(I32), 1)
+        deal(w23_scales[:, H:].bitcast(I32), raw_scales[:, H:].bitcast(I32), 1)
         w3_codes = held.tile([P, H], U32, name="w3_codes", align_bytes=ALIGN)
         deal(w3_codes[:].bitcast(I32), w3_raw[:], 4)
         w2_codes = held.tile([P, 2 * H], U8, name="w2_codes", align_bytes=ALIGN)
         deal(w2_codes[:].bitcast(I32), w2_raw[:], 2)
+        deal(w23_scales[:, :H].bitcast(I32), raw_scales[:, :H].bitcast(I32), 1)
+
+        for i in (2, 1, 0):
+            gather_words(1, i)
 
         def stationary(i, g, t):
             c0 = g * PASS + t * P
@@ -221,9 +223,10 @@ def tile_list_opcode_trigram_families_kernel(
                     nc.scalar.activation(out=y[:, s, :], in_=bank[:, e, :], func=ACT.Identity, bias=bias[:, s : s + 1])
             nc.sync.dma_start(out=y_rows[:, :, cols], in_=y[:])
             rounded = work.tile([P, width * PACK], BF16, name="y_rounded", align_bytes=ALIGN)
-            rounder(
-                out=rounded[:].rearrange("p (c i s) -> p c s i", s=PACK, i=4),
-                in_=y[:].rearrange("p s (c i) -> p c s i", i=4),
+            nc.gpsimd.tensor_scalar(
+                out=rounded[:].rearrange("p (c s) -> p c s", s=PACK),
+                in0=y[:].rearrange("p s c -> p c s"),
+                scalar1=1.0, scalar2=0.0, op0=ALU.mult, op1=ALU.add,
             )
             codes = work.tile([P, width], U32, name="y_codes", align_bytes=ALIGN)
             nc.vector.quantize_mx(out=codes[:].bitcast(FP8X4), scales=y_scales[:, cols], in_=rounded[:])
@@ -271,9 +274,6 @@ def tile_list_opcode_trigram_families_kernel(
                     first = (g * width + offset) * PACK
                     engine = nc.gpsimd
                     unit(start + offset, g, rounded[:, first : first + UNIT * PACK], engine)
-            if n + AHEAD < S // CHUNK:
-                for i in (2, 1, 0):
-                    gather_words(n + AHEAD, i)
             h_codes = work.tile([P, GROUPS * width], U32, name="h_codes", align_bytes=ALIGN)
             h_scales = work.tile([P, GROUPS * width], U8, name="h_scales", align_bytes=ALIGN)
             nc.vector.quantize_mx(out=h_codes[:].bitcast(FP8X4), scales=h_scales[:], in_=rounded[:])

@@ -186,11 +186,15 @@ def tile_list_opcode_trigram_families_kernel(
             nc.vector.tensor_tensor(out=pairs(bc), in0=pairs_of_bank(banks[1]), in1=pairs(c), op=ALU.max)
             abc = work.tile([P, PACK * UNIT], F32, name="abc")
             nc.vector.tensor_tensor(
-                out=abc[:].rearrange("p (c i t) -> p c t i", t=PACK, i=2),
+                out=pairs(abc),
                 in0=pairs_of_bank(banks[0]), in1=pairs(bc), op=ALU.max,
             )
             silu = work.tile([P, PACK * UNIT], F32, name="silu")
-            nc.scalar.activation(out=silu[:], in_=abc[:], func=ACT.Silu)
+            nc.scalar.activation(
+                out=silu[:].rearrange("p (c i t) -> p c i t", t=PACK, i=2),
+                in_=abc[:].rearrange("p (c t i) -> p c i t", t=PACK, i=2),
+                func=ACT.Silu,
+            )
             engine.tensor_tensor(
                 out=rounded.rearrange("p (c t) -> p c t", t=PACK),
                 in0=silu[:].rearrange("p (c t) -> p c t", t=PACK),
@@ -223,11 +227,17 @@ def tile_list_opcode_trigram_families_kernel(
                     nc.scalar.activation(out=y[:, s, :], in_=bank[:, e, :], func=ACT.Identity, bias=bias[:, s : s + 1])
             nc.sync.dma_start(out=y_rows[:, :, cols], in_=y[:])
             rounded = work.tile([P, width * PACK], BF16, name="y_rounded", align_bytes=ALIGN)
-            nc.gpsimd.tensor_scalar(
-                out=rounded[:].rearrange("p (c s) -> p c s", s=PACK),
-                in0=y[:].rearrange("p s c -> p c s"),
-                scalar1=1.0, scalar2=0.0, op0=ALU.mult, op1=ALU.add,
-            )
+            if rounder:
+                nc.gpsimd.tensor_scalar(
+                    out=rounded[:].rearrange("p (c s) -> p c s", s=PACK),
+                    in0=y[:].rearrange("p s c -> p c s"),
+                    scalar1=1.0, scalar2=0.0, op0=ALU.mult, op1=ALU.add,
+                )
+            else:
+                nc.scalar.copy(
+                    out=rounded[:].rearrange("p (c i s) -> p c s i", s=PACK, i=4),
+                    in_=y[:].rearrange("p s (c i) -> p c s i", i=4),
+                )
             codes = work.tile([P, width], U32, name="y_codes", align_bytes=ALIGN)
             nc.vector.quantize_mx(out=codes[:].bitcast(FP8X4), scales=y_scales[:, cols], in_=rounded[:])
             nc.sync.dma_start(out=y_words[:, cols], in_=codes[:].bitcast(I32))
@@ -236,7 +246,7 @@ def tile_list_opcode_trigram_families_kernel(
             cols = slice(start, start + UNIT)
             banks = [psum.tile([P, 2, UNIT], F32, name="logits") for b in range(2)]
             for g in range(GROUPS):
-                rounded = work.tile([P, UNIT * PACK], BF16, name="h_rounded", align_bytes=ALIGN)
+                rounded = work.tile([P, UNIT * PACK], BF16, name="h_rounded", align_bytes=ALIGN, bufs=1)
                 unit(start, g, rounded[:], nc.gpsimd if g == 0 else nc.vector)
                 h_codes = work.tile([P, UNIT], U32, name="h_codes", align_bytes=ALIGN)
                 h_scales = work.tile([P, UNIT], U8, name="h_scales", align_bytes=ALIGN)
@@ -268,7 +278,7 @@ def tile_list_opcode_trigram_families_kernel(
 
         start = 0
         for n, width in enumerate(STRETCHES):
-            rounded = work.tile([P, GROUPS * width * PACK], BF16, name="h_rounded", align_bytes=ALIGN)
+            rounded = work.tile([P, GROUPS * width * PACK], BF16, name="h_rounded", align_bytes=ALIGN, bufs=1)
             for g in range(GROUPS):
                 for offset in range(0, width, UNIT):
                     first = (g * width + offset) * PACK
@@ -277,7 +287,7 @@ def tile_list_opcode_trigram_families_kernel(
             h_codes = work.tile([P, GROUPS * width], U32, name="h_codes", align_bytes=ALIGN)
             h_scales = work.tile([P, GROUPS * width], U8, name="h_scales", align_bytes=ALIGN)
             nc.vector.quantize_mx(out=h_codes[:].bitcast(FP8X4), scales=h_scales[:], in_=rounded[:])
-            second(start, width, h_codes, h_scales, nc.scalar.copy)
+            second(start, width, h_codes, h_scales, n == len(STRETCHES) - 1)
             start = start + width
         last_stretch(start)
         for q in range(QUADS):

@@ -21,10 +21,17 @@ PACK = 4
 PASS = P * PACK
 GROUPS = H // PASS
 QUADS = 4
-UNIT = 128
+RUN = 4
+GAIN_SPAN = RUN * (PACK - 1) + 1
+PER_COLUMN = 16
+WORD = 4
 ALIGN = 64
-CHUNK = 512
+UNIT = 128
+EARLY = 640
+LATE = S - EARLY
 STRETCHES = (256, 256, 256, 128)
+WORK_BUFS = 4
+PRODUCTS = (2, 1, 0)
 
 
 def tile_list_opcode_trigram_families_kernel(
@@ -35,7 +42,7 @@ def tile_list_opcode_trigram_families_kernel(
     with ExitStack() as ctx:
         held = ctx.enter_context(tc.tile_pool(name="held", bufs=1))
         picked = ctx.enter_context(tc.tile_pool(name="picked", bufs=1))
-        work = ctx.enter_context(tc.tile_pool(name="work", bufs=3))
+        work = ctx.enter_context(tc.tile_pool(name="work", bufs=WORK_BUFS))
         psum = ctx.enter_context(tc.psum_pool(name="psum", bufs=2))
 
         table_scales = held.tile([P, T], U8, name="table_scales", align_bytes=ALIGN)
@@ -43,76 +50,67 @@ def tile_list_opcode_trigram_families_kernel(
         raw_scales = held.tile([P, 2 * H], U8, name="raw_scales", align_bytes=ALIGN)
         nc.vector.memset(raw_scales[:].bitcast(I32), 0)
 
-        def load_scale_rows(dst, rows):
-            for q in range(QUADS):
-                nc.sync.dma_start(out=dst[32 * q : 32 * q + 4, :].bitcast(I32), in_=rows[4 * q : 4 * q + 4, :].bitcast(I32))
-
-        lists = [held.tile([P, S // 16], U16, name=f"list{i}") for i in range(3)]
+        lists = [held.tile([P, S // PER_COLUMN], U16, name=f"list{i}") for i in range(3)]
         table_words = held.tile([P, T], I32, name="table_words", align_bytes=ALIGN)
-        w1_rows = w1.rearrange("(p j) r -> p j r", j=PACK)
         w1_raw = [held.tile([P, PACK, PASS], F32, name=f"w1_raw{g}") for g in range(GROUPS)]
         w2_raw = held.tile([P, H // 2], I32, name="w2_raw")
-        w3_raw = picked.tile([P, H], I32, name="w3_raw", offset=3 * CHUNK * 4 + CHUNK * 2)
-        gains = held.tile([P, GROUPS, 16], F32, name="gains")
-        gain_runs = gain.rearrange("(g u e) -> u g e", g=GROUPS, e=16)
-        wf_rows = wf.rearrange("(g u t v) n -> g v u t n", g=GROUPS, t=PACK, v=4)
+        w3_raw = picked.tile([P, H], I32, name="w3_raw", offset=(3 * EARLY + (3 * LATE - H) // 2) * WORD)
+        gains = held.tile([P, GROUPS, RUN * PACK], F32, name="gains")
         wf_raw = [held.tile([P, PACK, N], F32, name=f"wf_raw{g}") for g in range(GROUPS)]
         bias = held.tile([P, PACK], F32, name="bias")
 
-        def load_table():
-            nc.sync.dma_start(out=table_words[:], in_=tab_words[0].rearrange("p t i -> p (t i)").bitcast(I32))
+        w1_rows = w1.rearrange("(p j) r -> p j r", j=PACK)
+        wf_rows = wf.rearrange("(g u t v) n -> g v u t n", g=GROUPS, t=PACK, v=RUN)
+        gain_runs = gain.rearrange("(g u e) -> u g e", g=GROUPS, e=RUN * PACK)
+
+        def load_scale_rows(dst, rows):
+            for q in range(QUADS):
+                nc.sync.dma_start(
+                    out=dst[32 * q : 32 * q + 4, :].bitcast(I32), in_=rows[4 * q : 4 * q + 4, :].bitcast(I32)
+                )
 
         def load_w1(g):
             nc.sync.dma_start(out=w1_raw[g][:], in_=w1_rows[:, :, g * PASS : (g + 1) * PASS])
 
         def load_wf(g):
-            for v in range(4):
-                nc.sync.dma_start(out=wf_raw[g][v:P:4, :, :], in_=wf_rows[g, v])
-
-        def load_gains():
-            for v in range(4):
-                nc.sync.dma_start(out=gains[v:P:4, :, 0:13], in_=gain_runs[:, :, v : v + 13])
-
-        def load_bias():
-            nc.sync.dma_start(out=bias[:], in_=bf.rearrange("(p s) -> p s", s=PACK))
-
-        def load_w23():
-            nc.sync.dma_start(out=w2_raw[:], in_=w2_words[0].bitcast(I32))
-            nc.sync.dma_start(out=w3_raw[:], in_=w3_words[0].rearrange("p e i -> p (e i)").bitcast(I32))
+            for v in range(RUN):
+                nc.sync.dma_start(out=wf_raw[g][v:P:RUN, :, :], in_=wf_rows[g, v])
 
         nc.sync.dma_start(lists[0][:], offs)
         load_scale_rows(table_scales[:], tab_scales[0])
         nc.sync.dma_start(lists[1][:], offs2)
         nc.sync.dma_start(lists[2][:], offs3)
-        load_bias()
+        nc.sync.dma_start(out=bias[:], in_=bf.rearrange("(p s) -> p s", s=PACK))
         load_w1(0)
-        load_table()
+        nc.sync.dma_start(out=table_words[:], in_=tab_words[0].rearrange("p t i -> p (t i)").bitcast(I32))
         load_w1(1)
         nc.sync.dma_start(out=w2_raw[:], in_=w2_words[0].bitcast(I32))
         load_wf(0)
         load_scale_rows(raw_scales[:, :H], w2_scales[0])
         load_wf(1)
         load_scale_rows(raw_scales[:, H:], w3_scales[0])
-        load_gains()
+        for v in range(RUN):
+            nc.sync.dma_start(out=gains[v:P:RUN, :, 0:GAIN_SPAN], in_=gain_runs[:, :, v : v + GAIN_SPAN])
         nc.sync.dma_start(out=w3_raw[:], in_=w3_words[0].rearrange("p e i -> p (e i)").bitcast(I32))
 
         picked_scales = [held.tile([P, S], U8, name=f"picked_scales{i}", align_bytes=ALIGN) for i in range(3)]
         for i in range(3):
             nc.vector.tensor_copy(picked_scales[i][:], table_scales[:].indirect(lists[i][:]))
 
-        picked_words = {}
+        def gather_words(first, width):
+            tiles = {}
+            for i in PRODUCTS:
+                tiles[i] = picked.tile(
+                    [P, width], U32, name=f"picked_words{first}_{i}", align_bytes=ALIGN,
+                    offset=(3 * first + i * width) * WORD,
+                )
+                entries = lists[i][:, first // PER_COLUMN : (first + width) // PER_COLUMN]
+                nc.vector.tensor_copy(tiles[i][:], table_words[:].bitcast(U32).indirect(entries))
+            return tiles
 
-        def gather_words(chunk, i):
-            words = picked.tile([P, CHUNK], U32, name=f"picked_words{chunk}{i}", align_bytes=ALIGN, offset=(3 * chunk + i) * CHUNK * 4)
-            nc.vector.tensor_copy(
-                words[:], table_words[:].bitcast(U32).indirect(lists[i][:, chunk * CHUNK // 16 : (chunk + 1) * CHUNK // 16])
-            )
-            picked_words[chunk, i] = words
+        early_words = gather_words(0, EARLY)
 
-        for i in (2, 1, 0):
-            gather_words(0, i)
-
-        def quantize(rounded, name):
+        def quantize_weight(rounded, name):
             codes = held.tile([P, PASS], U32, name=f"{name}_codes", align_bytes=ALIGN)
             scales = held.tile([P, PASS], U8, name=f"{name}_scales", align_bytes=ALIGN)
             nc.vector.quantize_mx(out=codes[:].bitcast(FP8X4), scales=scales[:], in_=rounded[:])
@@ -122,175 +120,174 @@ def tile_list_opcode_trigram_families_kernel(
         for g in range(GROUPS):
             rounded = held.tile([P, PASS * PACK], BF16, name=f"w1_rounded{g}", align_bytes=ALIGN)
             nc.scalar.copy(
-                out=rounded[:].rearrange("p (t u v j) -> p t u j v", t=PACK, v=4, j=PACK),
-                in_=w1_raw[g][:].rearrange("p j (u t v) -> p t u j v", t=PACK, v=4),
+                out=rounded[:].rearrange("p (t u v j) -> p t u j v", t=PACK, v=RUN, j=PACK),
+                in_=w1_raw[g][:].rearrange("p j (u t v) -> p t u j v", t=PACK, v=RUN),
             )
-            w1_q.append(quantize(rounded, f"w1_{g}"))
+            w1_q.append(quantize_weight(rounded, f"w1_{g}"))
         for g in range(GROUPS):
             rounded = held.tile([P, N * PACK], BF16, name=f"wf_rounded{g}", align_bytes=ALIGN)
             nc.scalar.copy(
                 out=rounded[:].rearrange("p (s m t) -> p m t s", s=PACK, t=PACK),
                 in_=wf_raw[g][:].rearrange("p t (m s) -> p m t s", s=PACK),
             )
-            wf_q.append(quantize(rounded, f"wf_{g}"))
-        gain_cols = held.tile([P, GROUPS, PACK], F32, name="gain_cols")
-        nc.gpsimd.tensor_copy(out=gain_cols[:], in_=gains[:, :, 0:13:4])
+            wf_q.append(quantize_weight(rounded, f"wf_{g}"))
+        gain_slots = held.tile([P, GROUPS, PACK], F32, name="gain_slots")
+        nc.gpsimd.tensor_copy(out=gain_slots[:], in_=gains[:, :, 0:GAIN_SPAN:RUN])
 
-        def deal(dst, src, words_per_run):
+        def reorder_columns(dst, src, words_per_run):
             nc.vector.tensor_copy(
-                out=dst.rearrange("p (x t u e) -> p x t u e", t=PACK, u=32, e=words_per_run),
-                in_=src.rearrange("p (x u t e) -> p x t u e", t=PACK, u=32, e=words_per_run),
+                out=dst.rearrange("p (g t u e) -> p g t u e", t=PACK, u=P // RUN, e=words_per_run),
+                in_=src.rearrange("p (g u t e) -> p g t u e", t=PACK, u=P // RUN, e=words_per_run),
             )
 
         w23_scales = held.tile([P, 2 * H], U8, name="w23_scales", align_bytes=ALIGN)
-        deal(w23_scales[:, H:].bitcast(I32), raw_scales[:, H:].bitcast(I32), 1)
+        reorder_columns(w23_scales[:, H:].bitcast(I32), raw_scales[:, H:].bitcast(I32), 1)
         w3_codes = held.tile([P, H], U32, name="w3_codes", align_bytes=ALIGN)
-        deal(w3_codes[:].bitcast(I32), w3_raw[:], 4)
+        reorder_columns(w3_codes[:].bitcast(I32), w3_raw[:], 4)
         w2_codes = held.tile([P, 2 * H], U8, name="w2_codes", align_bytes=ALIGN)
-        deal(w2_codes[:].bitcast(I32), w2_raw[:], 2)
-        deal(w23_scales[:, :H].bitcast(I32), raw_scales[:, :H].bitcast(I32), 1)
+        reorder_columns(w2_codes[:].bitcast(I32), w2_raw[:], 2)
+        reorder_columns(w23_scales[:, :H].bitcast(I32), raw_scales[:, :H].bitcast(I32), 1)
 
-        for i in (2, 1, 0):
-            gather_words(1, i)
+        late_words = gather_words(EARLY, LATE)
 
         def stationary(i, g, t):
-            c0 = g * PASS + t * P
+            col = g * PASS + t * P
             if i == 0:
                 return w1_q[g][0][:, t * P : (t + 1) * P].bitcast(FP8X4), w1_q[g][1][:, t * P : (t + 1) * P]
             if i == 1:
-                return w2_codes[:, 2 * c0 : 2 * (c0 + P)].bitcast(FP4X4), w23_scales[:, c0 : c0 + P]
-            return w3_codes[:, c0 : c0 + P].bitcast(FP8X4), w23_scales[:, H + c0 : H + c0 + P]
+                return w2_codes[:, 2 * col : 2 * (col + P)].bitcast(FP4X4), w23_scales[:, col : col + P]
+            return w3_codes[:, col : col + P].bitcast(FP8X4), w23_scales[:, H + col : H + col + P]
 
-        def pairs_of_bank(bank):
+        def bank_by_pairs(bank):
             return bank[:].rearrange("p t (c i) -> p c t i", i=2)
 
-        def pairs(tile):
+        def by_pairs(tile):
             return tile[:].rearrange("p (c t i) -> p c t i", t=PACK, i=2)
 
-        def unit(start, g, rounded, engine):
-            cols = slice(start, start + UNIT)
+        def unit(start, g, h_rounded, gain_engine):
+            words, first = (early_words, start) if start < EARLY else (late_words, start - EARLY)
             banks = {}
-            for i in (2, 1, 0):
-                bank = psum.tile([P, PACK, UNIT], F32, name=f"first{i}")
+            for i in PRODUCTS:
+                banks[i] = psum.tile([P, PACK, UNIT], F32, name=f"first{i}")
                 for t in range(PACK):
                     codes, scales = stationary(i, g, t)
                     nc.tensor.matmul_mx(
-                        out=bank[:, t, :], lhsT=codes, lhsT_scale=scales,
-                        rhs=picked_words[start // CHUNK, i][:, start % CHUNK : start % CHUNK + UNIT].bitcast(FP8X4), rhs_scale=picked_scales[i][:, cols],
+                        out=banks[i][:, t, :], lhsT=codes, lhsT_scale=scales,
+                        rhs=words[i][:, first : first + UNIT].bitcast(FP8X4),
+                        rhs_scale=picked_scales[i][:, start : start + UNIT],
                         start=True, stop=True,
                     )
-                banks[i] = bank
             c = work.tile([P, PACK * UNIT], F32, name="c")
-            nc.scalar.copy(out=pairs(c), in_=pairs_of_bank(banks[2]))
+            nc.scalar.copy(out=by_pairs(c), in_=bank_by_pairs(banks[2]))
             bc = work.tile([P, PACK * UNIT], F32, name="bc")
-            nc.vector.tensor_tensor(out=pairs(bc), in0=pairs_of_bank(banks[1]), in1=pairs(c), op=ALU.max)
+            nc.vector.tensor_tensor(out=by_pairs(bc), in0=bank_by_pairs(banks[1]), in1=by_pairs(c), op=ALU.max)
             abc = work.tile([P, PACK * UNIT], F32, name="abc")
-            nc.vector.tensor_tensor(
-                out=pairs(abc),
-                in0=pairs_of_bank(banks[0]), in1=pairs(bc), op=ALU.max,
-            )
+            nc.vector.tensor_tensor(out=by_pairs(abc), in0=bank_by_pairs(banks[0]), in1=by_pairs(bc), op=ALU.max)
             silu = work.tile([P, PACK * UNIT], F32, name="silu")
             nc.scalar.activation(
                 out=silu[:].rearrange("p (c i t) -> p c i t", t=PACK, i=2),
                 in_=abc[:].rearrange("p (c t i) -> p c i t", t=PACK, i=2),
                 func=ACT.Silu,
             )
-            engine.tensor_tensor(
-                out=rounded.rearrange("p (c t) -> p c t", t=PACK),
-                in0=silu[:].rearrange("p (c t) -> p c t", t=PACK),
-                in1=gain_cols[:, g, :].unsqueeze(1).to_broadcast([P, UNIT, PACK]),
+            gain_engine.tensor_tensor(
+                out=h_rounded.rearrange("p (j t) -> p j t", t=PACK),
+                in0=silu[:].rearrange("p (j t) -> p j t", t=PACK),
+                in1=gain_slots[:, g, :].unsqueeze(1).to_broadcast([P, UNIT, PACK]),
                 op=ALU.mult,
             )
+
+        def quantize_h(h_rounded, columns):
+            codes = work.tile([P, columns], U32, name="h_codes", align_bytes=ALIGN)
+            scales = work.tile([P, columns], U8, name="h_scales", align_bytes=ALIGN)
+            nc.vector.quantize_mx(out=codes[:].bitcast(FP8X4), scales=scales[:], in_=h_rounded[:])
+            return codes, scales
+
+        def second_pass(out, g, s, h_codes, h_scales, start, stop):
+            nc.tensor.matmul_mx(
+                out=out, lhsT=wf_q[g][0][:, s * P : (s + 1) * P].bitcast(FP8X4),
+                lhsT_scale=wf_q[g][1][:, s * P : (s + 1) * P],
+                rhs=h_codes.bitcast(FP8X4), rhs_scale=h_scales, start=start, stop=stop,
+            )
+
+        def add_bias(y, s, logits, on_scalar):
+            if on_scalar:
+                nc.scalar.activation(out=y[:, s, :], in_=logits, func=ACT.Identity, bias=bias[:, s : s + 1])
+            else:
+                nc.vector.tensor_scalar(
+                    out=y[:, s, :], in0=logits, scalar1=bias[:, s : s + 1], scalar2=None, op0=ALU.add
+                )
 
         y_scales = held.tile([P, S], U8, name="y_scales", align_bytes=ALIGN)
         y_rows = out_0.rearrange("(p s) j -> p s j", s=PACK)
         y_words = out_1[0].rearrange("p m t -> p (m t)").bitcast(I32)
 
-        def second(start, width, h_codes, h_scales, rounder):
+        def round_by_copy(copy):
+            return lambda rounded, y: copy(
+                out=rounded[:].rearrange("p (c i s) -> p c s i", s=PACK, i=4),
+                in_=y[:].rearrange("p s (c i) -> p c s i", i=4),
+            )
+
+        def round_on_gpsimd(rounded, y):
+            nc.gpsimd.tensor_scalar(
+                out=rounded[:].rearrange("p (j s) -> p j s", s=PACK), in0=y[:].rearrange("p s j -> p j s"),
+                scalar1=1.0, scalar2=0.0, op0=ALU.mult, op1=ALU.add,
+            )
+
+        def store_y(y, start, width, queue, round_y):
             cols = slice(start, start + width)
+            queue.dma_start(out=y_rows[:, :, cols], in_=y[:])
+            y_rounded = work.tile([P, width * PACK], BF16, name="y_rounded", align_bytes=ALIGN)
+            round_y(y_rounded, y)
+            y_codes = work.tile([P, width], U32, name="y_codes", align_bytes=ALIGN)
+            nc.vector.quantize_mx(out=y_codes[:].bitcast(FP8X4), scales=y_scales[:, cols], in_=y_rounded[:])
+            nc.sync.dma_start(out=y_words[:, cols], in_=y_codes[:].bitcast(I32))
+
+        def stretch(start, width, round_y):
+            h_rounded = work.tile([P, GROUPS * width * PACK], BF16, name="h_rounded", align_bytes=ALIGN, bufs=1)
+            for g in range(GROUPS):
+                for offset in range(0, width, UNIT):
+                    first = (g * width + offset) * PACK
+                    unit(start + offset, g, h_rounded[:, first : first + UNIT * PACK], nc.gpsimd)
+            h_codes, h_scales = quantize_h(h_rounded, GROUPS * width)
             per_bank = PASS // width
             y = work.tile([P, PACK, width], F32, name="y")
             for b in range(PACK // per_bank):
                 bank = psum.tile([P, per_bank, width], F32, name="logits")
                 for e in range(per_bank):
-                    s = per_bank * b + e
                     for g in range(GROUPS):
-                        nc.tensor.matmul_mx(
-                            out=bank[:, e, :],
-                            lhsT=wf_q[g][0][:, s * P : (s + 1) * P].bitcast(FP8X4), lhsT_scale=wf_q[g][1][:, s * P : (s + 1) * P],
-                            rhs=h_codes[:, g * width : (g + 1) * width].bitcast(FP8X4),
-                            rhs_scale=h_scales[:, g * width : (g + 1) * width],
-                            start=(g == 0), stop=(g == GROUPS - 1),
+                        cols = slice(g * width, (g + 1) * width)
+                        second_pass(
+                            bank[:, e, :], g, per_bank * b + e, h_codes[:, cols], h_scales[:, cols],
+                            g == 0, g == GROUPS - 1,
                         )
                 for e in range(per_bank):
-                    s = per_bank * b + e
-                    nc.scalar.activation(out=y[:, s, :], in_=bank[:, e, :], func=ACT.Identity, bias=bias[:, s : s + 1])
-            nc.sync.dma_start(out=y_rows[:, :, cols], in_=y[:])
-            rounded = work.tile([P, width * PACK], BF16, name="y_rounded", align_bytes=ALIGN)
-            if rounder:
-                nc.gpsimd.tensor_scalar(
-                    out=rounded[:].rearrange("p (c s) -> p c s", s=PACK),
-                    in0=y[:].rearrange("p s c -> p c s"),
-                    scalar1=1.0, scalar2=0.0, op0=ALU.mult, op1=ALU.add,
-                )
-            else:
-                nc.scalar.copy(
-                    out=rounded[:].rearrange("p (c i s) -> p c s i", s=PACK, i=4),
-                    in_=y[:].rearrange("p s (c i) -> p c s i", i=4),
-                )
-            codes = work.tile([P, width], U32, name="y_codes", align_bytes=ALIGN)
-            nc.vector.quantize_mx(out=codes[:].bitcast(FP8X4), scales=y_scales[:, cols], in_=rounded[:])
-            nc.sync.dma_start(out=y_words[:, cols], in_=codes[:].bitcast(I32))
+                    add_bias(y, per_bank * b + e, bank[:, e, :], b == 0)
+            store_y(y, start, width, nc.sync, round_y)
 
         def last_stretch(start):
-            cols = slice(start, start + UNIT)
             banks = [psum.tile([P, 2, UNIT], F32, name="logits") for b in range(2)]
             for g in range(GROUPS):
-                rounded = work.tile([P, UNIT * PACK], BF16, name="h_rounded", align_bytes=ALIGN, bufs=1)
-                unit(start, g, rounded[:], nc.gpsimd if g == 0 else nc.vector)
-                h_codes = work.tile([P, UNIT], U32, name="h_codes", align_bytes=ALIGN)
-                h_scales = work.tile([P, UNIT], U8, name="h_scales", align_bytes=ALIGN)
-                nc.vector.quantize_mx(out=h_codes[:].bitcast(FP8X4), scales=h_scales[:], in_=rounded[:])
+                h_rounded = work.tile([P, UNIT * PACK], BF16, name="h_last", align_bytes=ALIGN)
+                unit(start, g, h_rounded[:], nc.vector)
+                h_codes, h_scales = quantize_h(h_rounded, UNIT)
                 for s in range(PACK):
-                    nc.tensor.matmul_mx(
-                        out=banks[s // 2][:, s % 2, :],
-                        lhsT=wf_q[g][0][:, s * P : (s + 1) * P].bitcast(FP8X4), lhsT_scale=wf_q[g][1][:, s * P : (s + 1) * P],
-                        rhs=h_codes[:].bitcast(FP8X4), rhs_scale=h_scales[:],
-                        start=(g == 0 and s % 2 == 0), stop=(g == GROUPS - 1 and s % 2 == 1),
+                    second_pass(
+                        banks[s // 2][:, s % 2, :], g, s, h_codes[:], h_scales[:],
+                        g == 0 and s % 2 == 0, g == GROUPS - 1 and s % 2 == 1,
                     )
             y = work.tile([P, PACK, UNIT], F32, name="y")
             for s in range(PACK):
-                if s < 2:
-                    nc.scalar.activation(out=y[:, s, :], in_=banks[0][:, s, :], func=ACT.Identity, bias=bias[:, s : s + 1])
-                else:
-                    nc.vector.tensor_scalar(
-                        out=y[:, s, :], in0=banks[1][:, s - 2, :], scalar1=bias[:, s : s + 1], scalar2=None, op0=ALU.add
-                    )
-            nc.scalar.dma_start(out=y_rows[:, :, cols], in_=y[:])
-            rounded = work.tile([P, UNIT * PACK], BF16, name="y_rounded", align_bytes=ALIGN)
-            nc.vector.tensor_copy(
-                out=rounded[:].rearrange("p (c i s) -> p c s i", s=PACK, i=4),
-                in_=y[:].rearrange("p s (c i) -> p c s i", i=4),
-            )
-            codes = work.tile([P, UNIT], U32, name="y_codes", align_bytes=ALIGN)
-            nc.vector.quantize_mx(out=codes[:].bitcast(FP8X4), scales=y_scales[:, cols], in_=rounded[:])
-            nc.sync.dma_start(out=y_words[:, cols], in_=codes[:].bitcast(I32))
+                add_bias(y, s, banks[s // 2][:, s % 2, :], s < 2)
+            store_y(y, start, UNIT, nc.scalar, round_by_copy(nc.vector.tensor_copy))
 
         start = 0
-        for n, width in enumerate(STRETCHES):
-            rounded = work.tile([P, GROUPS * width * PACK], BF16, name="h_rounded", align_bytes=ALIGN, bufs=1)
-            for g in range(GROUPS):
-                for offset in range(0, width, UNIT):
-                    first = (g * width + offset) * PACK
-                    engine = nc.gpsimd
-                    unit(start + offset, g, rounded[:, first : first + UNIT * PACK], engine)
-            h_codes = work.tile([P, GROUPS * width], U32, name="h_codes", align_bytes=ALIGN)
-            h_scales = work.tile([P, GROUPS * width], U8, name="h_scales", align_bytes=ALIGN)
-            nc.vector.quantize_mx(out=h_codes[:].bitcast(FP8X4), scales=h_scales[:], in_=rounded[:])
-            second(start, width, h_codes, h_scales, n == len(STRETCHES) - 1)
+        for width in STRETCHES[:-1]:
+            stretch(start, width, round_by_copy(nc.scalar.copy))
             start = start + width
-        last_stretch(start)
+        stretch(start, STRETCHES[-1], round_on_gpsimd)
+        last_stretch(S - UNIT)
         for q in range(QUADS):
-            (nc.scalar if q % 2 == 0 else nc.sync).dma_start(
+            queue = nc.scalar if q % 2 == 0 else nc.sync
+            queue.dma_start(
                 out=out_2[0, 4 * q : 4 * q + 4, :].bitcast(I32), in_=y_scales[32 * q : 32 * q + 4, :].bitcast(I32)
             )

@@ -164,25 +164,43 @@ def tile_list_opcode_trigram_families_kernel(
         def by_pairs(tile):
             return tile[:].rearrange("p (c t i) -> p c t i", t=PACK, i=2)
 
-        def unit(start, g, h_rounded, gain_engine):
+        def first_product(i, start, g):
             words, first = (early_words, start) if start < EARLY else (late_words, start - EARLY)
-            banks = {}
-            for i in PRODUCTS:
-                banks[i] = psum.tile([P, PACK, UNIT], F32, name=f"first{i}")
-                for t in range(PACK):
-                    codes, scales = stationary(i, g, t)
-                    nc.tensor.matmul_mx(
-                        out=banks[i][:, t, :], lhsT=codes, lhsT_scale=scales,
-                        rhs=words[i][:, first : first + UNIT].bitcast(FP8X4),
-                        rhs_scale=picked_scales[i][:, start : start + UNIT],
-                        start=True, stop=True,
-                    )
+            bank = psum.tile([P, PACK, UNIT], F32, name=f"first{i}")
+            for t in range(PACK):
+                codes, scales = stationary(i, g, t)
+                nc.tensor.matmul_mx(
+                    out=bank[:, t, :], lhsT=codes, lhsT_scale=scales,
+                    rhs=words[i][:, first : first + UNIT].bitcast(FP8X4),
+                    rhs_scale=picked_scales[i][:, start : start + UNIT],
+                    start=True, stop=True,
+                )
+            return bank
+
+        def first_max(start, g):
+            bank_c = first_product(PRODUCTS[0], start, g)
+            bank_b = first_product(PRODUCTS[1], start, g)
             c = work.tile([P, PACK * UNIT], F32, name="c")
-            nc.scalar.copy(out=by_pairs(c), in_=bank_by_pairs(banks[2]))
+            nc.scalar.copy(out=by_pairs(c), in_=bank_by_pairs(bank_c))
             bc = work.tile([P, PACK * UNIT], F32, name="bc")
-            nc.vector.tensor_tensor(out=by_pairs(bc), in0=bank_by_pairs(banks[1]), in1=by_pairs(c), op=ALU.max)
+            nc.vector.tensor_tensor(out=by_pairs(bc), in0=bank_by_pairs(bank_b), in1=by_pairs(c), op=ALU.max)
+            return bc
+
+        order = []
+        first = 0
+        for width in STRETCHES + (UNIT,):
+            order.extend((first + offset, g) for g in range(GROUPS) for offset in range(0, width, UNIT))
+            first = first + width
+        pending = {order[0]: first_max(*order[0])}
+
+        def unit(start, g, h_rounded, gain_engine):
+            bank_a = first_product(PRODUCTS[2], start, g)
+            following = order.index((start, g)) + 1
+            if following < len(order):
+                pending[order[following]] = first_max(*order[following])
+            bc = pending[(start, g)]
             abc = work.tile([P, PACK * UNIT], F32, name="abc")
-            nc.vector.tensor_tensor(out=by_pairs(abc), in0=bank_by_pairs(banks[0]), in1=by_pairs(bc), op=ALU.max)
+            nc.vector.tensor_tensor(out=by_pairs(abc), in0=bank_by_pairs(bank_a), in1=by_pairs(bc), op=ALU.max)
             silu = work.tile([P, PACK * UNIT], F32, name="silu")
             nc.scalar.activation(
                 out=silu[:].rearrange("p (c i t) -> p c i t", t=PACK, i=2),

@@ -27,8 +27,11 @@ PER_COLUMN = 16
 WORD = 4
 ALIGN = 64
 UNIT = 128
-EARLY = 640
-LATE = S - EARLY
+LATE_FROM = 3
+DELAY = 3
+SCALAR_SLOTS = 4
+LAST_STEP = 14
+PIECES = ((0, 256), (256, 384), (640, 384))
 STRETCHES = (256, 256, 256, 128)
 WORK_BUFS = 4
 PRODUCTS = (2, 1, 0)
@@ -47,68 +50,73 @@ def tile_list_opcode_trigram_families_kernel(
 
         table_scales = held.tile([P, T], U8, name="table_scales", align_bytes=ALIGN)
         nc.vector.memset(table_scales[:].bitcast(I32), 0)
-        raw_scales = held.tile([P, 2 * H], U8, name="raw_scales", align_bytes=ALIGN)
+        raw_scales = held.tile([P, H], U8, name="raw_scales", align_bytes=ALIGN)
         nc.vector.memset(raw_scales[:].bitcast(I32), 0)
 
         lists = [held.tile([P, S // PER_COLUMN], U16, name=f"list{i}") for i in range(3)]
         table_words = held.tile([P, T], I32, name="table_words", align_bytes=ALIGN)
         w1_raw = [held.tile([P, PACK, PASS], F32, name=f"w1_raw{g}") for g in range(GROUPS)]
         w2_raw = held.tile([P, H // 2], I32, name="w2_raw")
-        w3_raw = picked.tile([P, H], I32, name="w3_raw", offset=(3 * EARLY + (3 * LATE - H) // 2) * WORD)
-        gains = held.tile([P, GROUPS, RUN * PACK], F32, name="gains")
-        wf_raw = [held.tile([P, PACK, N], F32, name=f"wf_raw{g}") for g in range(GROUPS)]
+        middle_offset = GROUPS * PACK * N * WORD
+        late_offset = middle_offset + 3 * PIECES[1][1] * WORD
+        w3_raw = picked.tile([P, H], I32, name="w3_raw", offset=middle_offset + (3 * PIECES[1][1] - H) // 2 * WORD)
+        gains = held.tile([P, GROUPS, PACK], F32, name="gains")
+        wf_offset = [g * PACK * N * WORD for g in range(GROUPS)]
+        wf_raw = [picked.tile([P, PACK, N], F32, name=f"wf_raw{g}", offset=wf_offset[g]) for g in range(GROUPS)]
         bias = held.tile([P, PACK], F32, name="bias")
 
         w1_rows = w1.rearrange("(p j) r -> p j r", j=PACK)
-        wf_rows = wf.rearrange("(g u t v) n -> g v u t n", g=GROUPS, t=PACK, v=RUN)
-        gain_runs = gain.rearrange("(g u e) -> u g e", g=GROUPS, e=RUN * PACK)
+        wf_rows = wf.rearrange("(g p t) n -> g p t n", g=GROUPS, t=PACK)
 
-        def load_scale_rows(dst, rows):
-            for q in range(QUADS):
+        def load_scale_rows(dst, rows, quads, shift=0):
+            for q in quads:
                 nc.sync.dma_start(
-                    out=dst[32 * q : 32 * q + 4, :].bitcast(I32), in_=rows[4 * q : 4 * q + 4, :].bitcast(I32)
+                    out=dst[32 * q + shift : 32 * q + shift + 4, :].bitcast(I32), in_=rows[4 * q : 4 * q + 4, :].bitcast(I32)
                 )
 
         def load_w1(g):
             nc.sync.dma_start(out=w1_raw[g][:], in_=w1_rows[:, :, g * PASS : (g + 1) * PASS])
 
         def load_wf(g):
-            for v in range(RUN):
-                nc.sync.dma_start(out=wf_raw[g][v:P:RUN, :, :], in_=wf_rows[g, v])
+            nc.sync.dma_start(out=wf_raw[g][:], in_=wf_rows[g])
+
+        warm = held.tile([P, 2], F32, name="warm")
+        nc.gpsimd.memset(warm[:, 0:1], 0.0)
+        nc.scalar.activation(out=warm[:, 1:2], in_=warm[:, 0:1], func=ACT.Silu)
 
         nc.sync.dma_start(lists[0][:], offs)
-        load_scale_rows(table_scales[:], tab_scales[0])
+        load_scale_rows(table_scales[:], tab_scales[0], range(QUADS))
         nc.sync.dma_start(lists[1][:], offs2)
         nc.sync.dma_start(lists[2][:], offs3)
-        nc.sync.dma_start(out=bias[:], in_=bf.rearrange("(p s) -> p s", s=PACK))
         load_w1(0)
         nc.sync.dma_start(out=table_words[:], in_=tab_words[0].rearrange("p t i -> p (t i)").bitcast(I32))
+        load_scale_rows(raw_scales[:], w2_scales[0], range(QUADS))
+        load_scale_rows(raw_scales[:], w3_scales[0], range(2), 4)
         load_w1(1)
+        load_scale_rows(raw_scales[:], w3_scales[0], range(2, QUADS), 4)
         nc.sync.dma_start(out=w2_raw[:], in_=w2_words[0].bitcast(I32))
-        load_wf(0)
-        load_scale_rows(raw_scales[:, :H], w2_scales[0])
-        load_wf(1)
-        load_scale_rows(raw_scales[:, H:], w3_scales[0])
-        for v in range(RUN):
-            nc.sync.dma_start(out=gains[v:P:RUN, :, 0:GAIN_SPAN], in_=gain_runs[:, :, v : v + GAIN_SPAN])
         nc.sync.dma_start(out=w3_raw[:], in_=w3_words[0].rearrange("p e i -> p (e i)").bitcast(I32))
+        nc.sync.dma_start(out=gains[:], in_=gain.rearrange("(g p t) -> p g t", g=GROUPS, t=PACK))
+        nc.sync.dma_start(out=bias[:], in_=bf.rearrange("(p s) -> p s", s=PACK))
+        load_wf(0)
+        load_wf(1)
 
         picked_scales = [held.tile([P, S], U8, name=f"picked_scales{i}", align_bytes=ALIGN) for i in range(3)]
         for i in range(3):
             nc.vector.tensor_copy(picked_scales[i][:], table_scales[:].indirect(lists[i][:]))
 
-        def gather_words(first, width):
-            tiles = {}
-            for i in PRODUCTS:
-                tiles[i] = picked.tile(
-                    [P, width], U32, name=f"picked_words{first}_{i}", align_bytes=ALIGN,
-                    offset=(3 * first + i * width) * WORD,
-                )
-                entries = lists[i][:, first // PER_COLUMN : (first + width) // PER_COLUMN]
-                nc.vector.tensor_copy(tiles[i][:], table_words[:].bitcast(U32).indirect(entries))
-            return tiles
+        picked_words = [{}, {}, {}]
 
-        early_words = gather_words(0, EARLY)
+        def gather_words(piece, i, offset):
+            first, width = PIECES[piece]
+            tile = picked.tile([P, width], U32, name=f"picked_words{first}_{i}", align_bytes=ALIGN, offset=offset)
+            entries = lists[i][:, first // PER_COLUMN : (first + width) // PER_COLUMN]
+            nc.vector.tensor_copy(tile[:], table_words[:].bitcast(U32).indirect(entries))
+            picked_words[piece][i] = tile
+
+        unit_bytes = PACK * UNIT * WORD
+        for i in PRODUCTS:
+            gather_words(0, i, late_offset + 3 * unit_bytes + i * PIECES[0][1] * WORD)
 
         def quantize_weight(rounded, name):
             codes = held.tile([P, PASS], U32, name=f"{name}_codes", align_bytes=ALIGN)
@@ -120,35 +128,38 @@ def tile_list_opcode_trigram_families_kernel(
         for g in range(GROUPS):
             rounded = held.tile([P, PASS * PACK], BF16, name=f"w1_rounded{g}", align_bytes=ALIGN)
             nc.scalar.copy(
-                out=rounded[:].rearrange("p (t u v j) -> p t u j v", t=PACK, v=RUN, j=PACK),
-                in_=w1_raw[g][:].rearrange("p j (u t v) -> p t u j v", t=PACK, v=RUN),
+                out=rounded[:].rearrange("p (t m j) -> p m j t", t=PACK, j=PACK),
+                in_=w1_raw[g][:].rearrange("p j (m t) -> p m j t", t=PACK),
             )
             w1_q.append(quantize_weight(rounded, f"w1_{g}"))
-        for g in range(GROUPS):
+
+        def quantize_wf(g):
             rounded = held.tile([P, N * PACK], BF16, name=f"wf_rounded{g}", align_bytes=ALIGN)
-            nc.scalar.copy(
-                out=rounded[:].rearrange("p (s m t) -> p m t s", s=PACK, t=PACK),
-                in_=wf_raw[g][:].rearrange("p t (m s) -> p m t s", s=PACK),
-            )
+            for half in range(2):
+                cols = slice(half * P // 2, (half + 1) * P // 2)
+                nc.scalar.copy(
+                    out=rounded[:].rearrange("p (s m t) -> p m t s", s=PACK, t=PACK)[:, cols],
+                    in_=wf_raw[g][:].rearrange("p t (m s) -> p m t s", s=PACK)[:, cols],
+                )
             wf_q.append(quantize_weight(rounded, f"wf_{g}"))
-        gain_slots = held.tile([P, GROUPS, PACK], F32, name="gain_slots")
-        nc.gpsimd.tensor_copy(out=gain_slots[:], in_=gains[:, :, 0:GAIN_SPAN:RUN])
 
-        def reorder_columns(dst, src, words_per_run):
+        quantize_wf(0)
+
+        def reorder_columns(dst, src, per_line):
             nc.vector.tensor_copy(
-                out=dst.rearrange("p (g t u e) -> p g t u e", t=PACK, u=P // RUN, e=words_per_run),
-                in_=src.rearrange("p (g u t e) -> p g t u e", t=PACK, u=P // RUN, e=words_per_run),
+                out=dst.rearrange("p (g t c i) -> p g c t i", g=GROUPS, t=PACK, i=per_line),
+                in_=src.rearrange("p (g c i t) -> p g c t i", g=GROUPS, t=PACK, i=per_line),
             )
 
-        w23_scales = held.tile([P, 2 * H], U8, name="w23_scales", align_bytes=ALIGN)
-        reorder_columns(w23_scales[:, H:].bitcast(I32), raw_scales[:, H:].bitcast(I32), 1)
+        w23_scales = held.tile([P, H], U8, name="w23_scales", align_bytes=ALIGN)
+        reorder_columns(w23_scales[:], raw_scales[:], 16)
+        w2_codes = held.tile([P, 2 * H], U8, name="w2_codes", align_bytes=ALIGN)
+        reorder_columns(w2_codes[:].bitcast(U16), w2_raw[:].bitcast(U16), 8)
         w3_codes = held.tile([P, H], U32, name="w3_codes", align_bytes=ALIGN)
         reorder_columns(w3_codes[:].bitcast(I32), w3_raw[:], 4)
-        w2_codes = held.tile([P, 2 * H], U8, name="w2_codes", align_bytes=ALIGN)
-        reorder_columns(w2_codes[:].bitcast(I32), w2_raw[:], 2)
-        reorder_columns(w23_scales[:, :H].bitcast(I32), raw_scales[:, :H].bitcast(I32), 1)
 
-        late_words = gather_words(EARLY, LATE)
+        for i in PRODUCTS:
+            gather_words(1, i, middle_offset + i * PIECES[1][1] * WORD)
 
         def stationary(i, g, t):
             col = g * PASS + t * P
@@ -156,7 +167,7 @@ def tile_list_opcode_trigram_families_kernel(
                 return w1_q[g][0][:, t * P : (t + 1) * P].bitcast(FP8X4), w1_q[g][1][:, t * P : (t + 1) * P]
             if i == 1:
                 return w2_codes[:, 2 * col : 2 * (col + P)].bitcast(FP4X4), w23_scales[:, col : col + P]
-            return w3_codes[:, col : col + P].bitcast(FP8X4), w23_scales[:, H + col : H + col + P]
+            return w3_codes[:, col : col + P].bitcast(FP8X4), w23_scales[4:P, col : col + P]
 
         def bank_by_pairs(bank):
             return bank[:].rearrange("p t (c i) -> p c t i", i=2)
@@ -165,54 +176,78 @@ def tile_list_opcode_trigram_families_kernel(
             return tile[:].rearrange("p (c t i) -> p c t i", t=PACK, i=2)
 
         def first_product(i, start, g):
-            words, first = (early_words, start) if start < EARLY else (late_words, start - EARLY)
+            piece = max(k for k in range(len(PIECES)) if PIECES[k][0] <= start)
+            words, column = picked_words[piece], start - PIECES[piece][0]
             bank = psum.tile([P, PACK, UNIT], F32, name=f"first{i}")
             for t in range(PACK):
                 codes, scales = stationary(i, g, t)
                 nc.tensor.matmul_mx(
                     out=bank[:, t, :], lhsT=codes, lhsT_scale=scales,
-                    rhs=words[i][:, first : first + UNIT].bitcast(FP8X4),
+                    rhs=words[i][:, column : column + UNIT].bitcast(FP8X4),
                     rhs_scale=picked_scales[i][:, start : start + UNIT],
                     start=True, stop=True,
                 )
             return bank
-
-        def first_max(start, g):
-            bank_c = first_product(PRODUCTS[0], start, g)
-            bank_b = first_product(PRODUCTS[1], start, g)
-            c = work.tile([P, PACK * UNIT], F32, name="c")
-            nc.scalar.copy(out=by_pairs(c), in_=bank_by_pairs(bank_c))
-            bc = work.tile([P, PACK * UNIT], F32, name="bc")
-            nc.vector.tensor_tensor(out=by_pairs(bc), in0=bank_by_pairs(bank_b), in1=by_pairs(c), op=ALU.max)
-            return bc
 
         order = []
         first = 0
         for width in STRETCHES + (UNIT,):
             order.extend((first + offset, g) for g in range(GROUPS) for offset in range(0, width, UNIT))
             first = first + width
-        pending = {order[0]: first_max(*order[0])}
+        copied, first_maxima, later = {}, {}, {}
+
+        def copy_out(k):
+            bank = first_product(PRODUCTS[0], *order[k])
+            if k < 2:
+                c = picked.tile([P, PACK * UNIT], F32, name=f"c_held{k}", offset=wf_offset[0] + k * unit_bytes)
+            else:
+                c = work.tile([P, PACK * UNIT], F32, name="c")
+            nc.scalar.copy(out=by_pairs(c), in_=bank_by_pairs(bank))
+            copied[k] = c
+
+        def first_max(k):
+            bank = first_product(PRODUCTS[1], *order[k])
+            bc = work.tile([P, PACK * UNIT], F32, name="bc")
+            nc.vector.tensor_tensor(out=by_pairs(bc), in0=bank_by_pairs(bank), in1=by_pairs(copied[k]), op=ALU.max)
+            first_maxima[k] = bc
+
+        copy_out(0)
+        copy_out(1)
+        first_max(0)
 
         def unit(start, g, h_rounded, gain_engine):
-            bank_a = first_product(PRODUCTS[2], start, g)
-            following = order.index((start, g)) + 1
-            if following < len(order):
-                pending[order[following]] = first_max(*order[following])
-            bc = pending[(start, g)]
-            abc = work.tile([P, PACK * UNIT], F32, name="abc")
-            nc.vector.tensor_tensor(out=by_pairs(abc), in0=bank_by_pairs(bank_a), in1=by_pairs(bc), op=ALU.max)
+            k = order.index((start, g))
+            if k + 2 < len(order):
+                copy_out(k + 2)
+            bank = first_product(PRODUCTS[2], start, g)
+            if k + 1 < len(order):
+                first_max(k + 1)
+            late = k - LATE_FROM
+            if 0 <= late < 3:
+                abc = picked.tile([P, PACK * UNIT], F32, name=f"abc_held{late}", offset=late_offset + late * unit_bytes)
+            else:
+                abc = work.tile([P, PACK * UNIT], F32, name="abc")
+            nc.vector.tensor_tensor(
+                out=by_pairs(abc), in0=bank_by_pairs(bank), in1=by_pairs(first_maxima[k]), op=ALU.max
+            )
             silu = work.tile([P, PACK * UNIT], F32, name="silu")
             nc.scalar.activation(
                 out=silu[:].rearrange("p (c i t) -> p c i t", t=PACK, i=2),
                 in_=abc[:].rearrange("p (c t i) -> p c i t", t=PACK, i=2),
                 func=ACT.Silu,
             )
+            if 0 <= late < 3:
+                gather_words(2, PRODUCTS[late], late_offset + late * unit_bytes)
+            if k == 3:
+                quantize_wf(1)
             gain_engine.tensor_tensor(
                 out=h_rounded.rearrange("p (j t) -> p j t", t=PACK),
                 in0=silu[:].rearrange("p (j t) -> p j t", t=PACK),
-                in1=gain_slots[:, g, :].unsqueeze(1).to_broadcast([P, UNIT, PACK]),
+                in1=gains[:, g, :].unsqueeze(1).to_broadcast([P, UNIT, PACK]),
                 op=ALU.mult,
             )
+            for step in later.get(k, []):
+                step()
 
         def quantize_h(h_rounded, columns):
             codes = work.tile([P, columns], U32, name="h_codes", align_bytes=ALIGN)
@@ -239,54 +274,62 @@ def tile_list_opcode_trigram_families_kernel(
         y_rows = out_0.rearrange("(p s) j -> p s j", s=PACK)
         y_words = out_1[0].rearrange("p m t -> p (m t)").bitcast(I32)
 
-        def round_by_copy(copy):
-            return lambda rounded, y: copy(
-                out=rounded[:].rearrange("p (c i s) -> p c s i", s=PACK, i=4),
-                in_=y[:].rearrange("p s (c i) -> p c s i", i=4),
+        def round_y(copy, y_rounded, y, cols):
+            copy(
+                out=y_rounded[:].rearrange("p (j s) -> p j s", s=PACK)[:, cols].rearrange("p (c i) s -> p c s i", i=4),
+                in_=y[:, :, cols].rearrange("p s (c i) -> p c s i", i=4),
             )
 
-        def round_on_gpsimd(rounded, y):
-            nc.gpsimd.tensor_scalar(
-                out=rounded[:].rearrange("p (j s) -> p j s", s=PACK), in0=y[:].rearrange("p s j -> p j s"),
-                scalar1=1.0, scalar2=0.0, op0=ALU.mult, op1=ALU.add,
-            )
+        def round_on_gpsimd(out, in_):
+            nc.gpsimd.tensor_scalar(out=out, in0=in_, scalar1=1.0, scalar2=0.0, op0=ALU.mult, op1=ALU.add)
 
-        def store_y(y, start, width, queue, round_y):
+        def store_codes(y_rounded, start, width):
             cols = slice(start, start + width)
-            queue.dma_start(out=y_rows[:, :, cols], in_=y[:])
-            y_rounded = work.tile([P, width * PACK], BF16, name="y_rounded", align_bytes=ALIGN)
-            round_y(y_rounded, y)
             y_codes = work.tile([P, width], U32, name="y_codes", align_bytes=ALIGN)
             nc.vector.quantize_mx(out=y_codes[:].bitcast(FP8X4), scales=y_scales[:, cols], in_=y_rounded[:])
             nc.sync.dma_start(out=y_words[:, cols], in_=y_codes[:].bitcast(I32))
 
-        def stretch(start, width, round_y):
+        def stretch(start, width, copy):
             h_rounded = work.tile([P, GROUPS * width * PACK], BF16, name="h_rounded", align_bytes=ALIGN, bufs=1)
             for g in range(GROUPS):
                 for offset in range(0, width, UNIT):
                     first = (g * width + offset) * PACK
                     unit(start + offset, g, h_rounded[:, first : first + UNIT * PACK], nc.gpsimd)
+            last = order.index((start + width - UNIT, GROUPS - 1))
             h_codes, h_scales = quantize_h(h_rounded, GROUPS * width)
             per_bank = PASS // width
             y = work.tile([P, PACK, width], F32, name="y")
+            y_rounded = work.tile([P, width * PACK], BF16, name="y_rounded", align_bytes=ALIGN)
+            banks = []
             for b in range(PACK // per_bank):
-                bank = psum.tile([P, per_bank, width], F32, name="logits")
+                banks.append(psum.tile([P, per_bank, width], F32, name="logits"))
                 for e in range(per_bank):
                     for g in range(GROUPS):
                         cols = slice(g * width, (g + 1) * width)
                         second_pass(
-                            bank[:, e, :], g, per_bank * b + e, h_codes[:, cols], h_scales[:, cols],
+                            banks[b][:, e, :], g, per_bank * b + e, h_codes[:, cols], h_scales[:, cols],
                             g == 0, g == GROUPS - 1,
                         )
-                for e in range(per_bank):
-                    add_bias(y, per_bank * b + e, bank[:, e, :], b == 0)
-            store_y(y, start, width, nc.sync, round_y)
+
+            def biases():
+                for s in range(PACK):
+                    add_bias(y, s, banks[s // per_bank][:, s % per_bank, :], s < SCALAR_SLOTS or per_bank == PACK)
+                nc.sync.dma_start(out=y_rows[:, :, start : start + width], in_=y[:])
+
+            def rounding(offset):
+                return lambda: round_y(copy, y_rounded, y, slice(offset, offset + UNIT))
+
+            steps = [biases] + [rounding(offset) for offset in range(0, width, UNIT)]
+            for n, step in enumerate(steps):
+                later.setdefault(min(last + DELAY + n, LAST_STEP), []).append(step)
+            later[min(last + DELAY + len(steps) - 1, LAST_STEP)].append(lambda: store_codes(y_rounded, start, width))
 
         def last_stretch(start):
-            banks = [psum.tile([P, 2, UNIT], F32, name="logits") for b in range(2)]
+            banks = []
             for g in range(GROUPS):
                 h_rounded = work.tile([P, UNIT * PACK], BF16, name="h_last", align_bytes=ALIGN)
-                unit(start, g, h_rounded[:], nc.vector)
+                unit(start, g, h_rounded[:], nc.vector if g == GROUPS - 1 else nc.gpsimd)
+                banks.extend(psum.tile([P, 2, UNIT], F32, name="logits") for b in range(2 - len(banks)))
                 h_codes, h_scales = quantize_h(h_rounded, UNIT)
                 for s in range(PACK):
                     second_pass(
@@ -296,13 +339,16 @@ def tile_list_opcode_trigram_families_kernel(
             y = work.tile([P, PACK, UNIT], F32, name="y")
             for s in range(PACK):
                 add_bias(y, s, banks[s // 2][:, s % 2, :], s < 2)
-            store_y(y, start, UNIT, nc.scalar, round_by_copy(nc.vector.tensor_copy))
+            nc.scalar.dma_start(out=y_rows[:, :, start : start + UNIT], in_=y[:])
+            y_rounded = work.tile([P, UNIT * PACK], BF16, name="y_rounded", align_bytes=ALIGN)
+            round_y(nc.vector.tensor_copy, y_rounded, y, slice(0, UNIT))
+            store_codes(y_rounded, start, UNIT)
 
         start = 0
         for width in STRETCHES[:-1]:
-            stretch(start, width, round_by_copy(nc.scalar.copy))
+            stretch(start, width, nc.scalar.copy)
             start = start + width
-        stretch(start, STRETCHES[-1], round_on_gpsimd)
+        stretch(start, STRETCHES[-1], nc.vector.tensor_copy)
         last_stretch(S - UNIT)
         for q in range(QUADS):
             queue = nc.scalar if q % 2 == 0 else nc.sync

@@ -27,10 +27,9 @@ PER_COLUMN = 16
 WORD = 4
 ALIGN = 64
 UNIT = 128
-LATE_FROM = 3
+LATE_FROM = 5
 DELAY = 3
 SCALAR_SLOTS = 4
-LAST_STEP = 14
 PIECES = ((0, 256), (256, 384), (640, 384))
 STRETCHES = (256, 256, 256, 128)
 WORK_BUFS = 4
@@ -49,7 +48,7 @@ def tile_list_opcode_trigram_families_kernel(
         psum = ctx.enter_context(tc.psum_pool(name="psum", bufs=2))
 
         table_scales = held.tile([P, T], U8, name="table_scales", align_bytes=ALIGN)
-        nc.vector.memset(table_scales[:].bitcast(I32), 0)
+        nc.gpsimd.memset(table_scales[:].bitcast(I32), 0)
         raw_scales = held.tile([P, H], U8, name="raw_scales", align_bytes=ALIGN)
         nc.vector.memset(raw_scales[:].bitcast(I32), 0)
 
@@ -227,25 +226,32 @@ def tile_list_opcode_trigram_families_kernel(
                 abc = picked.tile([P, PACK * UNIT], F32, name=f"abc_held{late}", offset=late_offset + late * unit_bytes)
             else:
                 abc = work.tile([P, PACK * UNIT], F32, name="abc")
-            nc.vector.tensor_tensor(
-                out=by_pairs(abc), in0=bank_by_pairs(bank), in1=by_pairs(first_maxima[k]), op=ALU.max
-            )
+            parts = 2 if k == len(order) - 1 else 1
+            size = UNIT // parts
             silu = work.tile([P, PACK * UNIT], F32, name="silu")
-            nc.scalar.activation(
-                out=silu[:].rearrange("p (c i t) -> p c i t", t=PACK, i=2),
-                in_=abc[:].rearrange("p (c t i) -> p c i t", t=PACK, i=2),
-                func=ACT.Silu,
-            )
+            for part in range(parts):
+                pairs = slice(part * size // 2, (part + 1) * size // 2)
+                nc.vector.tensor_tensor(
+                    out=by_pairs(abc)[:, pairs], in0=bank_by_pairs(bank)[:, pairs],
+                    in1=by_pairs(first_maxima[k])[:, pairs], op=ALU.max,
+                )
+                nc.scalar.activation(
+                    out=silu[:].rearrange("p (c i t) -> p c i t", t=PACK, i=2)[:, pairs],
+                    in_=abc[:].rearrange("p (c t i) -> p c i t", t=PACK, i=2)[:, pairs],
+                    func=ACT.Silu,
+                )
             if 0 <= late < 3:
                 gather_words(2, PRODUCTS[late], late_offset + late * unit_bytes)
             if k == 3:
                 quantize_wf(1)
-            gain_engine.tensor_tensor(
-                out=h_rounded.rearrange("p (j t) -> p j t", t=PACK),
-                in0=silu[:].rearrange("p (j t) -> p j t", t=PACK),
-                in1=gains[:, g, :].unsqueeze(1).to_broadcast([P, UNIT, PACK]),
-                op=ALU.mult,
-            )
+            for part in range(parts):
+                cols = slice(part * size, (part + 1) * size)
+                gain_engine.tensor_tensor(
+                    out=h_rounded.rearrange("p (j t) -> p j t", t=PACK)[:, cols],
+                    in0=silu[:].rearrange("p (j t) -> p j t", t=PACK)[:, cols],
+                    in1=gains[:, g, :].unsqueeze(1).to_broadcast([P, size, PACK]),
+                    op=ALU.mult,
+                )
             for step in later.get(k, []):
                 step()
 
@@ -320,16 +326,16 @@ def tile_list_opcode_trigram_families_kernel(
                 return lambda: round_y(copy, y_rounded, y, slice(offset, offset + UNIT))
 
             steps = [biases] + [rounding(offset) for offset in range(0, width, UNIT)]
+            steps.append(lambda: store_codes(y_rounded, start, width))
             for n, step in enumerate(steps):
-                later.setdefault(min(last + DELAY + n, LAST_STEP), []).append(step)
-            later[min(last + DELAY + len(steps) - 1, LAST_STEP)].append(lambda: store_codes(y_rounded, start, width))
+                later.setdefault(min(last + DELAY + min(n, len(steps) - 2), len(order) - 1), []).append(step)
 
         def last_stretch(start):
             banks = []
             for g in range(GROUPS):
                 h_rounded = work.tile([P, UNIT * PACK], BF16, name="h_last", align_bytes=ALIGN)
                 unit(start, g, h_rounded[:], nc.vector if g == GROUPS - 1 else nc.gpsimd)
-                banks.extend(psum.tile([P, 2, UNIT], F32, name="logits") for b in range(2 - len(banks)))
+                banks.extend(psum.tile([P, 2, UNIT], F32, name=f"first{PRODUCTS[0]}") for b in range(2 - len(banks)))
                 h_codes, h_scales = quantize_h(h_rounded, UNIT)
                 for s in range(PACK):
                     second_pass(
@@ -346,7 +352,7 @@ def tile_list_opcode_trigram_families_kernel(
 
         start = 0
         for width in STRETCHES[:-1]:
-            stretch(start, width, nc.scalar.copy)
+            stretch(start, width, nc.scalar.copy if start < S // 2 else nc.vector.tensor_copy)
             start = start + width
         stretch(start, STRETCHES[-1], nc.vector.tensor_copy)
         last_stretch(S - UNIT)

@@ -27,13 +27,13 @@ PER_COLUMN = 16
 WORD = 4
 ALIGN = 64
 UNIT = 128
-LATE_FROM = 5
 DELAY = 3
-SCALAR_SLOTS = 4
-PIECES = ((0, 256), (256, 384), (640, 384))
-STRETCHES = (256, 256, 256, 128)
+PIECES = ((0, 512), (512, 256), (768, 256))
+AHEAD = 3
+STRETCHES = (256, 256, 128, 128)
+FIRST = 256
 WORK_BUFS = 4
-PRODUCTS = (2, 1, 0)
+PRODUCTS = (0, 2, 1)
 
 
 def tile_list_opcode_trigram_families_kernel(
@@ -54,14 +54,16 @@ def tile_list_opcode_trigram_families_kernel(
 
         lists = [held.tile([P, S // PER_COLUMN], U16, name=f"list{i}") for i in range(3)]
         table_words = held.tile([P, T], I32, name="table_words", align_bytes=ALIGN)
-        w1_raw = [held.tile([P, PACK, PASS], F32, name=f"w1_raw{g}") for g in range(GROUPS)]
         w2_raw = held.tile([P, H // 2], I32, name="w2_raw")
-        middle_offset = GROUPS * PACK * N * WORD
-        late_offset = middle_offset + 3 * PIECES[1][1] * WORD
-        w3_raw = picked.tile([P, H], I32, name="w3_raw", offset=middle_offset + (3 * PIECES[1][1] - H) // 2 * WORD)
+        unit_bytes = PACK * UNIT * WORD
+        w3_raw = picked.tile([P, H], I32, name="w3_raw", offset=0)
+        c_offset = H * WORD
         gains = held.tile([P, GROUPS, PACK], F32, name="gains")
-        wf_offset = [g * PACK * N * WORD for g in range(GROUPS)]
-        wf_raw = [picked.tile([P, PACK, N], F32, name=f"wf_raw{g}", offset=wf_offset[g]) for g in range(GROUPS)]
+        wf_offset = [c_offset + (2 + PACK * g) * unit_bytes for g in range(GROUPS)]
+        w1_offset = [c_offset + (20 + PACK * g) * unit_bytes for g in range(GROUPS)]
+        w1_raw = [picked.tile([P, PACK, PASS], F32, name=f"w1_raw{g}", offset=w1_offset[g]) for g in range(GROUPS)]
+        lane_offset = [c_offset + (28 + 7 * lane) * unit_bytes for lane in range(2)]
+        wf_raw = [held.tile([P, PACK, N], F32, name=f"wf_raw{g}") for g in range(GROUPS)]
         bias = held.tile([P, PACK], F32, name="bias")
 
         w1_rows = w1.rearrange("(p j) r -> p j r", j=PACK)
@@ -85,64 +87,70 @@ def tile_list_opcode_trigram_families_kernel(
 
         nc.sync.dma_start(lists[0][:], offs)
         load_scale_rows(table_scales[:], tab_scales[0], range(QUADS))
-        nc.sync.dma_start(lists[1][:], offs2)
         nc.sync.dma_start(lists[2][:], offs3)
-        load_w1(0)
         nc.sync.dma_start(out=table_words[:], in_=tab_words[0].rearrange("p t i -> p (t i)").bitcast(I32))
+        nc.sync.dma_start(lists[1][:], offs2)
+        load_scale_rows(raw_scales[:], w3_scales[0], range(QUADS), 4)
+        load_w1(0)
         load_scale_rows(raw_scales[:], w2_scales[0], range(QUADS))
-        load_scale_rows(raw_scales[:], w3_scales[0], range(2), 4)
         load_w1(1)
-        load_scale_rows(raw_scales[:], w3_scales[0], range(2, QUADS), 4)
-        nc.sync.dma_start(out=w2_raw[:], in_=w2_words[0].bitcast(I32))
-        nc.sync.dma_start(out=w3_raw[:], in_=w3_words[0].rearrange("p e i -> p (e i)").bitcast(I32))
         nc.sync.dma_start(out=gains[:], in_=gain.rearrange("(g p t) -> p g t", g=GROUPS, t=PACK))
         nc.sync.dma_start(out=bias[:], in_=bf.rearrange("(p s) -> p s", s=PACK))
+        nc.sync.dma_start(out=w3_raw[:], in_=w3_words[0].rearrange("p e i -> p (e i)").bitcast(I32))
+        nc.sync.dma_start(out=w2_raw[:], in_=w2_words[0].bitcast(I32))
         load_wf(0)
         load_wf(1)
 
-        picked_scales = [held.tile([P, S], U8, name=f"picked_scales{i}", align_bytes=ALIGN) for i in range(3)]
-        for i in range(3):
-            nc.vector.tensor_copy(picked_scales[i][:], table_scales[:].indirect(lists[i][:]))
-
         picked_words = [{}, {}, {}]
+        picked_scales = [{}, {}, {}]
 
-        def gather_words(piece, i, offset):
+        def gather(piece, i, window, dtype, into, pool, offset, label):
             first, width = PIECES[piece]
-            tile = picked.tile([P, width], U32, name=f"picked_words{first}_{i}", align_bytes=ALIGN, offset=offset)
+            tile = pool.tile([P, width], dtype, name=f"{label}{first}_{i}", align_bytes=ALIGN, offset=offset)
             entries = lists[i][:, first // PER_COLUMN : (first + width) // PER_COLUMN]
-            nc.vector.tensor_copy(tile[:], table_words[:].bitcast(U32).indirect(entries))
-            picked_words[piece][i] = tile
+            nc.vector.tensor_copy(tile[:], window.indirect(entries))
+            into[piece][i] = tile
 
-        unit_bytes = PACK * UNIT * WORD
-        for i in PRODUCTS:
-            gather_words(0, i, late_offset + 3 * unit_bytes + i * PIECES[0][1] * WORD)
+        def gather_words(piece, i, pool, offset=None):
+            gather(piece, i, table_words[:].bitcast(U32), U32, picked_words, pool, offset, "picked_words")
 
-        def quantize_weight(rounded, name):
-            codes = held.tile([P, PASS], U32, name=f"{name}_codes", align_bytes=ALIGN)
-            scales = held.tile([P, PASS], U8, name=f"{name}_scales", align_bytes=ALIGN)
+        def gather_scales(piece, i, pool, offset=None):
+            gather(piece, i, table_scales[:], U8, picked_scales, pool, offset, "picked_scales")
+
+        gather_scales(0, PRODUCTS[0], held)
+        gather_scales(0, PRODUCTS[1], held)
+        gather_words(0, PRODUCTS[0], held)
+        gather_scales(0, PRODUCTS[2], held)
+        gather_words(0, PRODUCTS[1], held)
+        gather_words(0, PRODUCTS[2], held)
+
+        def quantize_weight(rounded, name, pool=held, offset=None):
+            width = rounded.shape[1] // PACK
+            codes = pool.tile([P, width], U32, name=f"{name}_codes", align_bytes=ALIGN, offset=offset)
+            scales = held.tile([P, width], U8, name=f"{name}_scales", align_bytes=ALIGN)
             nc.vector.quantize_mx(out=codes[:].bitcast(FP8X4), scales=scales[:], in_=rounded[:])
             return codes, scales
 
-        w1_q, wf_q = [], []
-        for g in range(GROUPS):
-            rounded = held.tile([P, PASS * PACK], BF16, name=f"w1_rounded{g}", align_bytes=ALIGN)
+        w1_q, wf_q = {}, {}
+        w1_rounded = [held.tile([P, PASS * PACK], BF16, name=f"w1_rounded{g}", align_bytes=ALIGN) for g in range(GROUPS)]
+        wf_rounded = picked.tile([P, GROUPS * N * PACK], BF16, name="wf_rounded", align_bytes=ALIGN, offset=wf_offset[0])
+
+        def round_w1(g, cols):
             nc.scalar.copy(
-                out=rounded[:].rearrange("p (t m j) -> p m j t", t=PACK, j=PACK),
-                in_=w1_raw[g][:].rearrange("p j (m t) -> p m j t", t=PACK),
+                out=w1_rounded[g][:].rearrange("p (t m j) -> p m j t", t=PACK, j=PACK)[:, cols],
+                in_=w1_raw[g][:].rearrange("p j (m t) -> p m j t", t=PACK)[:, cols],
             )
-            w1_q.append(quantize_weight(rounded, f"w1_{g}"))
 
-        def quantize_wf(g):
-            rounded = held.tile([P, N * PACK], BF16, name=f"wf_rounded{g}", align_bytes=ALIGN)
-            for half in range(2):
-                cols = slice(half * P // 2, (half + 1) * P // 2)
-                nc.scalar.copy(
-                    out=rounded[:].rearrange("p (s m t) -> p m t s", s=PACK, t=PACK)[:, cols],
-                    in_=wf_raw[g][:].rearrange("p t (m s) -> p m t s", s=PACK)[:, cols],
-                )
-            wf_q.append(quantize_weight(rounded, f"wf_{g}"))
+        def round_wf(g):
+            nc.gpsimd.tensor_scalar(
+                out=wf_rounded[:].rearrange("p (g s m t) -> p g m s t", g=GROUPS, s=PACK, t=PACK)[:, g],
+                in0=wf_raw[g][:].rearrange("p t (m s) -> p m s t", s=PACK),
+                scalar1=1.0, scalar2=0.0, op0=ALU.mult, op1=ALU.add,
+            )
 
-        quantize_wf(0)
+        round_w1(0, slice(0, P))
+        round_w1(1, slice(0, P))
+        w1_q[0] = quantize_weight(w1_rounded[0], "w1_0")
 
         def reorder_columns(dst, src, per_line):
             nc.vector.tensor_copy(
@@ -152,13 +160,19 @@ def tile_list_opcode_trigram_families_kernel(
 
         w23_scales = held.tile([P, H], U8, name="w23_scales", align_bytes=ALIGN)
         reorder_columns(w23_scales[:], raw_scales[:], 16)
-        w2_codes = held.tile([P, 2 * H], U8, name="w2_codes", align_bytes=ALIGN)
-        reorder_columns(w2_codes[:].bitcast(U16), w2_raw[:].bitcast(U16), 8)
         w3_codes = held.tile([P, H], U32, name="w3_codes", align_bytes=ALIGN)
         reorder_columns(w3_codes[:].bitcast(I32), w3_raw[:], 4)
-
-        for i in PRODUCTS:
-            gather_words(1, i, middle_offset + i * PIECES[1][1] * WORD)
+        w2_codes = held.tile([P, 2 * H], U8, name="w2_codes", align_bytes=ALIGN)
+        reorder_columns(w2_codes[:].bitcast(U16), w2_raw[:].bitcast(U16), 8)
+        late = [(piece, i, call) for piece in (1, 2) for i in PRODUCTS for call in (gather_scales, gather_words)]
+        for n in range(2):
+            piece, i, call = late[n]
+            call(piece, i, picked, (2 + n) * unit_bytes // 2)
+        late = late[2:]
+        w1_q[1] = quantize_weight(w1_rounded[1], "w1_1", picked, 0)
+        round_wf(0)
+        round_wf(1)
+        wf_q[0] = quantize_weight(wf_rounded, "wf")
 
         def stationary(i, g, t):
             col = g * PASS + t * P
@@ -176,29 +190,33 @@ def tile_list_opcode_trigram_families_kernel(
 
         def first_product(i, start, g):
             piece = max(k for k in range(len(PIECES)) if PIECES[k][0] <= start)
-            words, column = picked_words[piece], start - PIECES[piece][0]
+            words, planes, column = picked_words[piece], picked_scales[piece], start - PIECES[piece][0]
             bank = psum.tile([P, PACK, UNIT], F32, name=f"first{i}")
             for t in range(PACK):
                 codes, scales = stationary(i, g, t)
                 nc.tensor.matmul_mx(
                     out=bank[:, t, :], lhsT=codes, lhsT_scale=scales,
                     rhs=words[i][:, column : column + UNIT].bitcast(FP8X4),
-                    rhs_scale=picked_scales[i][:, start : start + UNIT],
+                    rhs_scale=planes[i][:, column : column + UNIT],
                     start=True, stop=True,
                 )
             return bank
 
         order = []
         first = 0
-        for width in STRETCHES + (UNIT,):
+        for width in STRETCHES + (2 * UNIT,):
             order.extend((first + offset, g) for g in range(GROUPS) for offset in range(0, width, UNIT))
             first = first + width
         copied, first_maxima, later = {}, {}, {}
+        c_place = {k: w1_offset[1] + k * unit_bytes for k in range(3)}
+        silu_place = {}
+        bc_place = {k: wf_offset[0] + (k - 1) * unit_bytes for k in (3, 4)}
+        abc_place = [lane_offset[k % 2] + k // 2 * 3 * unit_bytes // 4 for k in range(len(order))]
 
         def copy_out(k):
             bank = first_product(PRODUCTS[0], *order[k])
-            if k < 2:
-                c = picked.tile([P, PACK * UNIT], F32, name=f"c_held{k}", offset=wf_offset[0] + k * unit_bytes)
+            if k in c_place:
+                c = picked.tile([P, PACK * UNIT], F32, name=f"c_held{k}", offset=c_place[k])
             else:
                 c = work.tile([P, PACK * UNIT], F32, name="c")
             nc.scalar.copy(out=by_pairs(c), in_=bank_by_pairs(bank))
@@ -206,29 +224,45 @@ def tile_list_opcode_trigram_families_kernel(
 
         def first_max(k):
             bank = first_product(PRODUCTS[1], *order[k])
-            bc = work.tile([P, PACK * UNIT], F32, name="bc")
+            if k in bc_place:
+                bc = picked.tile([P, PACK * UNIT], F32, name=f"bc_held{k}", offset=bc_place[k])
+            else:
+                bc = work.tile([P, PACK * UNIT], F32, name="bc")
             nc.vector.tensor_tensor(out=by_pairs(bc), in0=bank_by_pairs(bank), in1=by_pairs(copied[k]), op=ALU.max)
             first_maxima[k] = bc
 
-        copy_out(0)
-        copy_out(1)
+        for k in range(AHEAD):
+            copy_out(k)
         first_max(0)
+
+        silus = {}
+
+        def apply_gain(engine, k, h_rounded):
+            parts = 2 if k == len(order) - 1 else 1
+            size = UNIT // parts
+            for part in range(parts):
+                cols = slice(part * size, (part + 1) * size)
+                engine.tensor_tensor(
+                    out=h_rounded.rearrange("p (j t) -> p j t", t=PACK)[:, cols],
+                    in0=silus[k][:].rearrange("p (j t) -> p j t", t=PACK)[:, cols],
+                    in1=gains[:, order[k][1], :].unsqueeze(1).to_broadcast([P, size, PACK]),
+                    op=ALU.mult,
+                )
 
         def unit(start, g, h_rounded, gain_engine):
             k = order.index((start, g))
-            if k + 2 < len(order):
-                copy_out(k + 2)
+            if k + AHEAD < len(order):
+                copy_out(k + AHEAD)
             bank = first_product(PRODUCTS[2], start, g)
             if k + 1 < len(order):
                 first_max(k + 1)
-            late = k - LATE_FROM
-            if 0 <= late < 3:
-                abc = picked.tile([P, PACK * UNIT], F32, name=f"abc_held{late}", offset=late_offset + late * unit_bytes)
-            else:
-                abc = work.tile([P, PACK * UNIT], F32, name="abc")
+            abc = picked.tile([P, PACK * UNIT], F32, name=f"abc{k}", offset=abc_place[k])
             parts = 2 if k == len(order) - 1 else 1
             size = UNIT // parts
-            silu = work.tile([P, PACK * UNIT], F32, name="silu")
+            if k in silu_place:
+                silu = picked.tile([P, PACK * UNIT], F32, name=f"silu_held{k}", offset=silu_place[k])
+            else:
+                silu = work.tile([P, PACK * UNIT], F32, name="silu")
             for part in range(parts):
                 pairs = slice(part * size // 2, (part + 1) * size // 2)
                 nc.vector.tensor_tensor(
@@ -240,35 +274,32 @@ def tile_list_opcode_trigram_families_kernel(
                     in_=abc[:].rearrange("p (c t i) -> p c i t", t=PACK, i=2)[:, pairs],
                     func=ACT.Silu,
                 )
-            if 0 <= late < 3:
-                gather_words(2, PRODUCTS[late], late_offset + late * unit_bytes)
-            if k == 3:
-                quantize_wf(1)
-            for part in range(parts):
-                cols = slice(part * size, (part + 1) * size)
-                gain_engine.tensor_tensor(
-                    out=h_rounded.rearrange("p (j t) -> p j t", t=PACK)[:, cols],
-                    in0=silu[:].rearrange("p (j t) -> p j t", t=PACK)[:, cols],
-                    in1=gains[:, g, :].unsqueeze(1).to_broadcast([P, size, PACK]),
-                    op=ALU.mult,
-                )
+            if k < len(late):
+                piece, i, call = late[k]
+                call(piece, i, picked, c_place[k + 1] if k < 2 else abc_place[k - 2])
+            silus[k] = silu
+            if gain_engine is not None:
+                apply_gain(gain_engine, k, h_rounded)
             for step in later.get(k, []):
                 step()
 
-        def quantize_h(h_rounded, columns):
+        def quantize_h(h_rounded, columns, place=None):
             codes = work.tile([P, columns], U32, name="h_codes", align_bytes=ALIGN)
-            scales = work.tile([P, columns], U8, name="h_scales", align_bytes=ALIGN)
+            if place is None:
+                scales = work.tile([P, columns], U8, name="h_scales", align_bytes=ALIGN)
+            else:
+                scales = picked.tile([P, columns], U8, name=f"h_scales{place}", align_bytes=ALIGN, offset=place)
             nc.vector.quantize_mx(out=codes[:].bitcast(FP8X4), scales=scales[:], in_=h_rounded[:])
             return codes, scales
 
         def second_pass(out, g, s, h_codes, h_scales, start, stop):
             nc.tensor.matmul_mx(
-                out=out, lhsT=wf_q[g][0][:, s * P : (s + 1) * P].bitcast(FP8X4),
-                lhsT_scale=wf_q[g][1][:, s * P : (s + 1) * P],
+                out=out, lhsT=wf_q[0][0][:, g * N + s * P : g * N + (s + 1) * P].bitcast(FP8X4),
+                lhsT_scale=wf_q[0][1][:, g * N + s * P : g * N + (s + 1) * P],
                 rhs=h_codes.bitcast(FP8X4), rhs_scale=h_scales, start=start, stop=stop,
             )
 
-        def add_bias(y, s, logits, on_scalar):
+        def add_bias(y, s, logits, on_scalar=True):
             if on_scalar:
                 nc.scalar.activation(out=y[:, s, :], in_=logits, func=ACT.Identity, bias=bias[:, s : s + 1])
             else:
@@ -286,23 +317,32 @@ def tile_list_opcode_trigram_families_kernel(
                 in_=y[:, :, cols].rearrange("p s (c i) -> p c s i", i=4),
             )
 
-        def round_on_gpsimd(out, in_):
-            nc.gpsimd.tensor_scalar(out=out, in0=in_, scalar1=1.0, scalar2=0.0, op0=ALU.mult, op1=ALU.add)
-
         def store_codes(y_rounded, start, width):
             cols = slice(start, start + width)
             y_codes = work.tile([P, width], U32, name="y_codes", align_bytes=ALIGN)
             nc.vector.quantize_mx(out=y_codes[:].bitcast(FP8X4), scales=y_scales[:, cols], in_=y_rounded[:])
             nc.sync.dma_start(out=y_words[:, cols], in_=y_codes[:].bitcast(I32))
 
+        h_q = {}
+
+        def batch(units):
+            if units[0] == order[0]:
+                h_rounded = picked.tile([P, len(units) * UNIT * PACK], BF16, name="h_first", align_bytes=ALIGN, offset=wf_offset[0])
+            else:
+                h_rounded = work.tile([P, len(units) * UNIT * PACK], BF16, name="h_rounded", align_bytes=ALIGN, bufs=2)
+            for n, (first, g) in enumerate(units):
+                unit(first, g, h_rounded[:, n * UNIT * PACK : (n + 1) * UNIT * PACK], nc.gpsimd)
+            last = order.index(units[-1])
+
+            def quantize():
+                codes, scales = quantize_h(h_rounded, len(units) * UNIT, abc_place[last + 1] + unit_bytes // 2)
+                for n, key in enumerate(units):
+                    h_q[key] = (codes, scales, n * UNIT)
+
+            return last, quantize
+
         def stretch(start, width, copy):
-            h_rounded = work.tile([P, GROUPS * width * PACK], BF16, name="h_rounded", align_bytes=ALIGN, bufs=1)
-            for g in range(GROUPS):
-                for offset in range(0, width, UNIT):
-                    first = (g * width + offset) * PACK
-                    unit(start + offset, g, h_rounded[:, first : first + UNIT * PACK], nc.gpsimd)
             last = order.index((start + width - UNIT, GROUPS - 1))
-            h_codes, h_scales = quantize_h(h_rounded, GROUPS * width)
             per_bank = PASS // width
             y = work.tile([P, PACK, width], F32, name="y")
             y_rounded = work.tile([P, width * PACK], BF16, name="y_rounded", align_bytes=ALIGN)
@@ -311,7 +351,8 @@ def tile_list_opcode_trigram_families_kernel(
                 banks.append(psum.tile([P, per_bank, width], F32, name="logits"))
                 for e in range(per_bank):
                     for g in range(GROUPS):
-                        cols = slice(g * width, (g + 1) * width)
+                        h_codes, h_scales, column = h_q[(start, g)]
+                        cols = slice(column, column + width)
                         second_pass(
                             banks[b][:, e, :], g, per_bank * b + e, h_codes[:, cols], h_scales[:, cols],
                             g == 0, g == GROUPS - 1,
@@ -319,7 +360,7 @@ def tile_list_opcode_trigram_families_kernel(
 
             def biases():
                 for s in range(PACK):
-                    add_bias(y, s, banks[s // per_bank][:, s % per_bank, :], s < SCALAR_SLOTS or per_bank == PACK)
+                    add_bias(y, s, banks[s // per_bank][:, s % per_bank, :])
                 nc.sync.dma_start(out=y_rows[:, :, start : start + width], in_=y[:])
 
             def rounding(offset):
@@ -328,34 +369,53 @@ def tile_list_opcode_trigram_families_kernel(
             steps = [biases] + [rounding(offset) for offset in range(0, width, UNIT)]
             steps.append(lambda: store_codes(y_rounded, start, width))
             for n, step in enumerate(steps):
-                later.setdefault(min(last + DELAY + min(n, len(steps) - 2), len(order) - 1), []).append(step)
+                when = last + DELAY + min(n, len(steps) - 2)
+                later.setdefault(when if when < len(order) - 2 else len(order), []).append(step)
+
+        def second_stage(start, width, copy):
+            return lambda: stretch(start, width, copy)
 
         def last_stretch(start):
+            last, quantize = batch([(start, 0), (start + UNIT, 0)])
+            rounded = []
+            for n in range(2):
+                rounded.append(work.tile([P, UNIT * PACK], BF16, name="h_last", align_bytes=ALIGN))
+                unit(start + n * UNIT, 1, rounded[n][:], None)
+            for n in range(2):
+                apply_gain(nc.vector, len(order) - 2 + n, rounded[n][:])
+                if n == 0:
+                    quantize()
             banks = []
-            for g in range(GROUPS):
-                h_rounded = work.tile([P, UNIT * PACK], BF16, name="h_last", align_bytes=ALIGN)
-                unit(start, g, h_rounded[:], nc.vector if g == GROUPS - 1 else nc.gpsimd)
-                banks.extend(psum.tile([P, 2, UNIT], F32, name=f"first{PRODUCTS[0]}") for b in range(2 - len(banks)))
-                h_codes, h_scales = quantize_h(h_rounded, UNIT)
+            for n in range(2):
+                banks.append([psum.tile([P, 2, UNIT], F32, name=f"first{PRODUCTS[n]}") for b in range(2)])
+                h_codes, h_scales, column = h_q[(start + n * UNIT, 0)]
+                cols = slice(column, column + UNIT)
                 for s in range(PACK):
-                    second_pass(
-                        banks[s // 2][:, s % 2, :], g, s, h_codes[:], h_scales[:],
-                        g == 0 and s % 2 == 0, g == GROUPS - 1 and s % 2 == 1,
-                    )
-            y = work.tile([P, PACK, UNIT], F32, name="y")
-            for s in range(PACK):
-                add_bias(y, s, banks[s // 2][:, s % 2, :], s < 2)
-            nc.scalar.dma_start(out=y_rows[:, :, start : start + UNIT], in_=y[:])
-            y_rounded = work.tile([P, UNIT * PACK], BF16, name="y_rounded", align_bytes=ALIGN)
-            round_y(nc.vector.tensor_copy, y_rounded, y, slice(0, UNIT))
-            store_codes(y_rounded, start, UNIT)
+                    second_pass(banks[n][s // 2][:, s % 2, :], 0, s, h_codes[:, cols], h_scales[:, cols], s % 2 == 0, False)
+            for n in range(2):
+                h_codes, h_scales = quantize_h(rounded[n], UNIT)
+                for s in range(PACK):
+                    second_pass(banks[n][s // 2][:, s % 2, :], 1, s, h_codes[:], h_scales[:], False, s % 2 == 1)
+            for step in later.get(len(order), []):
+                step()
+            for n in range(2):
+                first = start + n * UNIT
+                y = work.tile([P, PACK, UNIT], F32, name="y")
+                for s in range(PACK):
+                    add_bias(y, s, banks[n][s // 2][:, s % 2, :], n == 0 or s < 2)
+                queue = nc.sync if n == 0 else nc.scalar
+                queue.dma_start(out=y_rows[:, :, first : first + UNIT], in_=y[:])
+                y_rounded = work.tile([P, UNIT * PACK], BF16, name="y_rounded", align_bytes=ALIGN)
+                round_y(nc.vector.tensor_copy, y_rounded, y, slice(0, UNIT))
+                store_codes(y_rounded, first, UNIT)
 
         start = 0
-        for width in STRETCHES[:-1]:
-            stretch(start, width, nc.scalar.copy if start < S // 2 else nc.vector.tensor_copy)
+        for width in STRETCHES:
+            last, quantize = batch([(first, g) for first, g in order if start <= first < start + width])
+            copy = nc.scalar.copy if start < S - 3 * UNIT else nc.vector.tensor_copy
+            later.setdefault(last + 2, []).extend([quantize, second_stage(start, width, copy)])
             start = start + width
-        stretch(start, STRETCHES[-1], nc.vector.tensor_copy)
-        last_stretch(S - UNIT)
+        last_stretch(S - 2 * UNIT)
         for q in range(QUADS):
             queue = nc.scalar if q % 2 == 0 else nc.sync
             queue.dma_start(

@@ -28,8 +28,14 @@ WORD = 4
 ALIGN = 64
 UNIT = 128
 DELAY = 3
-PIECES = ((0, 512), (512, 256), (768, 256))
-AHEAD = 3
+PIECES = ((0, 256), (256, 256), (512, 256), (768, 256))
+AHEAD = 2
+COPY_AHEAD = 2
+EARLY = 1
+GATHER_AT = (0, 1, 4, 5, 6, 8, 9, 10)
+C_LEAD = 5
+Y_LAG = 8
+LAST_ON_VECTOR = False
 STRETCHES = (256, 256, 128, 128)
 FIRST = 256
 WORK_BUFS = 4
@@ -49,8 +55,6 @@ def tile_list_opcode_trigram_families_kernel(
 
         table_scales = held.tile([P, T], U8, name="table_scales", align_bytes=ALIGN)
         nc.gpsimd.memset(table_scales[:].bitcast(I32), 0)
-        raw_scales = held.tile([P, H], U8, name="raw_scales", align_bytes=ALIGN)
-        nc.vector.memset(raw_scales[:].bitcast(I32), 0)
 
         lists = [held.tile([P, S // PER_COLUMN], U16, name=f"list{i}") for i in range(3)]
         table_words = held.tile([P, T], I32, name="table_words", align_bytes=ALIGN)
@@ -59,11 +63,14 @@ def tile_list_opcode_trigram_families_kernel(
         w3_raw = picked.tile([P, H], I32, name="w3_raw", offset=0)
         c_offset = H * WORD
         gains = held.tile([P, GROUPS, PACK], F32, name="gains")
-        wf_offset = [c_offset + (2 + PACK * g) * unit_bytes for g in range(GROUPS)]
-        w1_offset = [c_offset + (20 + PACK * g) * unit_bytes for g in range(GROUPS)]
+        w1_offset = [c_offset + (PACK * g) * unit_bytes for g in range(GROUPS)]
         w1_raw = [picked.tile([P, PACK, PASS], F32, name=f"w1_raw{g}", offset=w1_offset[g]) for g in range(GROUPS)]
-        lane_offset = [c_offset + (28 + 7 * lane) * unit_bytes for lane in range(2)]
-        wf_raw = [held.tile([P, PACK, N], F32, name=f"wf_raw{g}") for g in range(GROUPS)]
+        wf_offset = [c_offset + PACK * (GROUPS + g) * unit_bytes for g in range(GROUPS)]
+        wf_raw = [picked.tile([P, PACK, N], F32, name=f"wf_raw{g}", offset=wf_offset[g]) for g in range(GROUPS)]
+        scales_offset = c_offset + 2 * GROUPS * PACK * unit_bytes
+        region_offset = scales_offset + 2 * H
+        raw_scales = picked.tile([P, H], U8, name="raw_scales", align_bytes=ALIGN, offset=scales_offset)
+        nc.vector.memset(raw_scales[:].bitcast(I32), 0)
         bias = held.tile([P, PACK], F32, name="bias")
 
         w1_rows = w1.rearrange("(p j) r -> p j r", j=PACK)
@@ -86,54 +93,51 @@ def tile_list_opcode_trigram_families_kernel(
         nc.scalar.activation(out=warm[:, 1:2], in_=warm[:, 0:1], func=ACT.Silu)
 
         nc.sync.dma_start(lists[0][:], offs)
-        load_scale_rows(table_scales[:], tab_scales[0], range(QUADS))
         nc.sync.dma_start(lists[2][:], offs3)
-        nc.sync.dma_start(out=table_words[:], in_=tab_words[0].rearrange("p t i -> p (t i)").bitcast(I32))
-        nc.sync.dma_start(lists[1][:], offs2)
-        load_scale_rows(raw_scales[:], w3_scales[0], range(QUADS), 4)
+        load_scale_rows(table_scales[:], tab_scales[0], range(QUADS))
         load_w1(0)
-        load_scale_rows(raw_scales[:], w2_scales[0], range(QUADS))
+        nc.sync.dma_start(lists[1][:], offs2)
         load_w1(1)
-        nc.sync.dma_start(out=gains[:], in_=gain.rearrange("(g p t) -> p g t", g=GROUPS, t=PACK))
-        nc.sync.dma_start(out=bias[:], in_=bf.rearrange("(p s) -> p s", s=PACK))
+        load_scale_rows(raw_scales[:], w3_scales[0], range(QUADS), 4)
+        nc.sync.dma_start(out=table_words[:], in_=tab_words[0].rearrange("p t i -> p (t i)").bitcast(I32))
+        load_scale_rows(raw_scales[:], w2_scales[0], range(QUADS))
+        load_wf(0)
         nc.sync.dma_start(out=w3_raw[:], in_=w3_words[0].rearrange("p e i -> p (e i)").bitcast(I32))
         nc.sync.dma_start(out=w2_raw[:], in_=w2_words[0].bitcast(I32))
-        load_wf(0)
+        nc.sync.dma_start(out=gains[:], in_=gain.rearrange("(g p t) -> p g t", g=GROUPS, t=PACK))
+        nc.sync.dma_start(out=bias[:], in_=bf.rearrange("(p s) -> p s", s=PACK))
         load_wf(1)
 
-        picked_words = [{}, {}, {}]
-        picked_scales = [{}, {}, {}]
+        picked_scales = [held.tile([P, S], U8, name=f"picked_scales{i}", align_bytes=ALIGN) for i in range(3)]
+        for i in PRODUCTS:
+            nc.vector.tensor_copy(picked_scales[i][:], table_scales[:].indirect(lists[i][:]))
 
-        def gather(piece, i, window, dtype, into, pool, offset, label):
-            first, width = PIECES[piece]
-            tile = pool.tile([P, width], dtype, name=f"{label}{first}_{i}", align_bytes=ALIGN, offset=offset)
-            entries = lists[i][:, first // PER_COLUMN : (first + width) // PER_COLUMN]
-            nc.vector.tensor_copy(tile[:], window.indirect(entries))
-            into[piece][i] = tile
+        picked_words = [{} for piece in PIECES]
 
         def gather_words(piece, i, pool, offset=None):
-            gather(piece, i, table_words[:].bitcast(U32), U32, picked_words, pool, offset, "picked_words")
+            first, width = PIECES[piece]
+            tile = pool.tile([P, width], U32, name=f"picked_words{first}_{i}", align_bytes=ALIGN, offset=offset)
+            entries = lists[i][:, first // PER_COLUMN : (first + width) // PER_COLUMN]
+            nc.vector.tensor_copy(tile[:], table_words[:].bitcast(U32).indirect(entries))
+            picked_words[piece][i] = tile
 
-        def gather_scales(piece, i, pool, offset=None):
-            gather(piece, i, table_scales[:], U8, picked_scales, pool, offset, "picked_scales")
-
-        gather_scales(0, PRODUCTS[0], held)
-        gather_scales(0, PRODUCTS[1], held)
         gather_words(0, PRODUCTS[0], held)
-        gather_scales(0, PRODUCTS[2], held)
         gather_words(0, PRODUCTS[1], held)
         gather_words(0, PRODUCTS[2], held)
 
-        def quantize_weight(rounded, name, pool=held, offset=None):
-            width = rounded.shape[1] // PACK
-            codes = pool.tile([P, width], U32, name=f"{name}_codes", align_bytes=ALIGN, offset=offset)
-            scales = held.tile([P, width], U8, name=f"{name}_scales", align_bytes=ALIGN)
+        def quantize_weight(rounded, name, offset=None):
+            codes = held.tile([P, PASS], U32, name=f"{name}_codes", align_bytes=ALIGN)
+            pool = held if offset is None else picked
+            scales = pool.tile([P, PASS], U8, name=f"{name}_scales", align_bytes=ALIGN, offset=offset)
             nc.vector.quantize_mx(out=codes[:].bitcast(FP8X4), scales=scales[:], in_=rounded[:])
             return codes, scales
 
         w1_q, wf_q = {}, {}
         w1_rounded = [held.tile([P, PASS * PACK], BF16, name=f"w1_rounded{g}", align_bytes=ALIGN) for g in range(GROUPS)]
-        wf_rounded = picked.tile([P, GROUPS * N * PACK], BF16, name="wf_rounded", align_bytes=ALIGN, offset=wf_offset[0])
+        wf_rounded = [
+            work.tile([P, PACK * N], BF16, name="h_rounded", align_bytes=ALIGN, bufs=1),
+            held.tile([P, PACK * N], BF16, name="wf_rounded", align_bytes=ALIGN),
+        ]
 
         def round_w1(g, cols):
             nc.scalar.copy(
@@ -141,38 +145,32 @@ def tile_list_opcode_trigram_families_kernel(
                 in_=w1_raw[g][:].rearrange("p j (m t) -> p m j t", t=PACK)[:, cols],
             )
 
-        def round_wf(g):
-            nc.gpsimd.tensor_scalar(
-                out=wf_rounded[:].rearrange("p (g s m t) -> p g m s t", g=GROUPS, s=PACK, t=PACK)[:, g],
-                in0=wf_raw[g][:].rearrange("p t (m s) -> p m s t", s=PACK),
-                scalar1=1.0, scalar2=0.0, op0=ALU.mult, op1=ALU.add,
+        def round_wf(g, cols):
+            nc.scalar.copy(
+                out=wf_rounded[g][:].rearrange("p (s m t) -> p m t s", s=PACK, t=PACK)[:, cols],
+                in_=wf_raw[g][:].rearrange("p t (m s) -> p m t s", s=PACK)[:, cols],
             )
 
         round_w1(0, slice(0, P))
         round_w1(1, slice(0, P))
         w1_q[0] = quantize_weight(w1_rounded[0], "w1_0")
 
-        def reorder_columns(dst, src, per_line):
-            nc.vector.tensor_copy(
+        def reorder_columns(dst, src, per_line, engine=nc.vector):
+            engine.tensor_copy(
                 out=dst.rearrange("p (g t c i) -> p g c t i", g=GROUPS, t=PACK, i=per_line),
                 in_=src.rearrange("p (g c i t) -> p g c t i", g=GROUPS, t=PACK, i=per_line),
             )
 
         w23_scales = held.tile([P, H], U8, name="w23_scales", align_bytes=ALIGN)
-        reorder_columns(w23_scales[:], raw_scales[:], 16)
+        reorder_columns(w23_scales[:], raw_scales[:], 16, nc.gpsimd)
+        w1_q[1] = quantize_weight(w1_rounded[1], "w1_1", scales_offset)
+        late = [(piece, i) for piece in range(1, len(PIECES)) for i in PRODUCTS]
+        for n in range(EARLY):
+            gather_words(*late[n], picked, scales_offset + H // 2)
         w3_codes = held.tile([P, H], U32, name="w3_codes", align_bytes=ALIGN)
         reorder_columns(w3_codes[:].bitcast(I32), w3_raw[:], 4)
         w2_codes = held.tile([P, 2 * H], U8, name="w2_codes", align_bytes=ALIGN)
         reorder_columns(w2_codes[:].bitcast(U16), w2_raw[:].bitcast(U16), 8)
-        late = [(piece, i, call) for piece in (1, 2) for i in PRODUCTS for call in (gather_scales, gather_words)]
-        for n in range(2):
-            piece, i, call = late[n]
-            call(piece, i, picked, (2 + n) * unit_bytes // 2)
-        late = late[2:]
-        w1_q[1] = quantize_weight(w1_rounded[1], "w1_1", picked, 0)
-        round_wf(0)
-        round_wf(1)
-        wf_q[0] = quantize_weight(wf_rounded, "wf")
 
         def stationary(i, g, t):
             col = g * PASS + t * P
@@ -190,14 +188,14 @@ def tile_list_opcode_trigram_families_kernel(
 
         def first_product(i, start, g):
             piece = max(k for k in range(len(PIECES)) if PIECES[k][0] <= start)
-            words, planes, column = picked_words[piece], picked_scales[piece], start - PIECES[piece][0]
+            words, column = picked_words[piece], start - PIECES[piece][0]
             bank = psum.tile([P, PACK, UNIT], F32, name=f"first{i}")
             for t in range(PACK):
                 codes, scales = stationary(i, g, t)
                 nc.tensor.matmul_mx(
                     out=bank[:, t, :], lhsT=codes, lhsT_scale=scales,
                     rhs=words[i][:, column : column + UNIT].bitcast(FP8X4),
-                    rhs_scale=planes[i][:, column : column + UNIT],
+                    rhs_scale=picked_scales[i][:, start : start + UNIT],
                     start=True, stop=True,
                 )
             return bank
@@ -207,33 +205,46 @@ def tile_list_opcode_trigram_families_kernel(
         for width in STRETCHES + (2 * UNIT,):
             order.extend((first + offset, g) for g in range(GROUPS) for offset in range(0, width, UNIT))
             first = first + width
-        copied, first_maxima, later = {}, {}, {}
-        c_place = {k: w1_offset[1] + k * unit_bytes for k in range(3)}
-        silu_place = {}
-        bc_place = {k: wf_offset[0] + (k - 1) * unit_bytes for k in (3, 4)}
-        abc_place = [lane_offset[k % 2] + k // 2 * 3 * unit_bytes // 4 for k in range(len(order))]
+        copied, first_maxima, later, sooner, window = {}, {}, {}, {}, {}
+        ends = [GROUPS * sum(STRETCHES[: n + 1]) // UNIT - 1 for n in range(len(STRETCHES))] + [len(order) - 3]
+        region_bytes = [(7 if k in ends else 5) * unit_bytes // 2 for k in range(len(order))]
+        region = [region_offset + sum(region_bytes[:k]) for k in range(len(order))]
+        taken = [0] * len(order)
+
+        def behind_gain(k, size):
+            taken[k] = taken[k] + size
+            assert taken[k] <= region_bytes[k]
+            return region[k] + taken[k] - size
+
+        c_place = {k: w1_offset[1] + k * unit_bytes for k in range(4)}
+        abc_place = {k: w1_offset[0] + k * unit_bytes for k in range(3)}
+        c_place.update({k: abc_place[k - 4] for k in range(4, C_LEAD)})
+        for k in range(3, len(order)):
+            abc_place[k] = behind_gain(k - 3, unit_bytes)
+        for k in range(C_LEAD, len(order)):
+            c_place[k] = behind_gain(k - C_LEAD, unit_bytes)
+        gather_place = {}
+        for n in range(EARLY, len(late)):
+            k = GATHER_AT[n - EARLY]
+            gather_place[k] = [(n, behind_gain(k - 3, unit_bytes // 2) if k >= 3 else c_place[k + 1])]
 
         def copy_out(k):
             bank = first_product(PRODUCTS[0], *order[k])
-            if k in c_place:
-                c = picked.tile([P, PACK * UNIT], F32, name=f"c_held{k}", offset=c_place[k])
-            else:
-                c = work.tile([P, PACK * UNIT], F32, name="c")
+            c = picked.tile([P, PACK * UNIT], F32, name=f"c_held{k}", offset=c_place[k])
             nc.scalar.copy(out=by_pairs(c), in_=bank_by_pairs(bank))
             copied[k] = c
 
         def first_max(k):
             bank = first_product(PRODUCTS[1], *order[k])
-            if k in bc_place:
-                bc = picked.tile([P, PACK * UNIT], F32, name=f"bc_held{k}", offset=bc_place[k])
-            else:
-                bc = work.tile([P, PACK * UNIT], F32, name="bc")
+            bc = work.tile([P, PACK * UNIT], F32, name="bc")
             nc.vector.tensor_tensor(out=by_pairs(bc), in0=bank_by_pairs(bank), in1=by_pairs(copied[k]), op=ALU.max)
             first_maxima[k] = bc
 
-        for k in range(AHEAD):
+        for k in range(COPY_AHEAD + 1):
             copy_out(k)
-        first_max(0)
+        round_wf(0, slice(0, P))
+        for k in range(AHEAD):
+            first_max(k)
 
         silus = {}
 
@@ -244,25 +255,22 @@ def tile_list_opcode_trigram_families_kernel(
                 cols = slice(part * size, (part + 1) * size)
                 engine.tensor_tensor(
                     out=h_rounded.rearrange("p (j t) -> p j t", t=PACK)[:, cols],
-                    in0=silus[k][:].rearrange("p (j t) -> p j t", t=PACK)[:, cols],
+                    in0=silus[k].rearrange("p (j t) -> p j t", t=PACK)[:, cols],
                     in1=gains[:, order[k][1], :].unsqueeze(1).to_broadcast([P, size, PACK]),
                     op=ALU.mult,
                 )
 
         def unit(start, g, h_rounded, gain_engine):
             k = order.index((start, g))
-            if k + AHEAD < len(order):
-                copy_out(k + AHEAD)
+            for step in sooner.get(k, []):
+                step()
+            if k > 0 and k + COPY_AHEAD < len(order):
+                copy_out(k + COPY_AHEAD)
             bank = first_product(PRODUCTS[2], start, g)
-            if k + 1 < len(order):
-                first_max(k + 1)
             abc = picked.tile([P, PACK * UNIT], F32, name=f"abc{k}", offset=abc_place[k])
             parts = 2 if k == len(order) - 1 else 1
             size = UNIT // parts
-            if k in silu_place:
-                silu = picked.tile([P, PACK * UNIT], F32, name=f"silu_held{k}", offset=silu_place[k])
-            else:
-                silu = work.tile([P, PACK * UNIT], F32, name="silu")
+            silu = picked.tile([P, region_bytes[k] // WORD], F32, name=f"silu{k}", offset=region[k])[:, : PACK * UNIT]
             for part in range(parts):
                 pairs = slice(part * size // 2, (part + 1) * size // 2)
                 nc.vector.tensor_tensor(
@@ -270,14 +278,19 @@ def tile_list_opcode_trigram_families_kernel(
                     in1=by_pairs(first_maxima[k])[:, pairs], op=ALU.max,
                 )
                 nc.scalar.activation(
-                    out=silu[:].rearrange("p (c i t) -> p c i t", t=PACK, i=2)[:, pairs],
+                    out=silu.rearrange("p (c i t) -> p c i t", t=PACK, i=2)[:, pairs],
                     in_=abc[:].rearrange("p (c t i) -> p c i t", t=PACK, i=2)[:, pairs],
                     func=ACT.Silu,
                 )
-            if k < len(late):
-                piece, i, call = late[k]
-                call(piece, i, picked, c_place[k + 1] if k < 2 else abc_place[k - 2])
+            if k == 0:
+                wf_q[0] = quantize_weight(wf_rounded[0], "wf_0", c_place[1] + unit_bytes // 2)
+            for n, place in gather_place.get(k, []):
+                gather_words(*late[n], picked, place)
+            if k + AHEAD < len(order):
+                first_max(k + AHEAD)
             silus[k] = silu
+            if k in (1, 2):
+                round_wf(1, slice((k - 1) * P // 2, k * P // 2))
             if gain_engine is not None:
                 apply_gain(gain_engine, k, h_rounded)
             for step in later.get(k, []):
@@ -294,8 +307,8 @@ def tile_list_opcode_trigram_families_kernel(
 
         def second_pass(out, g, s, h_codes, h_scales, start, stop):
             nc.tensor.matmul_mx(
-                out=out, lhsT=wf_q[0][0][:, g * N + s * P : g * N + (s + 1) * P].bitcast(FP8X4),
-                lhsT_scale=wf_q[0][1][:, g * N + s * P : g * N + (s + 1) * P],
+                out=out, lhsT=wf_q[g][0][:, s * P : (s + 1) * P].bitcast(FP8X4),
+                lhsT_scale=wf_q[g][1][:, s * P : (s + 1) * P],
                 rhs=h_codes.bitcast(FP8X4), rhs_scale=h_scales, start=start, stop=stop,
             )
 
@@ -317,35 +330,45 @@ def tile_list_opcode_trigram_families_kernel(
                 in_=y[:, :, cols].rearrange("p s (c i) -> p c s i", i=4),
             )
 
-        def store_codes(y_rounded, start, width):
+        def store_codes(y_rounded, start, width, gain_index=None):
             cols = slice(start, start + width)
-            y_codes = work.tile([P, width], U32, name="y_codes", align_bytes=ALIGN)
+            if gain_index is None:
+                y_codes = work.tile([P, width], U32, name="y_codes", align_bytes=ALIGN)
+            else:
+                place = behind_gain(gain_index, width * WORD)
+                y_codes = picked.tile([P, width], U32, name=f"y_codes{start}", align_bytes=ALIGN, offset=place)
             nc.vector.quantize_mx(out=y_codes[:].bitcast(FP8X4), scales=y_scales[:, cols], in_=y_rounded[:])
             nc.sync.dma_start(out=y_words[:, cols], in_=y_codes[:].bitcast(I32))
 
         h_q = {}
 
         def batch(units):
-            if units[0] == order[0]:
-                h_rounded = picked.tile([P, len(units) * UNIT * PACK], BF16, name="h_first", align_bytes=ALIGN, offset=wf_offset[0])
-            else:
-                h_rounded = work.tile([P, len(units) * UNIT * PACK], BF16, name="h_rounded", align_bytes=ALIGN, bufs=2)
+            h_rounded = work.tile([P, len(units) * UNIT * PACK], BF16, name="h_rounded", align_bytes=ALIGN, bufs=1)
             for n, (first, g) in enumerate(units):
                 unit(first, g, h_rounded[:, n * UNIT * PACK : (n + 1) * UNIT * PACK], nc.gpsimd)
             last = order.index(units[-1])
 
             def quantize():
-                codes, scales = quantize_h(h_rounded, len(units) * UNIT, abc_place[last + 1] + unit_bytes // 2)
+                if last == ends[0]:
+                    wf_q[1] = quantize_weight(wf_rounded[1], "wf_1", behind_gain(last, PASS))
+                for step in window.get(last, []):
+                    step(last)
+                codes, scales = quantize_h(h_rounded, len(units) * UNIT)
                 for n, key in enumerate(units):
                     h_q[key] = (codes, scales, n * UNIT)
 
             return last, quantize
 
-        def stretch(start, width, copy):
+        def stretch(start, width, on_vector):
             last = order.index((start + width - UNIT, GROUPS - 1))
             per_bank = PASS // width
-            y = work.tile([P, PACK, width], F32, name="y")
-            y_rounded = work.tile([P, width * PACK], BF16, name="y_rounded", align_bytes=ALIGN)
+            y = work.tile([P, PACK, width], F32, name="y", bufs=3)
+            if on_vector:
+                place = behind_gain(ends[-1], width * PACK * 2)
+                y_rounded = picked.tile([P, width * PACK], BF16, name="y_late", align_bytes=ALIGN, offset=place)
+            else:
+                y_rounded = work.tile([P, width * PACK], BF16, name="y_rounded", align_bytes=ALIGN)
+            copy = nc.vector.tensor_copy if on_vector else nc.scalar.copy
             banks = []
             for b in range(PACK // per_bank):
                 banks.append(psum.tile([P, per_bank, width], F32, name="logits"))
@@ -358,19 +381,28 @@ def tile_list_opcode_trigram_families_kernel(
                             g == 0, g == GROUPS - 1,
                         )
 
-            def biases():
-                for s in range(PACK):
-                    add_bias(y, s, banks[s // per_bank][:, s % per_bank, :])
-                nc.sync.dma_start(out=y_rows[:, :, start : start + width], in_=y[:])
+            def biases(slots):
+                def step():
+                    for s in slots:
+                        add_bias(y, s, banks[s // per_bank][:, s % per_bank, :])
+                    if PACK - 1 in slots:
+                        nc.sync.dma_start(out=y_rows[:, :, start : start + width], in_=y[:])
+
+                return step
 
             def rounding(offset):
                 return lambda: round_y(copy, y_rounded, y, slice(offset, offset + UNIT))
 
-            steps = [biases] + [rounding(offset) for offset in range(0, width, UNIT)]
-            steps.append(lambda: store_codes(y_rounded, start, width))
+            steps = [biases(range(b * per_bank, (b + 1) * per_bank)) for b in range(len(banks))] + [rounding(offset) for offset in range(0, width, UNIT)]
+            free = [k for k in ends[:-1] if k >= last + Y_LAG]
             for n, step in enumerate(steps):
-                when = last + DELAY + min(n, len(steps) - 2)
+                when = last + DELAY + n
+                assert not free or when < free[0] + 2
                 later.setdefault(when if when < len(order) - 2 else len(order), []).append(step)
+            if free:
+                window.setdefault(free[0], []).append(lambda k: store_codes(y_rounded, start, width, k))
+            else:
+                later.setdefault(len(order), []).append(lambda: store_codes(y_rounded, start, width, ends[-1]))
 
         def second_stage(start, width, copy):
             return lambda: stretch(start, width, copy)
@@ -400,7 +432,7 @@ def tile_list_opcode_trigram_families_kernel(
                 step()
             for n in range(2):
                 first = start + n * UNIT
-                y = work.tile([P, PACK, UNIT], F32, name="y")
+                y = work.tile([P, PACK, UNIT], F32, name="y", bufs=3)
                 for s in range(PACK):
                     add_bias(y, s, banks[n][s // 2][:, s % 2, :], n == 0 or s < 2)
                 queue = nc.sync if n == 0 else nc.scalar
@@ -412,8 +444,8 @@ def tile_list_opcode_trigram_families_kernel(
         start = 0
         for width in STRETCHES:
             last, quantize = batch([(first, g) for first, g in order if start <= first < start + width])
-            copy = nc.scalar.copy if start < S - 3 * UNIT else nc.vector.tensor_copy
-            later.setdefault(last + 2, []).extend([quantize, second_stage(start, width, copy)])
+            copy = start + width == S - 2 * UNIT and LAST_ON_VECTOR
+            sooner.setdefault(last + 2, []).extend([quantize, second_stage(start, width, copy)])
             start = start + width
         last_stretch(S - 2 * UNIT)
         for q in range(QUADS):

@@ -30,13 +30,16 @@ UNIT = 128
 DELAY = 3
 PIECES = ((0, 256), (256, 256), (512, 256), (768, 256))
 AHEAD = 2
-COPY_AHEAD = 2
+COPY_AHEAD = 4
 EARLY = 1
-GATHER_AT = (0, 1, 4, 5, 6, 8, 9, 10)
-C_LEAD = 5
-Y_LAG = 8
-LAST_ON_VECTOR = False
-STRETCHES = (256, 256, 128, 128)
+C_LEAD = 7
+Y_LAG = 4
+ON_SCALAR = 0
+LAST_GAIN = 12
+FREE_FROM = 14
+VECTOR_FROM = 768
+HOLD_BACK = 0
+STRETCHES = (256, 256, 256)
 FIRST = 256
 WORK_BUFS = 4
 PRODUCTS = (0, 2, 1)
@@ -68,17 +71,17 @@ def tile_list_opcode_trigram_families_kernel(
         wf_offset = [c_offset + PACK * (GROUPS + g) * unit_bytes for g in range(GROUPS)]
         wf_raw = [picked.tile([P, PACK, N], F32, name=f"wf_raw{g}", offset=wf_offset[g]) for g in range(GROUPS)]
         scales_offset = c_offset + 2 * GROUPS * PACK * unit_bytes
-        region_offset = scales_offset + 2 * H
-        raw_scales = picked.tile([P, H], U8, name="raw_scales", align_bytes=ALIGN, offset=scales_offset)
-        nc.vector.memset(raw_scales[:].bitcast(I32), 0)
+        region_offset = scales_offset + 4 * H
+        raw_scales = picked.tile([P, 3 * H], U8, name="raw_scales", align_bytes=ALIGN, offset=scales_offset)[:, :H]
+        nc.vector.memset(raw_scales.bitcast(I32), 0)
         bias = held.tile([P, PACK], F32, name="bias")
 
         w1_rows = w1.rearrange("(p j) r -> p j r", j=PACK)
         wf_rows = wf.rearrange("(g p t) n -> g p t n", g=GROUPS, t=PACK)
 
-        def load_scale_rows(dst, rows, quads, shift=0):
+        def load_scale_rows(dst, rows, quads, shift=0, queue=nc.sync):
             for q in quads:
-                nc.sync.dma_start(
+                queue.dma_start(
                     out=dst[32 * q + shift : 32 * q + shift + 4, :].bitcast(I32), in_=rows[4 * q : 4 * q + 4, :].bitcast(I32)
                 )
 
@@ -88,19 +91,20 @@ def tile_list_opcode_trigram_families_kernel(
         def load_wf(g):
             nc.sync.dma_start(out=wf_raw[g][:], in_=wf_rows[g])
 
+        load_scale_rows(table_scales[:], tab_scales[0], range(ON_SCALAR), 0, nc.scalar)
         warm = held.tile([P, 2], F32, name="warm")
         nc.gpsimd.memset(warm[:, 0:1], 0.0)
         nc.scalar.activation(out=warm[:, 1:2], in_=warm[:, 0:1], func=ACT.Silu)
 
         nc.sync.dma_start(lists[0][:], offs)
         nc.sync.dma_start(lists[2][:], offs3)
-        load_scale_rows(table_scales[:], tab_scales[0], range(QUADS))
+        load_scale_rows(table_scales[:], tab_scales[0], range(ON_SCALAR, QUADS))
         load_w1(0)
         nc.sync.dma_start(lists[1][:], offs2)
         load_w1(1)
-        load_scale_rows(raw_scales[:], w3_scales[0], range(QUADS), 4)
+        load_scale_rows(raw_scales, w3_scales[0], range(QUADS), 4)
         nc.sync.dma_start(out=table_words[:], in_=tab_words[0].rearrange("p t i -> p (t i)").bitcast(I32))
-        load_scale_rows(raw_scales[:], w2_scales[0], range(QUADS))
+        load_scale_rows(raw_scales, w2_scales[0], range(QUADS))
         load_wf(0)
         nc.sync.dma_start(out=w3_raw[:], in_=w3_words[0].rearrange("p e i -> p (e i)").bitcast(I32))
         nc.sync.dma_start(out=w2_raw[:], in_=w2_words[0].bitcast(I32))
@@ -126,18 +130,15 @@ def tile_list_opcode_trigram_families_kernel(
         gather_words(0, PRODUCTS[2], held)
 
         def quantize_weight(rounded, name, offset=None):
-            codes = held.tile([P, PASS], U32, name=f"{name}_codes", align_bytes=ALIGN)
+            width = rounded.shape[1] // PACK
+            codes = held.tile([P, width], U32, name=f"{name}_codes", align_bytes=ALIGN)
             pool = held if offset is None else picked
-            scales = pool.tile([P, PASS], U8, name=f"{name}_scales", align_bytes=ALIGN, offset=offset)
+            scales = pool.tile([P, width], U8, name=f"{name}_scales", align_bytes=ALIGN, offset=offset)
             nc.vector.quantize_mx(out=codes[:].bitcast(FP8X4), scales=scales[:], in_=rounded[:])
             return codes, scales
 
         w1_q, wf_q = {}, {}
         w1_rounded = [held.tile([P, PASS * PACK], BF16, name=f"w1_rounded{g}", align_bytes=ALIGN) for g in range(GROUPS)]
-        wf_rounded = [
-            work.tile([P, PACK * N], BF16, name="h_rounded", align_bytes=ALIGN, bufs=1),
-            held.tile([P, PACK * N], BF16, name="wf_rounded", align_bytes=ALIGN),
-        ]
 
         def round_w1(g, cols):
             nc.scalar.copy(
@@ -145,10 +146,18 @@ def tile_list_opcode_trigram_families_kernel(
                 in_=w1_raw[g][:].rearrange("p j (m t) -> p m j t", t=PACK)[:, cols],
             )
 
-        def round_wf(g, cols):
+        wf_rounded = {}
+        first_h = work.tile([P, PACK * N], BF16, name="h_rounded", align_bytes=ALIGN, bufs=1)
+
+        def round_wf(n, offset):
+            g, slots = n // 2, slice(n % 2 * 2, n % 2 * 2 + 2)
+            if offset is None:
+                wf_rounded[n] = first_h[:, n * 2 * PASS : (n + 1) * 2 * PASS]
+            else:
+                wf_rounded[n] = picked.tile([P, 2 * PASS], BF16, name=f"wf_rounded{n}", align_bytes=ALIGN, offset=offset)
             nc.scalar.copy(
-                out=wf_rounded[g][:].rearrange("p (s m t) -> p m t s", s=PACK, t=PACK)[:, cols],
-                in_=wf_raw[g][:].rearrange("p t (m s) -> p m t s", s=PACK)[:, cols],
+                out=wf_rounded[n][:].rearrange("p (s m t) -> p m t s", s=2, t=PACK),
+                in_=wf_raw[g][:].rearrange("p t (m s) -> p m t s", s=PACK)[:, :, :, slots],
             )
 
         round_w1(0, slice(0, P))
@@ -162,11 +171,11 @@ def tile_list_opcode_trigram_families_kernel(
             )
 
         w23_scales = held.tile([P, H], U8, name="w23_scales", align_bytes=ALIGN)
-        reorder_columns(w23_scales[:], raw_scales[:], 16, nc.gpsimd)
+        reorder_columns(w23_scales[:], raw_scales, 16, nc.gpsimd)
         w1_q[1] = quantize_weight(w1_rounded[1], "w1_1", scales_offset)
         late = [(piece, i) for piece in range(1, len(PIECES)) for i in PRODUCTS]
         for n in range(EARLY):
-            gather_words(*late[n], picked, scales_offset + H // 2)
+            gather_words(*late[n], picked, scales_offset + H // 2 + n * H)
         w3_codes = held.tile([P, H], U32, name="w3_codes", align_bytes=ALIGN)
         reorder_columns(w3_codes[:].bitcast(I32), w3_raw[:], 4)
         w2_codes = held.tile([P, 2 * H], U8, name="w2_codes", align_bytes=ALIGN)
@@ -206,8 +215,8 @@ def tile_list_opcode_trigram_families_kernel(
             order.extend((first + offset, g) for g in range(GROUPS) for offset in range(0, width, UNIT))
             first = first + width
         copied, first_maxima, later, sooner, window = {}, {}, {}, {}, {}
-        ends = [GROUPS * sum(STRETCHES[: n + 1]) // UNIT - 1 for n in range(len(STRETCHES))] + [len(order) - 3]
-        region_bytes = [(7 if k in ends else 5) * unit_bytes // 2 for k in range(len(order))]
+        ends = [GROUPS * sum(STRETCHES[: n + 1]) // UNIT - 1 for n in range(len(STRETCHES))] + [LAST_GAIN]
+        region_bytes = [(12 if k == ends[-1] else 9 if k in ends or k == FREE_FROM - 3 else 5) * unit_bytes // 2 for k in range(len(order))]
         region = [region_offset + sum(region_bytes[:k]) for k in range(len(order))]
         taken = [0] * len(order)
 
@@ -218,14 +227,15 @@ def tile_list_opcode_trigram_families_kernel(
 
         c_place = {k: w1_offset[1] + k * unit_bytes for k in range(4)}
         abc_place = {k: w1_offset[0] + k * unit_bytes for k in range(3)}
-        c_place.update({k: abc_place[k - 4] for k in range(4, C_LEAD)})
+        c_place.update({k: region[-1] + (k - 3) * unit_bytes for k in range(4, C_LEAD)})
         for k in range(3, len(order)):
-            abc_place[k] = behind_gain(k - 3, unit_bytes)
+            abc_place[k] = behind_gain(min(k, FREE_FROM) - 3, unit_bytes)
         for k in range(C_LEAD, len(order)):
             c_place[k] = behind_gain(k - C_LEAD, unit_bytes)
         gather_place = {}
         for n in range(EARLY, len(late)):
-            k = GATHER_AT[n - EARLY]
+            reader = GROUPS * PIECES[late[n][0]][0] // UNIT
+            k = reader - (COPY_AHEAD + 1, AHEAD + 2, 2)[n % 3]
             gather_place[k] = [(n, behind_gain(k - 3, unit_bytes // 2) if k >= 3 else c_place[k + 1])]
 
         def copy_out(k):
@@ -240,9 +250,10 @@ def tile_list_opcode_trigram_families_kernel(
             nc.vector.tensor_tensor(out=by_pairs(bc), in0=bank_by_pairs(bank), in1=by_pairs(copied[k]), op=ALU.max)
             first_maxima[k] = bc
 
-        for k in range(COPY_AHEAD + 1):
+        for k in range(4):
             copy_out(k)
-        round_wf(0, slice(0, P))
+        for n in range(2):
+            round_wf(n, None)
         for k in range(AHEAD):
             first_max(k)
 
@@ -264,13 +275,13 @@ def tile_list_opcode_trigram_families_kernel(
             k = order.index((start, g))
             for step in sooner.get(k, []):
                 step()
-            if k > 0 and k + COPY_AHEAD < len(order):
+            if k + COPY_AHEAD < len(order):
                 copy_out(k + COPY_AHEAD)
             bank = first_product(PRODUCTS[2], start, g)
             abc = picked.tile([P, PACK * UNIT], F32, name=f"abc{k}", offset=abc_place[k])
             parts = 2 if k == len(order) - 1 else 1
             size = UNIT // parts
-            silu = picked.tile([P, region_bytes[k] // WORD], F32, name=f"silu{k}", offset=region[k])[:, : PACK * UNIT]
+            silu = picked.tile([P, (region_bytes[k] if k <= LAST_GAIN else unit_bytes) // WORD], F32, name=f"silu{k}", offset=region[k])[:, : PACK * UNIT]
             for part in range(parts):
                 pairs = slice(part * size // 2, (part + 1) * size // 2)
                 nc.vector.tensor_tensor(
@@ -283,14 +294,15 @@ def tile_list_opcode_trigram_families_kernel(
                     func=ACT.Silu,
                 )
             if k == 0:
-                wf_q[0] = quantize_weight(wf_rounded[0], "wf_0", c_place[1] + unit_bytes // 2)
+                for n in range(2):
+                    wf_q[n] = quantize_weight(wf_rounded[n], f"wf_{n}", c_place[1] + (2 + n) * unit_bytes // 4)
             for n, place in gather_place.get(k, []):
                 gather_words(*late[n], picked, place)
             if k + AHEAD < len(order):
                 first_max(k + AHEAD)
             silus[k] = silu
             if k in (1, 2):
-                round_wf(1, slice((k - 1) * P // 2, k * P // 2))
+                round_wf(k + 1, abc_place[k])
             if gain_engine is not None:
                 apply_gain(gain_engine, k, h_rounded)
             for step in later.get(k, []):
@@ -307,8 +319,8 @@ def tile_list_opcode_trigram_families_kernel(
 
         def second_pass(out, g, s, h_codes, h_scales, start, stop):
             nc.tensor.matmul_mx(
-                out=out, lhsT=wf_q[g][0][:, s * P : (s + 1) * P].bitcast(FP8X4),
-                lhsT_scale=wf_q[g][1][:, s * P : (s + 1) * P],
+                out=out, lhsT=wf_q[2 * g + s // 2][0][:, s % 2 * P : (s % 2 + 1) * P].bitcast(FP8X4),
+                lhsT_scale=wf_q[2 * g + s // 2][1][:, s % 2 * P : (s % 2 + 1) * P],
                 rhs=h_codes.bitcast(FP8X4), rhs_scale=h_scales, start=start, stop=stop,
             )
 
@@ -350,7 +362,8 @@ def tile_list_opcode_trigram_families_kernel(
 
             def quantize():
                 if last == ends[0]:
-                    wf_q[1] = quantize_weight(wf_rounded[1], "wf_1", behind_gain(last, PASS))
+                    for n in range(2, 2 * GROUPS):
+                        wf_q[n] = quantize_weight(wf_rounded[n], f"wf_{n}", behind_gain(last, PASS // 2))
                 for step in window.get(last, []):
                     step(last)
                 codes, scales = quantize_h(h_rounded, len(units) * UNIT)
@@ -363,11 +376,17 @@ def tile_list_opcode_trigram_families_kernel(
             last = order.index((start + width - UNIT, GROUPS - 1))
             per_bank = PASS // width
             y = work.tile([P, PACK, width], F32, name="y", bufs=3)
-            if on_vector:
-                place = behind_gain(ends[-1], width * PACK * 2)
-                y_rounded = picked.tile([P, width * PACK], BF16, name="y_late", align_bytes=ALIGN, offset=place)
-            else:
-                y_rounded = work.tile([P, width * PACK], BF16, name="y_rounded", align_bytes=ALIGN)
+            tiles = {}
+
+            def rounded_tile():
+                if not tiles:
+                    if on_vector:
+                        place = behind_gain(ends[-1], width * PACK * 2)
+                        tiles[0] = picked.tile([P, width * PACK], BF16, name=f"y_late{start}", align_bytes=ALIGN, offset=place)
+                    else:
+                        tiles[0] = work.tile([P, width * PACK], BF16, name="y_rounded", align_bytes=ALIGN)
+                return tiles[0]
+
             copy = nc.vector.tensor_copy if on_vector else nc.scalar.copy
             banks = []
             for b in range(PACK // per_bank):
@@ -391,45 +410,53 @@ def tile_list_opcode_trigram_families_kernel(
                 return step
 
             def rounding(offset):
-                return lambda: round_y(copy, y_rounded, y, slice(offset, offset + UNIT))
+                return lambda: round_y(copy, rounded_tile(), y, slice(offset, offset + UNIT))
 
             steps = [biases(range(b * per_bank, (b + 1) * per_bank)) for b in range(len(banks))] + [rounding(offset) for offset in range(0, width, UNIT)]
             free = [k for k in ends[:-1] if k >= last + Y_LAG]
             for n, step in enumerate(steps):
-                when = last + DELAY + n
+                when = last + DELAY + min(n, len(banks))
                 assert not free or when < free[0] + 2
-                later.setdefault(when if when < len(order) - 2 else len(order), []).append(step)
+                late_step = when >= len(order) - HOLD_BACK or (on_vector and n >= len(banks))
+                later.setdefault(len(order) if late_step else when, []).append(step)
             if free:
-                window.setdefault(free[0], []).append(lambda k: store_codes(y_rounded, start, width, k))
+                window.setdefault(free[0], []).append(lambda k: store_codes(rounded_tile(), start, width, k))
             else:
-                later.setdefault(len(order), []).append(lambda: store_codes(y_rounded, start, width, ends[-1]))
+                later.setdefault(len(order), []).append(lambda: store_codes(rounded_tile(), start, width, ends[-1]))
 
         def second_stage(start, width, copy):
             return lambda: stretch(start, width, copy)
 
+        def finish(k, h_rounded, banks):
+            n, g = k % 2, order[k][1]
+            h_codes, h_scales = quantize_h(h_rounded, UNIT, behind_gain(LAST_GAIN, UNIT) if k <= LAST_GAIN else None)
+            for s in range(PACK):
+                second_pass(banks[n][s // 2][:, s % 2, :], g, s, h_codes[:], h_scales[:], g == 0 and s % 2 == 0, g == 1 and s % 2 == 1)
+
         def last_stretch(start):
-            last, quantize = batch([(start, 0), (start + UNIT, 0)])
-            rounded = []
-            for n in range(2):
-                rounded.append(work.tile([P, UNIT * PACK], BF16, name="h_last", align_bytes=ALIGN))
-                unit(start + n * UNIT, 1, rounded[n][:], None)
-            for n in range(2):
-                apply_gain(nc.vector, len(order) - 2 + n, rounded[n][:])
-                if n == 0:
-                    quantize()
-            banks = []
-            for n in range(2):
-                banks.append([psum.tile([P, 2, UNIT], F32, name=f"first{PRODUCTS[n]}") for b in range(2)])
-                h_codes, h_scales, column = h_q[(start + n * UNIT, 0)]
-                cols = slice(column, column + UNIT)
-                for s in range(PACK):
-                    second_pass(banks[n][s // 2][:, s % 2, :], 0, s, h_codes[:, cols], h_scales[:, cols], s % 2 == 0, False)
-            for n in range(2):
-                h_codes, h_scales = quantize_h(rounded[n], UNIT)
-                for s in range(PACK):
-                    second_pass(banks[n][s // 2][:, s % 2, :], 1, s, h_codes[:], h_scales[:], False, s % 2 == 1)
+            tail = range(len(order) - 4, len(order))
+            rounded = {}
+            shared = work.tile([P, (LAST_GAIN + 1 - tail[0]) * UNIT * PACK], BF16, name="h_rounded", align_bytes=ALIGN, bufs=1)
+            for k in tail:
+                if k <= LAST_GAIN:
+                    rounded[k] = shared[:, (k - tail[0]) * UNIT * PACK : (k + 1 - tail[0]) * UNIT * PACK]
+                    unit(*order[k], rounded[k], nc.gpsimd)
+                else:
+                    unit(*order[k], None, None)
+            banks = [[psum.tile([P, 2, UNIT], F32, name=f"first{PRODUCTS[n]}") for b in range(2)] for n in range(2)]
+            for step in later.get("after", []):
+                step()
+            for k in tail:
+                if k > LAST_GAIN:
+                    place = behind_gain(LAST_GAIN, UNIT * PACK * 2)
+                    rounded[k] = picked.tile([P, UNIT * PACK], BF16, name=f"h_last{k}", align_bytes=ALIGN, offset=place)
+                    apply_gain(nc.vector, k, rounded[k][:])
+                if k > tail[0]:
+                    finish(k - 1, rounded[k - 1], banks)
+            finish(tail[-1], rounded[tail[-1]], banks)
             for step in later.get(len(order), []):
                 step()
+            y_rounded = work.tile([P, 2 * UNIT * PACK], BF16, name="y_rounded", align_bytes=ALIGN)
             for n in range(2):
                 first = start + n * UNIT
                 y = work.tile([P, PACK, UNIT], F32, name="y", bufs=3)
@@ -437,14 +464,14 @@ def tile_list_opcode_trigram_families_kernel(
                     add_bias(y, s, banks[n][s // 2][:, s % 2, :], n == 0 or s < 2)
                 queue = nc.sync if n == 0 else nc.scalar
                 queue.dma_start(out=y_rows[:, :, first : first + UNIT], in_=y[:])
-                y_rounded = work.tile([P, UNIT * PACK], BF16, name="y_rounded", align_bytes=ALIGN)
-                round_y(nc.vector.tensor_copy, y_rounded, y, slice(0, UNIT))
-                store_codes(y_rounded, first, UNIT)
+                half = y_rounded[:, n * UNIT * PACK : (n + 1) * UNIT * PACK]
+                round_y(nc.vector.tensor_copy, half, y, slice(0, UNIT))
+            store_codes(y_rounded, start, 2 * UNIT)
 
         start = 0
         for width in STRETCHES:
             last, quantize = batch([(first, g) for first, g in order if start <= first < start + width])
-            copy = start + width == S - 2 * UNIT and LAST_ON_VECTOR
+            copy = start >= VECTOR_FROM
             sooner.setdefault(last + 2, []).extend([quantize, second_stage(start, width, copy)])
             start = start + width
         last_stretch(S - 2 * UNIT)

@@ -31,7 +31,7 @@ DELAY = 3
 PIECES = ((0, 256), (256, 256), (512, 256), (768, 256))
 AHEAD = 2
 COPY_AHEAD = 4
-EARLY = 1
+EARLY = 2
 C_LEAD = 7
 Y_LAG = 4
 ON_SCALAR = 0
@@ -101,6 +101,7 @@ def tile_list_opcode_trigram_families_kernel(
         load_scale_rows(table_scales[:], tab_scales[0], range(ON_SCALAR, QUADS))
         load_w1(0)
         nc.sync.dma_start(lists[1][:], offs2)
+        nc.sync.dma_start(out=gains[:], in_=gain.rearrange("(g p t) -> p g t", g=GROUPS, t=PACK))
         load_w1(1)
         load_scale_rows(raw_scales, w3_scales[0], range(QUADS), 4)
         nc.sync.dma_start(out=table_words[:], in_=tab_words[0].rearrange("p t i -> p (t i)").bitcast(I32))
@@ -108,7 +109,6 @@ def tile_list_opcode_trigram_families_kernel(
         load_wf(0)
         nc.sync.dma_start(out=w3_raw[:], in_=w3_words[0].rearrange("p e i -> p (e i)").bitcast(I32))
         nc.sync.dma_start(out=w2_raw[:], in_=w2_words[0].bitcast(I32))
-        nc.sync.dma_start(out=gains[:], in_=gain.rearrange("(g p t) -> p g t", g=GROUPS, t=PACK))
         nc.sync.dma_start(out=bias[:], in_=bf.rearrange("(p s) -> p s", s=PACK))
         load_wf(1)
 
@@ -162,6 +162,8 @@ def tile_list_opcode_trigram_families_kernel(
 
         round_w1(0, slice(0, P))
         round_w1(1, slice(0, P))
+        wide_gains = held.tile([P, GROUPS, UNIT, PACK], F32, name="wide_gains")
+        nc.scalar.copy(out=wide_gains[:], in_=gains[:].unsqueeze(2).to_broadcast([P, GROUPS, UNIT, PACK]))
         w1_q[0] = quantize_weight(w1_rounded[0], "w1_0")
 
         def reorder_columns(dst, src, per_line, engine=nc.vector):
@@ -174,12 +176,12 @@ def tile_list_opcode_trigram_families_kernel(
         reorder_columns(w23_scales[:], raw_scales, 16, nc.gpsimd)
         w1_q[1] = quantize_weight(w1_rounded[1], "w1_1", scales_offset)
         late = [(piece, i) for piece in range(1, len(PIECES)) for i in PRODUCTS]
-        for n in range(EARLY):
-            gather_words(*late[n], picked, scales_offset + H // 2 + n * H)
+        gather_words(*late[0], picked, scales_offset + H // 2)
         w3_codes = held.tile([P, H], U32, name="w3_codes", align_bytes=ALIGN)
         reorder_columns(w3_codes[:].bitcast(I32), w3_raw[:], 4)
         w2_codes = held.tile([P, 2 * H], U8, name="w2_codes", align_bytes=ALIGN)
         reorder_columns(w2_codes[:].bitcast(U16), w2_raw[:].bitcast(U16), 8)
+        gather_words(*late[1], picked, 0)
 
         def stationary(i, g, t):
             col = g * PASS + t * P
@@ -261,22 +263,18 @@ def tile_list_opcode_trigram_families_kernel(
 
         def apply_gain(engine, k, h_rounded):
             parts = 2 if k == len(order) - 1 else 1
-            size = UNIT // parts
+            size = UNIT * PACK // parts
             for part in range(parts):
                 cols = slice(part * size, (part + 1) * size)
                 engine.tensor_tensor(
-                    out=h_rounded.rearrange("p (j t) -> p j t", t=PACK)[:, cols],
-                    in0=silus[k].rearrange("p (j t) -> p j t", t=PACK)[:, cols],
-                    in1=gains[:, order[k][1], :].unsqueeze(1).to_broadcast([P, size, PACK]),
-                    op=ALU.mult,
+                    out=h_rounded[:, cols], in0=silus[k][:, cols],
+                    in1=wide_gains[:, order[k][1]].rearrange("p j t -> p (j t)")[:, cols], op=ALU.mult,
                 )
 
         def unit(start, g, h_rounded, gain_engine):
             k = order.index((start, g))
             for step in sooner.get(k, []):
                 step()
-            if k + COPY_AHEAD < len(order):
-                copy_out(k + COPY_AHEAD)
             bank = first_product(PRODUCTS[2], start, g)
             abc = picked.tile([P, PACK * UNIT], F32, name=f"abc{k}", offset=abc_place[k])
             parts = 2 if k == len(order) - 1 else 1
@@ -293,6 +291,8 @@ def tile_list_opcode_trigram_families_kernel(
                     in_=abc[:].rearrange("p (c t i) -> p c i t", t=PACK, i=2)[:, pairs],
                     func=ACT.Silu,
                 )
+            if k + COPY_AHEAD < len(order):
+                copy_out(k + COPY_AHEAD)
             if k == 0:
                 for n in range(2):
                     wf_q[n] = quantize_weight(wf_rounded[n], f"wf_{n}", c_place[1] + (2 + n) * unit_bytes // 4)

@@ -21,28 +21,25 @@ PACK = 4
 PASS = P * PACK
 GROUPS = H // PASS
 QUADS = 4
-RUN = 4
-GAIN_SPAN = RUN * (PACK - 1) + 1
+W3_SHIFT = 4
 PER_COLUMN = 16
 WORD = 4
 ALIGN = 64
 UNIT = 128
-DELAY = 3
-PIECES = ((0, 256), (256, 256), (512, 256), (768, 256))
-AHEAD = 2
-COPY_AHEAD = 4
-EARLY = 2
-C_LEAD = 7
-Y_LAG = 4
-ON_SCALAR = 0
-LAST_GAIN = 12
-FREE_FROM = 14
-VECTOR_FROM = 768
-HOLD_BACK = 0
-STRETCHES = (256, 256, 256)
-FIRST = 256
+COLUMNS = PACK * UNIT
+UNIT_BYTES = COLUMNS * WORD
+STRETCH = 256
+PER_STRETCH = GROUPS * STRETCH // UNIT
+UNITS = GROUPS * S // UNIT
+COPIED, FIRST, SECOND = 0, 2, 1
 WORK_BUFS = 4
-PRODUCTS = (0, 2, 1)
+
+LEAD = 3
+COPY_AHEAD = LEAD + 1
+MAX_AHEAD = 2
+EARLY = 2
+Y_DELAY = 3
+LAST_GAIN = UNITS - PER_STRETCH
 
 
 def tile_list_opcode_trigram_families_kernel(
@@ -52,136 +49,131 @@ def tile_list_opcode_trigram_families_kernel(
     nc = tc.nc
     with ExitStack() as ctx:
         held = ctx.enter_context(tc.tile_pool(name="held", bufs=1))
-        picked = ctx.enter_context(tc.tile_pool(name="picked", bufs=1))
+        placed = ctx.enter_context(tc.tile_pool(name="placed", bufs=1))
         work = ctx.enter_context(tc.tile_pool(name="work", bufs=WORK_BUFS))
         psum = ctx.enter_context(tc.psum_pool(name="psum", bufs=2))
 
         table_scales = held.tile([P, T], U8, name="table_scales", align_bytes=ALIGN)
         nc.gpsimd.memset(table_scales[:].bitcast(I32), 0)
+        raw_scales = held.tile([P, H], U8, name="raw_scales", align_bytes=ALIGN)
+        nc.vector.memset(raw_scales[:].bitcast(I32), 0)
+
+        weight_bytes = PACK * PASS * WORD
+        w3_offset = 0
+        w1_offset = [H * WORD + g * weight_bytes for g in range(GROUPS)]
+        wf_offset = H * WORD + GROUPS * weight_bytes
+        silu_offset = wf_offset + weight_bytes
 
         lists = [held.tile([P, S // PER_COLUMN], U16, name=f"list{i}") for i in range(3)]
         table_words = held.tile([P, T], I32, name="table_words", align_bytes=ALIGN)
+        w1_raw = [placed.tile([P, PACK, PASS], F32, name=f"w1_raw{g}", offset=w1_offset[g]) for g in range(GROUPS)]
         w2_raw = held.tile([P, H // 2], I32, name="w2_raw")
-        unit_bytes = PACK * UNIT * WORD
-        w3_raw = picked.tile([P, H], I32, name="w3_raw", offset=0)
-        c_offset = H * WORD
+        w3_raw = placed.tile([P, H], I32, name="w3_raw", offset=w3_offset)
+        wf_raw = [
+            placed.tile([P, PACK, N], F32, name="wf_raw0", offset=wf_offset),
+            held.tile([P, PACK, N], F32, name="wf_raw1"),
+        ]
         gains = held.tile([P, GROUPS, PACK], F32, name="gains")
-        w1_offset = [c_offset + (PACK * g) * unit_bytes for g in range(GROUPS)]
-        w1_raw = [picked.tile([P, PACK, PASS], F32, name=f"w1_raw{g}", offset=w1_offset[g]) for g in range(GROUPS)]
-        wf_offset = [c_offset + PACK * (GROUPS + g) * unit_bytes for g in range(GROUPS)]
-        wf_raw = [picked.tile([P, PACK, N], F32, name=f"wf_raw{g}", offset=wf_offset[g]) for g in range(GROUPS)]
-        scales_offset = c_offset + 2 * GROUPS * PACK * unit_bytes
-        region_offset = scales_offset + 4 * H
-        raw_scales = picked.tile([P, 3 * H], U8, name="raw_scales", align_bytes=ALIGN, offset=scales_offset)[:, :H]
-        nc.vector.memset(raw_scales.bitcast(I32), 0)
         bias = held.tile([P, PACK], F32, name="bias")
 
         w1_rows = w1.rearrange("(p j) r -> p j r", j=PACK)
         wf_rows = wf.rearrange("(g p t) n -> g p t n", g=GROUPS, t=PACK)
 
-        def load_scale_rows(dst, rows, quads, shift=0, queue=nc.sync):
-            for q in quads:
-                queue.dma_start(
-                    out=dst[32 * q + shift : 32 * q + shift + 4, :].bitcast(I32), in_=rows[4 * q : 4 * q + 4, :].bitcast(I32)
+        def load_scale_rows(dst, rows, shift):
+            for q in range(QUADS):
+                nc.sync.dma_start(
+                    out=dst[32 * q + shift : 32 * q + shift + 4, :].bitcast(I32),
+                    in_=rows[4 * q : 4 * q + 4, :].bitcast(I32),
                 )
 
         def load_w1(g):
             nc.sync.dma_start(out=w1_raw[g][:], in_=w1_rows[:, :, g * PASS : (g + 1) * PASS])
 
-        def load_wf(g):
-            nc.sync.dma_start(out=wf_raw[g][:], in_=wf_rows[g])
-
-        load_scale_rows(table_scales[:], tab_scales[0], range(ON_SCALAR), 0, nc.scalar)
         warm = held.tile([P, 2], F32, name="warm")
         nc.gpsimd.memset(warm[:, 0:1], 0.0)
         nc.scalar.activation(out=warm[:, 1:2], in_=warm[:, 0:1], func=ACT.Silu)
 
-        nc.sync.dma_start(lists[0][:], offs)
-        nc.sync.dma_start(lists[2][:], offs3)
-        load_scale_rows(table_scales[:], tab_scales[0], range(ON_SCALAR, QUADS))
+        nc.sync.dma_start(lists[COPIED][:], offs)
+        nc.sync.dma_start(lists[FIRST][:], offs3)
+        load_scale_rows(table_scales[:], tab_scales[0], 0)
         load_w1(0)
-        nc.sync.dma_start(lists[1][:], offs2)
-        nc.sync.dma_start(out=gains[:], in_=gain.rearrange("(g p t) -> p g t", g=GROUPS, t=PACK))
+        nc.sync.dma_start(lists[SECOND][:], offs2)
+        load_scale_rows(raw_scales[:], w3_scales[0], W3_SHIFT)
         load_w1(1)
-        load_scale_rows(raw_scales, w3_scales[0], range(QUADS), 4)
+        load_scale_rows(raw_scales[:], w2_scales[0], 0)
         nc.sync.dma_start(out=table_words[:], in_=tab_words[0].rearrange("p t i -> p (t i)").bitcast(I32))
-        load_scale_rows(raw_scales, w2_scales[0], range(QUADS))
-        load_wf(0)
+        nc.sync.dma_start(out=gains[:], in_=gain.rearrange("(g p t) -> p g t", g=GROUPS, t=PACK))
+        nc.sync.dma_start(out=wf_raw[0][:], in_=wf_rows[0])
         nc.sync.dma_start(out=w3_raw[:], in_=w3_words[0].rearrange("p e i -> p (e i)").bitcast(I32))
         nc.sync.dma_start(out=w2_raw[:], in_=w2_words[0].bitcast(I32))
         nc.sync.dma_start(out=bias[:], in_=bf.rearrange("(p s) -> p s", s=PACK))
-        load_wf(1)
+        nc.sync.dma_start(out=wf_raw[1][:], in_=wf_rows[1])
 
         picked_scales = [held.tile([P, S], U8, name=f"picked_scales{i}", align_bytes=ALIGN) for i in range(3)]
-        for i in PRODUCTS:
+        for i in (COPIED, FIRST, SECOND):
             nc.vector.tensor_copy(picked_scales[i][:], table_scales[:].indirect(lists[i][:]))
 
-        picked_words = [{} for piece in PIECES]
+        picked_words = {}
 
-        def gather_words(piece, i, pool, offset=None):
-            first, width = PIECES[piece]
-            tile = pool.tile([P, width], U32, name=f"picked_words{first}_{i}", align_bytes=ALIGN, offset=offset)
-            entries = lists[i][:, first // PER_COLUMN : (first + width) // PER_COLUMN]
-            nc.vector.tensor_copy(tile[:], table_words[:].bitcast(U32).indirect(entries))
-            picked_words[piece][i] = tile
+        def gather_words(stretch, i, offset=None):
+            pool = held if offset is None else placed
+            words = pool.tile([P, STRETCH], U32, name=f"picked_words{stretch}_{i}", align_bytes=ALIGN, offset=offset)
+            columns = STRETCH // PER_COLUMN
+            entries = lists[i][:, stretch * columns : (stretch + 1) * columns]
+            nc.vector.tensor_copy(words[:], table_words[:].bitcast(U32).indirect(entries))
+            picked_words[(stretch, i)] = words
 
-        gather_words(0, PRODUCTS[0], held)
-        gather_words(0, PRODUCTS[1], held)
-        gather_words(0, PRODUCTS[2], held)
+        for i in (COPIED, FIRST, SECOND):
+            gather_words(0, i)
 
         def quantize_weight(rounded, name, offset=None):
             width = rounded.shape[1] // PACK
             codes = held.tile([P, width], U32, name=f"{name}_codes", align_bytes=ALIGN)
-            pool = held if offset is None else picked
+            pool = held if offset is None else placed
             scales = pool.tile([P, width], U8, name=f"{name}_scales", align_bytes=ALIGN, offset=offset)
             nc.vector.quantize_mx(out=codes[:].bitcast(FP8X4), scales=scales[:], in_=rounded[:])
             return codes, scales
 
-        w1_q, wf_q = {}, {}
+        w1_q, wf_q, wf_rounded = {}, {}, {}
         w1_rounded = [held.tile([P, PASS * PACK], BF16, name=f"w1_rounded{g}", align_bytes=ALIGN) for g in range(GROUPS)]
-
-        def round_w1(g, cols):
+        for g in range(GROUPS):
             nc.scalar.copy(
-                out=w1_rounded[g][:].rearrange("p (t m j) -> p m j t", t=PACK, j=PACK)[:, cols],
-                in_=w1_raw[g][:].rearrange("p j (m t) -> p m j t", t=PACK)[:, cols],
+                out=w1_rounded[g][:].rearrange("p (t m j) -> p m j t", t=PACK, j=PACK),
+                in_=w1_raw[g][:].rearrange("p j (m t) -> p m j t", t=PACK),
             )
 
-        wf_rounded = {}
-        first_h = work.tile([P, PACK * N], BF16, name="h_rounded", align_bytes=ALIGN, bufs=1)
+        def h_tile(units):
+            return work.tile([P, units * COLUMNS], BF16, name="h_rounded", align_bytes=ALIGN, bufs=1)
 
-        def round_wf(n, offset):
-            g, slots = n // 2, slice(n % 2 * 2, n % 2 * 2 + 2)
-            if offset is None:
-                wf_rounded[n] = first_h[:, n * 2 * PASS : (n + 1) * 2 * PASS]
-            else:
-                wf_rounded[n] = picked.tile([P, 2 * PASS], BF16, name=f"wf_rounded{n}", align_bytes=ALIGN, offset=offset)
+        def round_wf(g, half, rounded):
             nc.scalar.copy(
-                out=wf_rounded[n][:].rearrange("p (s m t) -> p m t s", s=2, t=PACK),
-                in_=wf_raw[g][:].rearrange("p t (m s) -> p m t s", s=PACK)[:, :, :, slots],
+                out=rounded.rearrange("p (s m t) -> p m t s", s=2, t=PACK),
+                in_=wf_raw[g][:].rearrange("p t (m s) -> p m t s", s=PACK)[:, :, :, 2 * half : 2 * half + 2],
             )
+            wf_rounded[(g, half)] = rounded
 
-        round_w1(0, slice(0, P))
-        round_w1(1, slice(0, P))
+        def quantize_wf(g, half, offset):
+            wf_q[(g, half)] = quantize_weight(wf_rounded[(g, half)], f"wf_{g}_{half}", offset)
+
         wide_gains = held.tile([P, GROUPS, UNIT, PACK], F32, name="wide_gains")
         nc.scalar.copy(out=wide_gains[:], in_=gains[:].unsqueeze(2).to_broadcast([P, GROUPS, UNIT, PACK]))
         w1_q[0] = quantize_weight(w1_rounded[0], "w1_0")
 
-        def reorder_columns(dst, src, per_line, engine=nc.vector):
+        def reorder_columns(engine, dst, src, per_line):
             engine.tensor_copy(
                 out=dst.rearrange("p (g t c i) -> p g c t i", g=GROUPS, t=PACK, i=per_line),
                 in_=src.rearrange("p (g c i t) -> p g c t i", g=GROUPS, t=PACK, i=per_line),
             )
 
         w23_scales = held.tile([P, H], U8, name="w23_scales", align_bytes=ALIGN)
-        reorder_columns(w23_scales[:], raw_scales, 16, nc.gpsimd)
-        w1_q[1] = quantize_weight(w1_rounded[1], "w1_1", scales_offset)
-        late = [(piece, i) for piece in range(1, len(PIECES)) for i in PRODUCTS]
-        gather_words(*late[0], picked, scales_offset + H // 2)
+        reorder_columns(nc.gpsimd, w23_scales[:], raw_scales[:], 16)
+        for i in (COPIED, FIRST, SECOND)[:EARLY]:
+            gather_words(1, i)
         w3_codes = held.tile([P, H], U32, name="w3_codes", align_bytes=ALIGN)
-        reorder_columns(w3_codes[:].bitcast(I32), w3_raw[:], 4)
+        reorder_columns(nc.vector, w3_codes[:].bitcast(I32), w3_raw[:], 4)
         w2_codes = held.tile([P, 2 * H], U8, name="w2_codes", align_bytes=ALIGN)
-        reorder_columns(w2_codes[:].bitcast(U16), w2_raw[:].bitcast(U16), 8)
-        gather_words(*late[1], picked, 0)
+        reorder_columns(nc.vector, w2_codes[:].bitcast(U16), w2_raw[:].bitcast(U16), 8)
+        w1_q[1] = quantize_weight(w1_rounded[1], "w1_1", w3_offset)
 
         def stationary(i, g, t):
             col = g * PASS + t * P
@@ -189,7 +181,52 @@ def tile_list_opcode_trigram_families_kernel(
                 return w1_q[g][0][:, t * P : (t + 1) * P].bitcast(FP8X4), w1_q[g][1][:, t * P : (t + 1) * P]
             if i == 1:
                 return w2_codes[:, 2 * col : 2 * (col + P)].bitcast(FP4X4), w23_scales[:, col : col + P]
-            return w3_codes[:, col : col + P].bitcast(FP8X4), w23_scales[4:P, col : col + P]
+            return w3_codes[:, col : col + P].bitcast(FP8X4), w23_scales[W3_SHIFT:P, col : col + P]
+
+        order = [
+            (first + offset, g)
+            for first in range(0, S, STRETCH) for g in range(GROUPS) for offset in range(0, STRETCH, UNIT)
+        ]
+
+        def first_product(i, k):
+            start, g = order[k]
+            words = picked_words[(start // STRETCH, i)][:, start % STRETCH : start % STRETCH + UNIT]
+            bank = psum.tile([P, PACK, UNIT], F32, name=f"first{i}")
+            for t in range(PACK):
+                codes, scales = stationary(i, g, t)
+                nc.tensor.matmul_mx(
+                    out=bank[:, t, :], lhsT=codes, lhsT_scale=scales,
+                    rhs=words.bitcast(FP8X4), rhs_scale=picked_scales[i][:, start : start + UNIT],
+                    start=True, stop=True,
+                )
+            return bank
+
+        def ends_stretch(k):
+            return k % PER_STRETCH == PER_STRETCH - 1
+
+        room = [(5 if ends_stretch(k) or k == LAST_GAIN else 5 / 2) * UNIT_BYTES for k in range(LAST_GAIN + 1)]
+        room = [int(size) for size in room]
+        taken = [0] * len(room)
+
+        def behind_gain(k, size):
+            taken[k] = taken[k] + size
+            assert taken[k] <= room[k]
+            return silu_offset + sum(room[:k]) + taken[k] - size
+
+        free_copies = LEAD + COPY_AHEAD
+        copy_place = [w1_offset[1] + k * UNIT_BYTES for k in range(COPY_AHEAD)]
+        copy_place.extend(wf_offset + k * UNIT_BYTES for k in range(free_copies - COPY_AHEAD))
+        max_place = [w1_offset[0] + k * UNIT_BYTES for k in range(LEAD)]
+        max_place.extend(behind_gain(min(k, UNITS - 2) - LEAD, UNIT_BYTES) for k in range(LEAD, UNITS))
+        copy_place.extend(behind_gain(k - free_copies, UNIT_BYTES) for k in range(free_copies, UNITS))
+
+        gathers = {}
+        for stretch in range(1, S // STRETCH):
+            for i, ahead in ((COPIED, COPY_AHEAD + 1), (FIRST, COPY_AHEAD), (SECOND, 2)):
+                if (stretch, i) not in picked_words:
+                    k = stretch * PER_STRETCH - ahead
+                    place = behind_gain(k - LEAD, STRETCH * WORD) if k >= LEAD else copy_place[k + 1]
+                    gathers[k] = (stretch, i, place)
 
         def bank_by_pairs(bank):
             return bank[:].rearrange("p t (c i) -> p c t i", i=2)
@@ -197,284 +234,197 @@ def tile_list_opcode_trigram_families_kernel(
         def by_pairs(tile):
             return tile[:].rearrange("p (c t i) -> p c t i", t=PACK, i=2)
 
-        def first_product(i, start, g):
-            piece = max(k for k in range(len(PIECES)) if PIECES[k][0] <= start)
-            words, column = picked_words[piece], start - PIECES[piece][0]
-            bank = psum.tile([P, PACK, UNIT], F32, name=f"first{i}")
-            for t in range(PACK):
-                codes, scales = stationary(i, g, t)
-                nc.tensor.matmul_mx(
-                    out=bank[:, t, :], lhsT=codes, lhsT_scale=scales,
-                    rhs=words[i][:, column : column + UNIT].bitcast(FP8X4),
-                    rhs_scale=picked_scales[i][:, start : start + UNIT],
-                    start=True, stop=True,
-                )
-            return bank
-
-        order = []
-        first = 0
-        for width in STRETCHES + (2 * UNIT,):
-            order.extend((first + offset, g) for g in range(GROUPS) for offset in range(0, width, UNIT))
-            first = first + width
-        copied, first_maxima, later, sooner, window = {}, {}, {}, {}, {}
-        ends = [GROUPS * sum(STRETCHES[: n + 1]) // UNIT - 1 for n in range(len(STRETCHES))] + [LAST_GAIN]
-        region_bytes = [(12 if k == ends[-1] else 9 if k in ends or k == FREE_FROM - 3 else 5) * unit_bytes // 2 for k in range(len(order))]
-        region = [region_offset + sum(region_bytes[:k]) for k in range(len(order))]
-        taken = [0] * len(order)
-
-        def behind_gain(k, size):
-            taken[k] = taken[k] + size
-            assert taken[k] <= region_bytes[k]
-            return region[k] + taken[k] - size
-
-        c_place = {k: w1_offset[1] + k * unit_bytes for k in range(4)}
-        abc_place = {k: w1_offset[0] + k * unit_bytes for k in range(3)}
-        c_place.update({k: region[-1] + (k - 3) * unit_bytes for k in range(4, C_LEAD)})
-        for k in range(3, len(order)):
-            abc_place[k] = behind_gain(min(k, FREE_FROM) - 3, unit_bytes)
-        for k in range(C_LEAD, len(order)):
-            c_place[k] = behind_gain(k - C_LEAD, unit_bytes)
-        gather_place = {}
-        for n in range(EARLY, len(late)):
-            reader = GROUPS * PIECES[late[n][0]][0] // UNIT
-            k = reader - (COPY_AHEAD + 1, AHEAD + 2, 2)[n % 3]
-            gather_place[k] = [(n, behind_gain(k - 3, unit_bytes // 2) if k >= 3 else c_place[k + 1])]
+        copied, first_maxima, silus = {}, {}, {}
 
         def copy_out(k):
-            bank = first_product(PRODUCTS[0], *order[k])
-            c = picked.tile([P, PACK * UNIT], F32, name=f"c_held{k}", offset=c_place[k])
-            nc.scalar.copy(out=by_pairs(c), in_=bank_by_pairs(bank))
-            copied[k] = c
+            bank = first_product(COPIED, k)
+            copied[k] = placed.tile([P, COLUMNS], F32, name=f"copied{k}", offset=copy_place[k])
+            nc.scalar.copy(out=by_pairs(copied[k]), in_=bank_by_pairs(bank))
 
         def first_max(k):
-            bank = first_product(PRODUCTS[1], *order[k])
-            bc = work.tile([P, PACK * UNIT], F32, name="bc")
-            nc.vector.tensor_tensor(out=by_pairs(bc), in0=bank_by_pairs(bank), in1=by_pairs(copied[k]), op=ALU.max)
-            first_maxima[k] = bc
+            bank = first_product(FIRST, k)
+            first_maxima[k] = work.tile([P, COLUMNS], F32, name="first_max")
+            nc.vector.tensor_tensor(
+                out=by_pairs(first_maxima[k]), in0=bank_by_pairs(bank), in1=by_pairs(copied[k]), op=ALU.max
+            )
 
-        for k in range(4):
-            copy_out(k)
-        for n in range(2):
-            round_wf(n, None)
-        for k in range(AHEAD):
-            first_max(k)
-
-        silus = {}
+        def second_max_and_silu(k):
+            bank = first_product(SECOND, k)
+            m = placed.tile([P, COLUMNS], F32, name=f"second_max{k}", offset=max_place[k])
+            if k <= LAST_GAIN:
+                offset = silu_offset + sum(room[:k])
+                silus[k] = placed.tile([P, room[k] // WORD], F32, name=f"silu{k}", offset=offset)[:, :COLUMNS]
+            else:
+                silus[k] = held.tile([P, COLUMNS], F32, name=f"silu{k}")[:]
+            nc.vector.tensor_tensor(
+                out=by_pairs(m), in0=bank_by_pairs(bank), in1=by_pairs(first_maxima[k]), op=ALU.max
+            )
+            nc.scalar.activation(
+                out=silus[k].rearrange("p (c i t) -> p c i t", t=PACK, i=2),
+                in_=m[:].rearrange("p (c t i) -> p c i t", t=PACK, i=2),
+                func=ACT.Silu,
+            )
 
         def apply_gain(engine, k, h_rounded):
-            parts = 2 if k == len(order) - 1 else 1
-            size = UNIT * PACK // parts
-            for part in range(parts):
-                cols = slice(part * size, (part + 1) * size)
-                engine.tensor_tensor(
-                    out=h_rounded[:, cols], in0=silus[k][:, cols],
-                    in1=wide_gains[:, order[k][1]].rearrange("p j t -> p (j t)")[:, cols], op=ALU.mult,
-                )
+            engine.tensor_tensor(
+                out=h_rounded, in0=silus[k], in1=wide_gains[:, order[k][1]].rearrange("p j t -> p (j t)"), op=ALU.mult
+            )
 
-        def unit(start, g, h_rounded, gain_engine):
-            k = order.index((start, g))
-            for step in sooner.get(k, []):
-                step()
-            bank = first_product(PRODUCTS[2], start, g)
-            abc = picked.tile([P, PACK * UNIT], F32, name=f"abc{k}", offset=abc_place[k])
-            parts = 2 if k == len(order) - 1 else 1
-            size = UNIT // parts
-            silu = picked.tile([P, (region_bytes[k] if k <= LAST_GAIN else unit_bytes) // WORD], F32, name=f"silu{k}", offset=region[k])[:, : PACK * UNIT]
-            for part in range(parts):
-                pairs = slice(part * size // 2, (part + 1) * size // 2)
-                nc.vector.tensor_tensor(
-                    out=by_pairs(abc)[:, pairs], in0=bank_by_pairs(bank)[:, pairs],
-                    in1=by_pairs(first_maxima[k])[:, pairs], op=ALU.max,
-                )
-                nc.scalar.activation(
-                    out=silu.rearrange("p (c i t) -> p c i t", t=PACK, i=2)[:, pairs],
-                    in_=abc[:].rearrange("p (c t i) -> p c i t", t=PACK, i=2)[:, pairs],
-                    func=ACT.Silu,
-                )
-            if k + COPY_AHEAD < len(order):
-                copy_out(k + COPY_AHEAD)
-            if k == 0:
-                for n in range(2):
-                    wf_q[n] = quantize_weight(wf_rounded[n], f"wf_{n}", c_place[1] + (2 + n) * unit_bytes // 4)
-            for n, place in gather_place.get(k, []):
-                gather_words(*late[n], picked, place)
-            if k + AHEAD < len(order):
-                first_max(k + AHEAD)
-            silus[k] = silu
-            if k in (1, 2):
-                round_wf(k + 1, abc_place[k])
-            if gain_engine is not None:
-                apply_gain(gain_engine, k, h_rounded)
-            for step in later.get(k, []):
-                step()
-
-        def quantize_h(h_rounded, columns, place=None):
-            codes = work.tile([P, columns], U32, name="h_codes", align_bytes=ALIGN)
-            if place is None:
-                scales = work.tile([P, columns], U8, name="h_scales", align_bytes=ALIGN)
+        def quantize_h(h_rounded, offset=None):
+            width = h_rounded.shape[1] // PACK
+            codes = work.tile([P, width], U32, name="h_codes", align_bytes=ALIGN)
+            if offset is None:
+                scales = work.tile([P, width], U8, name="h_scales", align_bytes=ALIGN)
             else:
-                scales = picked.tile([P, columns], U8, name=f"h_scales{place}", align_bytes=ALIGN, offset=place)
-            nc.vector.quantize_mx(out=codes[:].bitcast(FP8X4), scales=scales[:], in_=h_rounded[:])
+                scales = placed.tile([P, width], U8, name="h_scales_held", align_bytes=ALIGN, offset=offset)
+            nc.vector.quantize_mx(out=codes[:].bitcast(FP8X4), scales=scales[:], in_=h_rounded)
             return codes, scales
 
         def second_pass(out, g, s, h_codes, h_scales, start, stop):
+            codes, scales = wf_q[(g, s // 2)]
+            cols = slice(s % 2 * P, (s % 2 + 1) * P)
             nc.tensor.matmul_mx(
-                out=out, lhsT=wf_q[2 * g + s // 2][0][:, s % 2 * P : (s % 2 + 1) * P].bitcast(FP8X4),
-                lhsT_scale=wf_q[2 * g + s // 2][1][:, s % 2 * P : (s % 2 + 1) * P],
+                out=out, lhsT=codes[:, cols].bitcast(FP8X4), lhsT_scale=scales[:, cols],
                 rhs=h_codes.bitcast(FP8X4), rhs_scale=h_scales, start=start, stop=stop,
             )
 
-        def add_bias(y, s, logits, on_scalar=True):
-            if on_scalar:
-                nc.scalar.activation(out=y[:, s, :], in_=logits, func=ACT.Identity, bias=bias[:, s : s + 1])
-            else:
-                nc.vector.tensor_scalar(
-                    out=y[:, s, :], in0=logits, scalar1=bias[:, s : s + 1], scalar2=None, op0=ALU.add
-                )
+        def bias_on_scalar(y, s, logits):
+            nc.scalar.activation(out=y[:, s, :], in_=logits, func=ACT.Identity, bias=bias[:, s : s + 1])
+
+        def bias_on_vector(y, s, logits):
+            nc.vector.tensor_scalar(out=y[:, s, :], in0=logits, scalar1=bias[:, s : s + 1], scalar2=None, op0=ALU.add)
 
         y_scales = held.tile([P, S], U8, name="y_scales", align_bytes=ALIGN)
         y_rows = out_0.rearrange("(p s) j -> p s j", s=PACK)
         y_words = out_1[0].rearrange("p m t -> p (m t)").bitcast(I32)
 
-        def round_y(copy, y_rounded, y, cols):
+        def y_tile(width):
+            return work.tile([P, PACK, width], F32, name="y", bufs=3)
+
+        def round_y(copy, y_rounded, y):
             copy(
-                out=y_rounded[:].rearrange("p (j s) -> p j s", s=PACK)[:, cols].rearrange("p (c i) s -> p c s i", i=4),
-                in_=y[:, :, cols].rearrange("p s (c i) -> p c s i", i=4),
+                out=y_rounded.rearrange("p (c i s) -> p c s i", s=PACK, i=4),
+                in_=y.rearrange("p s (c i) -> p c s i", i=4),
             )
 
-        def store_codes(y_rounded, start, width, gain_index=None):
-            cols = slice(start, start + width)
-            if gain_index is None:
-                y_codes = work.tile([P, width], U32, name="y_codes", align_bytes=ALIGN)
+        h_rounded, logits, y, y_rounded = {}, {}, {}, {}
+
+        def store_codes(stretch, gain_index):
+            cols = slice(stretch * STRETCH, (stretch + 1) * STRETCH)
+            place = behind_gain(gain_index, STRETCH * WORD)
+            codes = placed.tile([P, STRETCH], U32, name=f"y_codes{stretch}", align_bytes=ALIGN, offset=place)
+            nc.vector.quantize_mx(out=codes[:].bitcast(FP8X4), scales=y_scales[:, cols], in_=y_rounded[stretch][:])
+            nc.sync.dma_start(out=y_words[:, cols], in_=codes[:].bitcast(I32))
+
+        def second_product(stretch):
+            last = (stretch + 1) * PER_STRETCH - 1
+            if stretch == 0:
+                for half in range(2):
+                    quantize_wf(1, half, behind_gain(last, PASS // 2))
             else:
-                place = behind_gain(gain_index, width * WORD)
-                y_codes = picked.tile([P, width], U32, name=f"y_codes{start}", align_bytes=ALIGN, offset=place)
-            nc.vector.quantize_mx(out=y_codes[:].bitcast(FP8X4), scales=y_scales[:, cols], in_=y_rounded[:])
-            nc.sync.dma_start(out=y_words[:, cols], in_=y_codes[:].bitcast(I32))
-
-        h_q = {}
-
-        def batch(units):
-            h_rounded = work.tile([P, len(units) * UNIT * PACK], BF16, name="h_rounded", align_bytes=ALIGN, bufs=1)
-            for n, (first, g) in enumerate(units):
-                unit(first, g, h_rounded[:, n * UNIT * PACK : (n + 1) * UNIT * PACK], nc.gpsimd)
-            last = order.index(units[-1])
-
-            def quantize():
-                if last == ends[0]:
-                    for n in range(2, 2 * GROUPS):
-                        wf_q[n] = quantize_weight(wf_rounded[n], f"wf_{n}", behind_gain(last, PASS // 2))
-                for step in window.get(last, []):
-                    step(last)
-                codes, scales = quantize_h(h_rounded, len(units) * UNIT)
-                for n, key in enumerate(units):
-                    h_q[key] = (codes, scales, n * UNIT)
-
-            return last, quantize
-
-        def stretch(start, width, on_vector):
-            last = order.index((start + width - UNIT, GROUPS - 1))
-            per_bank = PASS // width
-            y = work.tile([P, PACK, width], F32, name="y", bufs=3)
-            tiles = {}
-
-            def rounded_tile():
-                if not tiles:
-                    if on_vector:
-                        place = behind_gain(ends[-1], width * PACK * 2)
-                        tiles[0] = picked.tile([P, width * PACK], BF16, name=f"y_late{start}", align_bytes=ALIGN, offset=place)
-                    else:
-                        tiles[0] = work.tile([P, width * PACK], BF16, name="y_rounded", align_bytes=ALIGN)
-                return tiles[0]
-
-            copy = nc.vector.tensor_copy if on_vector else nc.scalar.copy
-            banks = []
-            for b in range(PACK // per_bank):
-                banks.append(psum.tile([P, per_bank, width], F32, name="logits"))
-                for e in range(per_bank):
+                store_codes(stretch - 1, last)
+            codes, scales = quantize_h(h_rounded[stretch][:])
+            y[stretch] = y_tile(STRETCH)
+            logits[stretch] = []
+            for b in range(2):
+                logits[stretch].append(psum.tile([P, 2, STRETCH], F32, name="logits"))
+                for e in range(2):
                     for g in range(GROUPS):
-                        h_codes, h_scales, column = h_q[(start, g)]
-                        cols = slice(column, column + width)
+                        cols = slice(g * STRETCH, (g + 1) * STRETCH)
                         second_pass(
-                            banks[b][:, e, :], g, per_bank * b + e, h_codes[:, cols], h_scales[:, cols],
+                            logits[stretch][b][:, e, :], g, 2 * b + e, codes[:, cols], scales[:, cols],
                             g == 0, g == GROUPS - 1,
                         )
 
-            def biases(slots):
-                def step():
-                    for s in slots:
-                        add_bias(y, s, banks[s // per_bank][:, s % per_bank, :])
-                    if PACK - 1 in slots:
-                        nc.sync.dma_start(out=y_rows[:, :, start : start + width], in_=y[:])
-
-                return step
-
-            def rounding(offset):
-                return lambda: round_y(copy, rounded_tile(), y, slice(offset, offset + UNIT))
-
-            steps = [biases(range(b * per_bank, (b + 1) * per_bank)) for b in range(len(banks))] + [rounding(offset) for offset in range(0, width, UNIT)]
-            free = [k for k in ends[:-1] if k >= last + Y_LAG]
-            for n, step in enumerate(steps):
-                when = last + DELAY + min(n, len(banks))
-                assert not free or when < free[0] + 2
-                late_step = when >= len(order) - HOLD_BACK or (on_vector and n >= len(banks))
-                later.setdefault(len(order) if late_step else when, []).append(step)
-            if free:
-                window.setdefault(free[0], []).append(lambda k: store_codes(rounded_tile(), start, width, k))
+        def y_step(stretch, step):
+            if step < 2:
+                for e in range(2):
+                    bias_on_scalar(y[stretch], 2 * step + e, logits[stretch][step][:, e, :])
+                if step == 1:
+                    nc.sync.dma_start(out=y_rows[:, :, stretch * STRETCH : (stretch + 1) * STRETCH], in_=y[stretch][:])
             else:
-                later.setdefault(len(order), []).append(lambda: store_codes(rounded_tile(), start, width, ends[-1]))
+                y_rounded[stretch] = work.tile([P, STRETCH * PACK], BF16, name="y_rounded", align_bytes=ALIGN)
+                round_y(nc.scalar.copy, y_rounded[stretch][:], y[stretch][:])
 
-        def second_stage(start, width, copy):
-            return lambda: stretch(start, width, copy)
+        wf_first = h_tile(PER_STRETCH)
+        for k in range(COPY_AHEAD):
+            copy_out(k)
+        for half in range(2):
+            round_wf(0, half, wf_first[:, half * 2 * PASS : (half + 1) * 2 * PASS])
+        for k in range(MAX_AHEAD):
+            first_max(k)
 
-        def finish(k, h_rounded, banks):
-            n, g = k % 2, order[k][1]
-            h_codes, h_scales = quantize_h(h_rounded, UNIT, behind_gain(LAST_GAIN, UNIT) if k <= LAST_GAIN else None)
+        last_stretch = S // STRETCH - 1
+        for k in range(UNITS):
+            stretch, place = divmod(k, PER_STRETCH)
+            if place == 0:
+                h_rounded[stretch] = h_tile(PER_STRETCH if stretch < last_stretch else 1)
+            if place == 1 and stretch > 0:
+                second_product(stretch - 1)
+            second_max_and_silu(k)
+            if k + COPY_AHEAD < UNITS:
+                copy_out(k + COPY_AHEAD)
+            if k == 0:
+                for half in range(2):
+                    quantize_wf(0, half, copy_place[1] + (2 + half) * UNIT_BYTES // 4)
+            if k in gathers:
+                gather_words(*gathers[k])
+            if k + MAX_AHEAD < UNITS:
+                first_max(k + MAX_AHEAD)
+            if 1 <= k <= 2:
+                rounded = placed.tile([P, 2 * PASS], BF16, name=f"wf_rounded{k}", align_bytes=ALIGN, offset=max_place[k])
+                round_wf(1, k - 1, rounded[:])
+            if k <= LAST_GAIN:
+                apply_gain(nc.gpsimd, k, h_rounded[stretch][:, place * COLUMNS : (place + 1) * COLUMNS])
+            done, step = divmod(k + 1 - Y_DELAY, PER_STRETCH)
+            if done > 0 and step < 3:
+                y_step(done - 1, step)
+
+        banks = [[psum.tile([P, 2, UNIT], F32, name=f"first{i}") for b in range(2)] for i in (COPIED, FIRST)]
+
+        def last_gain(k):
+            place = behind_gain(LAST_GAIN, COLUMNS * 2)
+            rounded = placed.tile([P, COLUMNS], BF16, name=f"h_last{k}", align_bytes=ALIGN, offset=place)
+            apply_gain(nc.vector, k, rounded[:])
+            return rounded[:]
+
+        def last_product(k, rounded, offset=None):
+            g = order[k][1]
+            codes, scales = quantize_h(rounded, offset)
             for s in range(PACK):
-                second_pass(banks[n][s // 2][:, s % 2, :], g, s, h_codes[:], h_scales[:], g == 0 and s % 2 == 0, g == 1 and s % 2 == 1)
+                second_pass(
+                    banks[k % 2][s // 2][:, s % 2, :], g, s, codes[:], scales[:],
+                    g == 0 and s % 2 == 0, g == GROUPS - 1 and s % 2 == 1,
+                )
 
-        def last_stretch(start):
-            tail = range(len(order) - 4, len(order))
-            rounded = {}
-            shared = work.tile([P, (LAST_GAIN + 1 - tail[0]) * UNIT * PACK], BF16, name="h_rounded", align_bytes=ALIGN, bufs=1)
-            for k in tail:
-                if k <= LAST_GAIN:
-                    rounded[k] = shared[:, (k - tail[0]) * UNIT * PACK : (k + 1 - tail[0]) * UNIT * PACK]
-                    unit(*order[k], rounded[k], nc.gpsimd)
-                else:
-                    unit(*order[k], None, None)
-            banks = [[psum.tile([P, 2, UNIT], F32, name=f"first{PRODUCTS[n]}") for b in range(2)] for n in range(2)]
-            for step in later.get("after", []):
-                step()
-            for k in tail:
-                if k > LAST_GAIN:
-                    place = behind_gain(LAST_GAIN, UNIT * PACK * 2)
-                    rounded[k] = picked.tile([P, UNIT * PACK], BF16, name=f"h_last{k}", align_bytes=ALIGN, offset=place)
-                    apply_gain(nc.vector, k, rounded[k][:])
-                if k > tail[0]:
-                    finish(k - 1, rounded[k - 1], banks)
-            finish(tail[-1], rounded[tail[-1]], banks)
-            for step in later.get(len(order), []):
-                step()
-            y_rounded = work.tile([P, 2 * UNIT * PACK], BF16, name="y_rounded", align_bytes=ALIGN)
-            for n in range(2):
-                first = start + n * UNIT
-                y = work.tile([P, PACK, UNIT], F32, name="y", bufs=3)
-                for s in range(PACK):
-                    add_bias(y, s, banks[n][s // 2][:, s % 2, :], n == 0 or s < 2)
-                queue = nc.sync if n == 0 else nc.scalar
-                queue.dma_start(out=y_rows[:, :, first : first + UNIT], in_=y[:])
-                half = y_rounded[:, n * UNIT * PACK : (n + 1) * UNIT * PACK]
-                round_y(nc.vector.tensor_copy, half, y, slice(0, UNIT))
-            store_codes(y_rounded, start, 2 * UNIT)
+        first_0, second_0, first_1, second_1 = range(LAST_GAIN, UNITS)
+        last_product(first_0, h_rounded[last_stretch][:], behind_gain(LAST_GAIN, UNIT))
+        h_first_1 = last_gain(first_1)
+        h_second_0 = last_gain(second_0)
+        last_product(first_1, h_first_1)
+        h_second_1 = last_gain(second_1)
+        last_product(second_0, h_second_0)
+        last_product(second_1, h_second_1)
+        y_step(last_stretch - 1, 2)
+        store_codes(last_stretch - 1, LAST_GAIN)
 
-        start = 0
-        for width in STRETCHES:
-            last, quantize = batch([(first, g) for first, g in order if start <= first < start + width])
-            copy = start >= VECTOR_FROM
-            sooner.setdefault(last + 2, []).extend([quantize, second_stage(start, width, copy)])
-            start = start + width
-        last_stretch(S - 2 * UNIT)
+        y_last_rounded = work.tile([P, STRETCH * PACK], BF16, name="y_rounded", align_bytes=ALIGN)
+        y_last_codes = work.tile([P, STRETCH], U32, name="y_codes", align_bytes=ALIGN)
+        for half in range(2):
+            first = last_stretch * STRETCH + half * UNIT
+            y_last = y_tile(UNIT)
+            for s in range(PACK):
+                add_bias = bias_on_scalar if half == 0 or s < 2 else bias_on_vector
+                add_bias(y_last, s, banks[half][s // 2][:, s % 2, :])
+            queue = nc.sync if half == 0 else nc.scalar
+            queue.dma_start(out=y_rows[:, :, first : first + UNIT], in_=y_last[:])
+            rounded = y_last_rounded[:, half * COLUMNS : (half + 1) * COLUMNS]
+            round_y(nc.vector.tensor_copy, rounded, y_last[:])
+            nc.vector.quantize_mx(
+                out=y_last_codes[:, half * UNIT : (half + 1) * UNIT].bitcast(FP8X4),
+                scales=y_scales[:, first : first + UNIT], in_=rounded,
+            )
+        nc.sync.dma_start(out=y_words[:, last_stretch * STRETCH :], in_=y_last_codes[:].bitcast(I32))
         for q in range(QUADS):
             queue = nc.scalar if q % 2 == 0 else nc.sync
             queue.dma_start(

@@ -166,7 +166,7 @@ def tile_list_opcode_trigram_families_kernel(
             )
 
         w23_scales = held.tile([P, H], U8, name="w23_scales", align_bytes=ALIGN)
-        reorder_columns(nc.gpsimd, w23_scales[:], raw_scales[:], 16)
+        reorder_columns(nc.vector, w23_scales[:], raw_scales[:], 16)
         for i in (COPIED, FIRST, SECOND)[:EARLY]:
             gather_words(1, i)
         w3_codes = held.tile([P, H], U32, name="w3_codes", align_bytes=ALIGN)

@@ -37,6 +37,7 @@ WORK_BUFS = 4
 LEAD = 3
 COPY_AHEAD = LEAD + 1
 MAX_AHEAD = 2
+WARM_PASSES = 5
 EARLY = 2
 Y_DELAY = 3
 LAST_GAIN = UNITS - PER_STRETCH
@@ -62,12 +63,15 @@ def tile_list_opcode_trigram_families_kernel(
         w3_offset = 0
         w1_offset = [H * WORD + g * weight_bytes for g in range(GROUPS)]
         wf_offset = H * WORD + GROUPS * weight_bytes
-        silu_offset = wf_offset + weight_bytes
+        rounded_offset = wf_offset + weight_bytes
+        second_offset = rounded_offset + PACK * PASS * 2
+        w2_offset = second_offset + PACK * PASS * 2
+        silu_offset = w2_offset + 2 * H
 
         lists = [held.tile([P, S // PER_COLUMN], U16, name=f"list{i}") for i in range(3)]
         table_words = held.tile([P, T], I32, name="table_words", align_bytes=ALIGN)
         w1_raw = [placed.tile([P, PACK, PASS], F32, name=f"w1_raw{g}", offset=w1_offset[g]) for g in range(GROUPS)]
-        w2_raw = held.tile([P, H // 2], I32, name="w2_raw")
+        w2_raw = placed.tile([P, H // 2], I32, name="w2_raw", offset=w2_offset)
         w3_raw = placed.tile([P, H], I32, name="w3_raw", offset=w3_offset)
         wf_raw = [
             placed.tile([P, PACK, N], F32, name="wf_raw0", offset=wf_offset),
@@ -103,15 +107,21 @@ def tile_list_opcode_trigram_families_kernel(
         load_scale_rows(raw_scales[:], w2_scales[0], 0)
         nc.sync.dma_start(out=table_words[:], in_=tab_words[0].rearrange("p t i -> p (t i)").bitcast(I32))
         nc.sync.dma_start(out=gains[:], in_=gain.rearrange("(g p t) -> p g t", g=GROUPS, t=PACK))
-        nc.sync.dma_start(out=wf_raw[0][:], in_=wf_rows[0])
         nc.sync.dma_start(out=w3_raw[:], in_=w3_words[0].rearrange("p e i -> p (e i)").bitcast(I32))
         nc.sync.dma_start(out=w2_raw[:], in_=w2_words[0].bitcast(I32))
+        nc.sync.dma_start(out=wf_raw[0][:], in_=wf_rows[0])
         nc.sync.dma_start(out=bias[:], in_=bf.rearrange("(p s) -> p s", s=PACK))
         nc.sync.dma_start(out=wf_raw[1][:], in_=wf_rows[1])
 
-        picked_scales = [held.tile([P, S], U8, name=f"picked_scales{i}", align_bytes=ALIGN) for i in range(3)]
-        for i in (COPIED, FIRST, SECOND):
+        picked_scales = {}
+
+        def gather_scales(i, offset=None):
+            pool = held if offset is None else placed
+            picked_scales[i] = pool.tile([P, S], U8, name=f"picked_scales{i}", align_bytes=ALIGN, offset=offset)
             nc.vector.tensor_copy(picked_scales[i][:], table_scales[:].indirect(lists[i][:]))
+
+        for i in (COPIED, FIRST):
+            gather_scales(i)
 
         picked_words = {}
 
@@ -123,9 +133,6 @@ def tile_list_opcode_trigram_families_kernel(
             nc.vector.tensor_copy(words[:], table_words[:].bitcast(U32).indirect(entries))
             picked_words[(stretch, i)] = words
 
-        for i in (COPIED, FIRST, SECOND):
-            gather_words(0, i)
-
         def quantize_weight(rounded, name, offset=None):
             width = rounded.shape[1] // PACK
             codes = held.tile([P, width], U32, name=f"{name}_codes", align_bytes=ALIGN)
@@ -135,15 +142,20 @@ def tile_list_opcode_trigram_families_kernel(
             return codes, scales
 
         w1_q, wf_q, wf_rounded = {}, {}, {}
-        w1_rounded = [held.tile([P, PASS * PACK], BF16, name=f"w1_rounded{g}", align_bytes=ALIGN) for g in range(GROUPS)]
-        for g in range(GROUPS):
+
+        def round_w1(g, rounded):
             nc.scalar.copy(
-                out=w1_rounded[g][:].rearrange("p (t m j) -> p m j t", t=PACK, j=PACK),
+                out=rounded[:].rearrange("p (t m j) -> p m j t", t=PACK, j=PACK),
                 in_=w1_raw[g][:].rearrange("p j (m t) -> p m j t", t=PACK),
             )
 
+        w1_first = placed.tile([P, PASS * PACK], BF16, name="w1_first", align_bytes=ALIGN, offset=rounded_offset)
+        round_w1(0, w1_first)
+        w1_second = placed.tile([P, PASS * PACK], BF16, name="w1_second", align_bytes=ALIGN, offset=second_offset)
+        round_w1(1, w1_second)
+
         def h_tile(units):
-            return work.tile([P, units * COLUMNS], BF16, name="h_rounded", align_bytes=ALIGN, bufs=1)
+            return placed.tile([P, units * COLUMNS], BF16, name="h_rounded", align_bytes=ALIGN, offset=wf_offset)
 
         def round_wf(g, half, rounded):
             nc.scalar.copy(
@@ -157,7 +169,17 @@ def tile_list_opcode_trigram_families_kernel(
 
         wide_gains = held.tile([P, GROUPS, UNIT, PACK], F32, name="wide_gains")
         nc.scalar.copy(out=wide_gains[:], in_=gains[:].unsqueeze(2).to_broadcast([P, GROUPS, UNIT, PACK]))
-        w1_q[0] = quantize_weight(w1_rounded[0], "w1_0")
+        w1_q[0] = quantize_weight(w1_first, "w1_0")
+        warm_bank = psum.tile([P, PASS], F32, name="logits")
+        for repeat in range(WARM_PASSES):
+            nc.tensor.matmul_mx(
+                out=warm_bank[:], lhsT=w1_q[0][0][:, :P].bitcast(FP8X4), lhsT_scale=w1_q[0][1][:, :P],
+                rhs=w1_q[0][0][:].bitcast(FP8X4), rhs_scale=w1_q[0][1][:], start=True, stop=True,
+            )
+        gather_scales(SECOND, rounded_offset)
+        w1_q[1] = quantize_weight(w1_second, "w1_1")
+        for i in (COPIED, FIRST, SECOND):
+            gather_words(0, i)
 
         def reorder_columns(engine, dst, src, per_line):
             engine.tensor_copy(
@@ -165,15 +187,22 @@ def tile_list_opcode_trigram_families_kernel(
                 in_=src.rearrange("p (g c i t) -> p g c t i", g=GROUPS, t=PACK, i=per_line),
             )
 
-        w23_scales = held.tile([P, H], U8, name="w23_scales", align_bytes=ALIGN)
-        reorder_columns(nc.vector, w23_scales[:], raw_scales[:], 16)
+        w23_scales = placed.tile([P, H], U8, name="w23_scales", align_bytes=ALIGN, offset=rounded_offset + S)
+        reorder_columns(nc.gpsimd, w23_scales[:], raw_scales[:], 16)
         for i in (COPIED, FIRST, SECOND)[:EARLY]:
             gather_words(1, i)
         w3_codes = held.tile([P, H], U32, name="w3_codes", align_bytes=ALIGN)
-        reorder_columns(nc.vector, w3_codes[:].bitcast(I32), w3_raw[:], 4)
+        reorder_columns(nc.gpsimd, w3_codes[:].bitcast(I32), w3_raw[:], 4)
         w2_codes = held.tile([P, 2 * H], U8, name="w2_codes", align_bytes=ALIGN)
-        reorder_columns(nc.vector, w2_codes[:].bitcast(U16), w2_raw[:].bitcast(U16), 8)
-        w1_q[1] = quantize_weight(w1_rounded[1], "w1_1", w3_offset)
+        reorder_columns(nc.gpsimd, w2_codes[:].bitcast(U16), w2_raw[:].bitcast(U16), 8)
+
+        wf_first = held.tile([P, PASS * PACK], BF16, name="wf_first", align_bytes=ALIGN)
+        nc.gpsimd.tensor_copy(
+            out=wf_first[:].rearrange("p (s m t) -> p m s t", s=PACK, t=PACK),
+            in_=wf_raw[0][:].rearrange("p t (m s) -> p m s t", s=PACK),
+        )
+        for half in range(2):
+            wf_rounded[(0, half)] = wf_first[:, half * 2 * PASS : (half + 1) * 2 * PASS]
 
         def stationary(i, g, t):
             col = g * PASS + t * P
@@ -215,7 +244,7 @@ def tile_list_opcode_trigram_families_kernel(
 
         free_copies = LEAD + COPY_AHEAD
         copy_place = [w1_offset[1] + k * UNIT_BYTES for k in range(COPY_AHEAD)]
-        copy_place.extend(wf_offset + k * UNIT_BYTES for k in range(free_copies - COPY_AHEAD))
+        copy_place.extend(copy_place[: free_copies - COPY_AHEAD])
         max_place = [w1_offset[0] + k * UNIT_BYTES for k in range(LEAD)]
         max_place.extend(behind_gain(min(k, UNITS - 2) - LEAD, UNIT_BYTES) for k in range(LEAD, UNITS))
         copy_place.extend(behind_gain(k - free_copies, UNIT_BYTES) for k in range(free_copies, UNITS))
@@ -319,8 +348,9 @@ def tile_list_opcode_trigram_families_kernel(
         def second_product(stretch):
             last = (stretch + 1) * PER_STRETCH - 1
             if stretch == 0:
-                for half in range(2):
-                    quantize_wf(1, half, behind_gain(last, PASS // 2))
+                for g in range(GROUPS):
+                    for half in range(2):
+                        quantize_wf(g, half, behind_gain(last, PASS // 2))
             else:
                 store_codes(stretch - 1, last)
             codes, scales = quantize_h(h_rounded[stretch][:])
@@ -346,11 +376,8 @@ def tile_list_opcode_trigram_families_kernel(
                 y_rounded[stretch] = work.tile([P, STRETCH * PACK], BF16, name="y_rounded", align_bytes=ALIGN)
                 round_y(nc.scalar.copy, y_rounded[stretch][:], y[stretch][:])
 
-        wf_first = h_tile(PER_STRETCH)
         for k in range(COPY_AHEAD):
             copy_out(k)
-        for half in range(2):
-            round_wf(0, half, wf_first[:, half * 2 * PASS : (half + 1) * 2 * PASS])
         for k in range(MAX_AHEAD):
             first_max(k)
 
@@ -362,18 +389,15 @@ def tile_list_opcode_trigram_families_kernel(
             if place == 1 and stretch > 0:
                 second_product(stretch - 1)
             second_max_and_silu(k)
-            if k + COPY_AHEAD < UNITS:
+            if k + COPY_AHEAD < UNITS and k + COPY_AHEAD not in copied:
                 copy_out(k + COPY_AHEAD)
-            if k == 0:
-                for half in range(2):
-                    quantize_wf(0, half, copy_place[1] + (2 + half) * UNIT_BYTES // 4)
             if k in gathers:
                 gather_words(*gathers[k])
             if k + MAX_AHEAD < UNITS:
                 first_max(k + MAX_AHEAD)
-            if 1 <= k <= 2:
+            if k < 2:
                 rounded = placed.tile([P, 2 * PASS], BF16, name=f"wf_rounded{k}", align_bytes=ALIGN, offset=max_place[k])
-                round_wf(1, k - 1, rounded[:])
+                round_wf(1, k, rounded[:])
             if k <= LAST_GAIN:
                 apply_gain(nc.gpsimd, k, h_rounded[stretch][:, place * COLUMNS : (place + 1) * COLUMNS])
             done, step = divmod(k + 1 - Y_DELAY, PER_STRETCH)

@@ -37,7 +37,6 @@ WORK_BUFS = 4
 LEAD = 3
 COPY_AHEAD = LEAD + 1
 MAX_AHEAD = 2
-WARM_PASSES = 5
 EARLY = 2
 Y_DELAY = 3
 LAST_GAIN = UNITS - PER_STRETCH
@@ -170,12 +169,6 @@ def tile_list_opcode_trigram_families_kernel(
         wide_gains = held.tile([P, GROUPS, UNIT, PACK], F32, name="wide_gains")
         nc.scalar.copy(out=wide_gains[:], in_=gains[:].unsqueeze(2).to_broadcast([P, GROUPS, UNIT, PACK]))
         w1_q[0] = quantize_weight(w1_first, "w1_0")
-        warm_bank = psum.tile([P, PASS], F32, name="logits")
-        for repeat in range(WARM_PASSES):
-            nc.tensor.matmul_mx(
-                out=warm_bank[:], lhsT=w1_q[0][0][:, :P].bitcast(FP8X4), lhsT_scale=w1_q[0][1][:, :P],
-                rhs=w1_q[0][0][:].bitcast(FP8X4), rhs_scale=w1_q[0][1][:], start=True, stop=True,
-            )
         gather_scales(SECOND, rounded_offset)
         w1_q[1] = quantize_weight(w1_second, "w1_1")
         for i in (COPIED, FIRST, SECOND):

@@ -21,25 +21,18 @@ PACK = 4
 PASS = P * PACK
 GROUPS = H // PASS
 QUADS = 4
-W3_SHIFT = 4
 PER_COLUMN = 16
 WORD = 4
 ALIGN = 64
 UNIT = 128
 COLUMNS = PACK * UNIT
 UNIT_BYTES = COLUMNS * WORD
-STRETCH = 256
-PER_STRETCH = GROUPS * STRETCH // UNIT
+CHUNK = 256
 UNITS = GROUPS * S // UNIT
-COPIED, FIRST, SECOND = 0, 2, 1
-WORK_BUFS = 4
-
-LEAD = 3
-COPY_AHEAD = LEAD + 1
-MAX_AHEAD = 2
-EARLY = 2
-Y_DELAY = 3
-LAST_GAIN = UNITS - PER_STRETCH
+W1, W2, W3 = 0, 1, 2
+COPIED, FIRST, SECOND = W3, W1, W2
+COPY_AHEAD = 4
+PAIRS = 6
 
 
 def tile_list_opcode_trigram_families_kernel(
@@ -50,31 +43,78 @@ def tile_list_opcode_trigram_families_kernel(
     with ExitStack() as ctx:
         held = ctx.enter_context(tc.tile_pool(name="held", bufs=1))
         placed = ctx.enter_context(tc.tile_pool(name="placed", bufs=1))
-        work = ctx.enter_context(tc.tile_pool(name="work", bufs=WORK_BUFS))
         psum = ctx.enter_context(tc.psum_pool(name="psum", bufs=2))
+
+        top = [0]
+
+        def fresh(size):
+            top[0] = top[0] + size
+            return top[0] - size
+
+        rooms = {}
+
+        def open_room(name, size):
+            start = fresh(size)
+            rooms[name] = [start, start + size]
+            return start
+
+        def behind(name, size):
+            rooms[name][0] = rooms[name][0] + size
+            assert rooms[name][0] <= rooms[name][1]
+            return rooms[name][0] - size
+
+        def at(offset, shape, dtype, name):
+            return placed.tile(shape, dtype, name=name, align_bytes=ALIGN, offset=offset)
+
+        order = [(c * CHUNK + j, g) for g in range(GROUPS) for c in (0, 1) for j in (0, UNIT)]
+        order.extend((2 * CHUNK + j, g) for g in range(GROUPS) for j in (0, UNIT))
+        order.extend((3 * CHUNK + j, g) for j in (0, UNIT) for g in range(GROUPS))
+
+        HALF = 2 * PASS * 2
+        Y_BYTES = PACK * CHUNK * WORD
+        extras = {
+            1: [("wf", 0, HALF)], 2: [("wf", 1, HALF)], 4: [("wf", 2, HALF)], 6: [("wf", 3, HALF)],
+            9: [("bias", 0, Y_BYTES)], 11: [("bias", 1, Y_BYTES)],
+            12: [("round", 0, Y_BYTES // 2)],
+        }
+        c2, c3a, c3b = 2 * CHUNK, 3 * CHUNK, 3 * CHUNK + UNIT
+        gathers = {
+            4: [("w", W3, c2, CHUNK)], 5: [("s", W2, c2, CHUNK)], 6: [("w", W1, c2, CHUNK)], 7: [("w", W2, c2, CHUNK)],
+            8: [("w", W3, c3a, UNIT)], 9: [("s", W1, c3a, CHUNK)], 10: [("w", W3, c3b, UNIT), ("w", W1, c3a, UNIT)],
+            11: [("s", W2, c3a, CHUNK)], 12: [("w", W2, c3a, UNIT)], 13: [("w", W1, c3b, UNIT)], 14: [("w", W2, c3b, UNIT)],
+        }
+        wf_quantisers = {2: [0, 1], 3: [2, 3]}
+        burst_units = [[3, 4, 5]] + [[2 * q + 4, 2 * q + 5] for q in range(1, PAIRS)] + [[UNITS]]
+
+        def first_max_bytes(k):
+            return UNIT_BYTES + sum(size for kind, index, size in extras.get(k, []))
+
+        def burst_bytes(q):
+            size = sum(first_max_bytes(k) * (k < UNITS) + UNIT_BYTES for k in burst_units[q])
+            size = size + sum(n * (WORD if kind == "w" else 1) for k in burst_units[q] for kind, i, first, n in gathers.get(k, []))
+            size = size + (len(wf_quantisers.get(q, [])) + 1) * PASS // 2 + (q == PAIRS) * 3 * UNIT_BYTES
+            return max(size, (2 + 4 * (q in wf_quantisers)) * UNIT_BYTES)
 
         table_scales = held.tile([P, T], U8, name="table_scales", align_bytes=ALIGN)
         nc.gpsimd.memset(table_scales[:].bitcast(I32), 0)
-        raw_scales = held.tile([P, H], U8, name="raw_scales", align_bytes=ALIGN)
+        raw_scales = held.tile([P, 2 * H], U8, name="raw_scales", align_bytes=ALIGN)
         nc.vector.memset(raw_scales[:].bitcast(I32), 0)
-
-        weight_bytes = PACK * PASS * WORD
-        w3_offset = 0
-        w1_offset = [H * WORD + g * weight_bytes for g in range(GROUPS)]
-        wf_offset = H * WORD + GROUPS * weight_bytes
-        rounded_offset = wf_offset + weight_bytes
-        second_offset = rounded_offset + PACK * PASS * 2
-        w2_offset = second_offset + PACK * PASS * 2
-        silu_offset = w2_offset + 2 * H
 
         lists = [held.tile([P, S // PER_COLUMN], U16, name=f"list{i}") for i in range(3)]
         table_words = held.tile([P, T], I32, name="table_words", align_bytes=ALIGN)
-        w1_raw = [placed.tile([P, PACK, PASS], F32, name=f"w1_raw{g}", offset=w1_offset[g]) for g in range(GROUPS)]
-        w2_raw = placed.tile([P, H // 2], I32, name="w2_raw", offset=w2_offset)
-        w3_raw = placed.tile([P, H], I32, name="w3_raw", offset=w3_offset)
+        weight_bytes = PACK * PASS * WORD
+        w1_raw = [held.tile([P, PACK * PASS], F32, name="w1_raw0")]
+        size = max(burst_bytes(0), weight_bytes)
+        w1_raw.append(at(open_room("burst0", size), [P, size // WORD], F32, "w1_raw1"))
+        w2_raw = held.tile([P, H // 2], I32, name="w2_raw")
+        w3_raw = [held.tile([P, PASS], I32, name=f"w3_raw{g}") for g in range(GROUPS)]
+        pairs = {}
+        for q in range(PAIRS):
+            size = burst_bytes(q + 1)
+            pairs[q] = at(open_room(f"burst{q + 1}", size), [P, size // WORD], F32, f"silu_pair{q}")
         wf_raw = [
-            placed.tile([P, PACK, N], F32, name="wf_raw0", offset=wf_offset),
-            held.tile([P, PACK, N], F32, name="wf_raw1"),
+            pairs[1 + g][:, 2 * COLUMNS : 2 * COLUMNS + PACK * N].rearrange("p (t n) -> p t n", t=PACK)
+            for g in range(GROUPS)
         ]
         gains = held.tile([P, GROUPS, PACK], F32, name="gains")
         bias = held.tile([P, PACK], F32, name="bias")
@@ -82,366 +122,310 @@ def tile_list_opcode_trigram_families_kernel(
         w1_rows = w1.rearrange("(p j) r -> p j r", j=PACK)
         wf_rows = wf.rearrange("(g p t) n -> g p t n", g=GROUPS, t=PACK)
 
-        def load_scale_rows(dst, rows, shift):
+        def load_scale_rows(dst, rows):
             for q in range(QUADS):
                 nc.sync.dma_start(
-                    out=dst[32 * q + shift : 32 * q + shift + 4, :].bitcast(I32),
-                    in_=rows[4 * q : 4 * q + 4, :].bitcast(I32),
+                    out=dst[32 * q : 32 * q + 4, :].bitcast(I32), in_=rows[4 * q : 4 * q + 4, :].bitcast(I32)
                 )
 
+        def w1_values(g):
+            return w1_raw[g][:, : PACK * PASS].rearrange("p (j r) -> p j r", j=PACK)
+
         def load_w1(g):
-            nc.sync.dma_start(out=w1_raw[g][:], in_=w1_rows[:, :, g * PASS : (g + 1) * PASS])
+            nc.sync.dma_start(out=w1_values(g), in_=w1_rows[:, :, g * PASS : (g + 1) * PASS])
 
         warm = held.tile([P, 2], F32, name="warm")
         nc.gpsimd.memset(warm[:, 0:1], 0.0)
         nc.scalar.activation(out=warm[:, 1:2], in_=warm[:, 0:1], func=ACT.Silu)
 
-        nc.sync.dma_start(lists[COPIED][:], offs)
-        nc.sync.dma_start(lists[FIRST][:], offs3)
-        load_scale_rows(table_scales[:], tab_scales[0], 0)
-        load_w1(0)
-        nc.sync.dma_start(lists[SECOND][:], offs2)
-        load_scale_rows(raw_scales[:], w3_scales[0], W3_SHIFT)
-        load_w1(1)
-        load_scale_rows(raw_scales[:], w2_scales[0], 0)
-        nc.sync.dma_start(out=table_words[:], in_=tab_words[0].rearrange("p t i -> p (t i)").bitcast(I32))
+        nc.sync.dma_start(lists[W3][:], offs3)
+        load_scale_rows(table_scales[:], tab_scales[0])
+        nc.sync.dma_start(lists[W1][:], offs)
         nc.sync.dma_start(out=gains[:], in_=gain.rearrange("(g p t) -> p g t", g=GROUPS, t=PACK))
-        nc.sync.dma_start(out=w3_raw[:], in_=w3_words[0].rearrange("p e i -> p (e i)").bitcast(I32))
+        load_w1(0)
+        nc.sync.dma_start(lists[W2][:], offs2)
+        load_scale_rows(raw_scales[:, :H], w3_scales[0])
+        w3_rows = w3_words[0].rearrange("p e i -> p (e i)").bitcast(I32)
+        nc.sync.dma_start(out=w3_raw[0][:], in_=w3_rows[:, :PASS])
+        nc.sync.dma_start(out=table_words[:], in_=tab_words[0].rearrange("p t i -> p (t i)").bitcast(I32))
         nc.sync.dma_start(out=w2_raw[:], in_=w2_words[0].bitcast(I32))
-        nc.sync.dma_start(out=wf_raw[0][:], in_=wf_rows[0])
+        load_scale_rows(raw_scales[:, H:], w2_scales[0])
+        nc.sync.dma_start(out=w3_raw[1][:], in_=w3_rows[:, PASS:])
+        load_w1(1)
+        nc.sync.dma_start(out=wf_raw[0], in_=wf_rows[0])
         nc.sync.dma_start(out=bias[:], in_=bf.rearrange("(p s) -> p s", s=PACK))
-        nc.sync.dma_start(out=wf_raw[1][:], in_=wf_rows[1])
+        nc.sync.dma_start(out=wf_raw[1], in_=wf_rows[1])
 
-        picked_scales = {}
+        picked = {}
 
-        def gather_scales(i, offset=None):
-            pool = held if offset is None else placed
-            picked_scales[i] = pool.tile([P, S], U8, name=f"picked_scales{i}", align_bytes=ALIGN, offset=offset)
-            nc.vector.tensor_copy(picked_scales[i][:], table_scales[:].indirect(lists[i][:]))
+        def gather(kind, i, first, n, offset=None):
+            dtype, window = (U32, table_words[:].bitcast(U32)) if kind == "w" else (U8, table_scales[:])
+            size = n * (WORD if kind == "w" else 1)
+            tile = at(fresh(size) if offset is None else offset, [P, n], dtype, f"picked_{kind}{i}_{first}")
+            entries = lists[i][:, first // PER_COLUMN : (first + n) // PER_COLUMN]
+            nc.vector.tensor_copy(tile[:], window.indirect(entries))
+            for j in range(0, n, UNIT):
+                picked[(kind, i, first + j)] = tile[:, j : j + UNIT]
 
-        for i in (COPIED, FIRST):
-            gather_scales(i)
-
-        picked_words = {}
-
-        def gather_words(stretch, i, offset=None):
-            pool = held if offset is None else placed
-            words = pool.tile([P, STRETCH], U32, name=f"picked_words{stretch}_{i}", align_bytes=ALIGN, offset=offset)
-            columns = STRETCH // PER_COLUMN
-            entries = lists[i][:, stretch * columns : (stretch + 1) * columns]
-            nc.vector.tensor_copy(words[:], table_words[:].bitcast(U32).indirect(entries))
-            picked_words[(stretch, i)] = words
-
-        def quantize_weight(rounded, name, offset=None):
+        def quantize(rounded, name, offset=None):
             width = rounded.shape[1] // PACK
             codes = held.tile([P, width], U32, name=f"{name}_codes", align_bytes=ALIGN)
-            pool = held if offset is None else placed
-            scales = pool.tile([P, width], U8, name=f"{name}_scales", align_bytes=ALIGN, offset=offset)
-            nc.vector.quantize_mx(out=codes[:].bitcast(FP8X4), scales=scales[:], in_=rounded[:])
+            scales = at(fresh(width) if offset is None else offset, [P, width], U8, f"{name}_scales")
+            nc.vector.quantize_mx(out=codes[:].bitcast(FP8X4), scales=scales[:], in_=rounded)
             return codes, scales
 
+        def reorder_columns(copy, dst, src, per_line):
+            copy(
+                out=dst.rearrange("p (g t c i) -> p g c t i", c=P // per_line, t=PACK, i=per_line),
+                in_=src.rearrange("p (g c i t) -> p g c t i", c=P // per_line, t=PACK, i=per_line),
+            )
+
         w1_q, wf_q, wf_rounded = {}, {}, {}
+        gather("s", W3, 0, S)
+        gather("s", W1, 0, 3 * CHUNK)
+        gather("s", W2, 0, 2 * CHUNK)
 
-        def round_w1(g, rounded):
-            nc.scalar.copy(
-                out=rounded[:].rearrange("p (t m j) -> p m j t", t=PACK, j=PACK),
-                in_=w1_raw[g][:].rearrange("p j (m t) -> p m j t", t=PACK),
-            )
+        w1_first = held.tile([P, PASS * PACK], BF16, name="w1_first", align_bytes=ALIGN)
+        nc.scalar.copy(
+            out=w1_first[:].rearrange("p (t m j) -> p m j t", t=PACK, j=PACK),
+            in_=w1_values(0).rearrange("p j (m t) -> p m j t", t=PACK),
+        )
+        w1_q[0] = quantize(w1_first[:], "w1_0")
 
-        w1_first = placed.tile([P, PASS * PACK], BF16, name="w1_first", align_bytes=ALIGN, offset=rounded_offset)
-        round_w1(0, w1_first)
-        w1_second = placed.tile([P, PASS * PACK], BF16, name="w1_second", align_bytes=ALIGN, offset=second_offset)
-        round_w1(1, w1_second)
-
-        def h_tile(units):
-            return placed.tile([P, units * COLUMNS], BF16, name="h_rounded", align_bytes=ALIGN, offset=wf_offset)
-
-        def round_wf(g, half, rounded):
-            nc.scalar.copy(
-                out=rounded.rearrange("p (s m t) -> p m t s", s=2, t=PACK),
-                in_=wf_raw[g][:].rearrange("p t (m s) -> p m t s", s=PACK)[:, :, :, 2 * half : 2 * half + 2],
-            )
-            wf_rounded[(g, half)] = rounded
-
-        def quantize_wf(g, half, offset):
-            wf_q[(g, half)] = quantize_weight(wf_rounded[(g, half)], f"wf_{g}_{half}", offset)
-
+        scales_q = {}
+        scales_q[W3] = held.tile([P, H], U8, name="w3_scales", align_bytes=ALIGN)
+        reorder_columns(nc.gpsimd.tensor_copy, scales_q[W3][:], raw_scales[:, :H], 16)
+        w3_codes = [held.tile([P, PASS], U32, name=f"w3_codes{g}", align_bytes=ALIGN) for g in range(GROUPS)]
+        reorder_columns(nc.gpsimd.tensor_copy, w3_codes[0][:].bitcast(I32), w3_raw[0][:], 4)
         wide_gains = held.tile([P, GROUPS, UNIT, PACK], F32, name="wide_gains")
         nc.scalar.copy(out=wide_gains[:], in_=gains[:].unsqueeze(2).to_broadcast([P, GROUPS, UNIT, PACK]))
-        w1_q[0] = quantize_weight(w1_first, "w1_0")
-        gather_scales(SECOND, rounded_offset)
-        w1_q[1] = quantize_weight(w1_second, "w1_1")
-        for i in (COPIED, FIRST, SECOND):
-            gather_words(0, i)
-
-        def reorder_columns(engine, dst, src, per_line):
-            engine.tensor_copy(
-                out=dst.rearrange("p (g t c i) -> p g c t i", g=GROUPS, t=PACK, i=per_line),
-                in_=src.rearrange("p (g c i t) -> p g c t i", g=GROUPS, t=PACK, i=per_line),
-            )
-
-        w23_scales = placed.tile([P, H], U8, name="w23_scales", align_bytes=ALIGN, offset=rounded_offset + S)
-        reorder_columns(nc.gpsimd, w23_scales[:], raw_scales[:], 16)
-        for i in (COPIED, FIRST, SECOND)[:EARLY]:
-            gather_words(1, i)
-        w3_codes = held.tile([P, H], U32, name="w3_codes", align_bytes=ALIGN)
-        reorder_columns(nc.gpsimd, w3_codes[:].bitcast(I32), w3_raw[:], 4)
         w2_codes = held.tile([P, 2 * H], U8, name="w2_codes", align_bytes=ALIGN)
-        reorder_columns(nc.gpsimd, w2_codes[:].bitcast(U16), w2_raw[:].bitcast(U16), 8)
+        reorder_columns(nc.scalar.copy, w2_codes[:].bitcast(U16), w2_raw[:].bitcast(U16), 8)
+        scales_q[W2] = held.tile([P, H], U8, name="w2_scales", align_bytes=ALIGN)
+        reorder_columns(nc.gpsimd.tensor_copy, scales_q[W2][:], raw_scales[:, H:], 16)
+        reorder_columns(nc.gpsimd.tensor_copy, w3_codes[1][:].bitcast(I32), w3_raw[1][:], 4)
 
-        wf_first = held.tile([P, PASS * PACK], BF16, name="wf_first", align_bytes=ALIGN)
+        h_offset = fresh(PASS * PACK * 2)
+        w1_second = at(h_offset, [P, PASS * PACK], BF16, "w1_second")
         nc.gpsimd.tensor_copy(
-            out=wf_first[:].rearrange("p (s m t) -> p m s t", s=PACK, t=PACK),
-            in_=wf_raw[0][:].rearrange("p t (m s) -> p m s t", s=PACK),
+            out=w1_second[:].rearrange("p (t m j) -> p m t j", t=PACK, j=PACK),
+            in_=w1_values(1).rearrange("p j (m t) -> p m t j", t=PACK),
         )
-        for half in range(2):
-            wf_rounded[(0, half)] = wf_first[:, half * 2 * PASS : (half + 1) * 2 * PASS]
+
+        for i, first in ((W3, 0), (W1, 0), (W3, CHUNK), (W2, 0), (W1, CHUNK)):
+            gather("w", i, first, CHUNK)
 
         def stationary(i, g, t):
             col = g * PASS + t * P
-            if i == 0:
+            if i == W1:
                 return w1_q[g][0][:, t * P : (t + 1) * P].bitcast(FP8X4), w1_q[g][1][:, t * P : (t + 1) * P]
-            if i == 1:
-                return w2_codes[:, 2 * col : 2 * (col + P)].bitcast(FP4X4), w23_scales[:, col : col + P]
-            return w3_codes[:, col : col + P].bitcast(FP8X4), w23_scales[W3_SHIFT:P, col : col + P]
-
-        order = [
-            (first + offset, g)
-            for first in range(0, S, STRETCH) for g in range(GROUPS) for offset in range(0, STRETCH, UNIT)
-        ]
+            if i == W2:
+                return w2_codes[:, 2 * col : 2 * (col + P)].bitcast(FP4X4), scales_q[W2][:, col : col + P]
+            return w3_codes[g][:, t * P : (t + 1) * P].bitcast(FP8X4), scales_q[W3][:, col : col + P]
 
         def first_product(i, k):
             start, g = order[k]
-            words = picked_words[(start // STRETCH, i)][:, start % STRETCH : start % STRETCH + UNIT]
             bank = psum.tile([P, PACK, UNIT], F32, name=f"first{i}")
             for t in range(PACK):
                 codes, scales = stationary(i, g, t)
                 nc.tensor.matmul_mx(
                     out=bank[:, t, :], lhsT=codes, lhsT_scale=scales,
-                    rhs=words.bitcast(FP8X4), rhs_scale=picked_scales[i][:, start : start + UNIT],
+                    rhs=picked[("w", i, start)].bitcast(FP8X4), rhs_scale=picked[("s", i, start)],
                     start=True, stop=True,
                 )
-            return bank
-
-        def ends_stretch(k):
-            return k % PER_STRETCH == PER_STRETCH - 1
-
-        room = [(5 if ends_stretch(k) or k == LAST_GAIN else 5 / 2) * UNIT_BYTES for k in range(LAST_GAIN + 1)]
-        room = [int(size) for size in room]
-        taken = [0] * len(room)
-
-        def behind_gain(k, size):
-            taken[k] = taken[k] + size
-            assert taken[k] <= room[k]
-            return silu_offset + sum(room[:k]) + taken[k] - size
-
-        free_copies = LEAD + COPY_AHEAD
-        copy_place = [w1_offset[1] + k * UNIT_BYTES for k in range(COPY_AHEAD)]
-        copy_place.extend(copy_place[: free_copies - COPY_AHEAD])
-        max_place = [w1_offset[0] + k * UNIT_BYTES for k in range(LEAD)]
-        max_place.extend(behind_gain(min(k, UNITS - 2) - LEAD, UNIT_BYTES) for k in range(LEAD, UNITS))
-        copy_place.extend(behind_gain(k - free_copies, UNIT_BYTES) for k in range(free_copies, UNITS))
-
-        gathers = {}
-        for stretch in range(1, S // STRETCH):
-            for i, ahead in ((COPIED, COPY_AHEAD + 1), (FIRST, COPY_AHEAD), (SECOND, 2)):
-                if (stretch, i) not in picked_words:
-                    k = stretch * PER_STRETCH - ahead
-                    place = behind_gain(k - LEAD, STRETCH * WORD) if k >= LEAD else copy_place[k + 1]
-                    gathers[k] = (stretch, i, place)
-
-        def bank_by_pairs(bank):
             return bank[:].rearrange("p t (c i) -> p c t i", i=2)
 
-        def by_pairs(tile):
-            return tile[:].rearrange("p (c t i) -> p c t i", t=PACK, i=2)
+        def by_pairs(values):
+            return values.rearrange("p (c t i) -> p c t i", t=PACK, i=2)
 
         copied, first_maxima, silus = {}, {}, {}
+        copy_place = {k: fresh(UNIT_BYTES) for k in range(COPY_AHEAD)}
 
         def copy_out(k):
             bank = first_product(COPIED, k)
-            copied[k] = placed.tile([P, COLUMNS], F32, name=f"copied{k}", offset=copy_place[k])
-            nc.scalar.copy(out=by_pairs(copied[k]), in_=bank_by_pairs(bank))
+            copied[k] = at(copy_place[k], [P, COLUMNS], F32, f"copied{k}")
+            nc.scalar.copy(out=by_pairs(copied[k][:]), in_=bank)
 
-        def first_max(k):
+        def first_max(k, room):
             bank = first_product(FIRST, k)
-            first_maxima[k] = work.tile([P, COLUMNS], F32, name="first_max")
-            nc.vector.tensor_tensor(
-                out=by_pairs(first_maxima[k]), in0=bank_by_pairs(bank), in1=by_pairs(copied[k]), op=ALU.max
-            )
+            size = first_max_bytes(k)
+            offset = fresh(size) if room is None else behind(room, size)
+            rooms[f"max{k}"] = [offset + UNIT_BYTES, offset + size]
+            copy_place[k + COPY_AHEAD] = offset
+            first_maxima[k] = at(offset, [P, size // WORD], F32, f"first_max{k}")[:, :COLUMNS]
+            nc.vector.tensor_tensor(out=by_pairs(first_maxima[k]), in0=bank, in1=by_pairs(copied[k][:]), op=ALU.max)
 
-        def second_max_and_silu(k):
-            bank = first_product(SECOND, k)
-            m = placed.tile([P, COLUMNS], F32, name=f"second_max{k}", offset=max_place[k])
-            if k <= LAST_GAIN:
-                offset = silu_offset + sum(room[:k])
-                silus[k] = placed.tile([P, room[k] // WORD], F32, name=f"silu{k}", offset=offset)[:, :COLUMNS]
+        def silu_tile(k):
+            if k < 2 * PAIRS:
+                silus[k] = pairs[k // 2][:, k % 2 * COLUMNS : (k % 2 + 1) * COLUMNS]
             else:
                 silus[k] = held.tile([P, COLUMNS], F32, name=f"silu{k}")[:]
-            nc.vector.tensor_tensor(
-                out=by_pairs(m), in0=bank_by_pairs(bank), in1=by_pairs(first_maxima[k]), op=ALU.max
+
+        y_scales = held.tile([P, S], U8, name="y_scales", align_bytes=ALIGN)
+        y_codes = held.tile([P, S], U32, name="y_codes", align_bytes=ALIGN)
+        y_rows = out_0.rearrange("(p s) j -> p s j", s=PACK)
+        y_words = out_1[0].rearrange("p m t -> p (m t)").bitcast(I32)
+        h_q, logits, y, y_rounded = {}, {}, {}, {}
+
+        def round_wf(index, offset):
+            g, half = divmod(index, 2)
+            wf_rounded[index] = at(offset, [P, 2 * PASS], BF16, f"wf_rounded{index}")
+            nc.scalar.copy(
+                out=wf_rounded[index][:].rearrange("p (s m t) -> p m t s", s=2, t=PACK),
+                in_=wf_raw[g].rearrange("p t (m s) -> p m t s", s=PACK)[:, :, :, 2 * half : 2 * half + 2],
             )
+
+        def bias_on_scalar(out, s, bank):
+            nc.scalar.activation(out=out, in_=bank, func=ACT.Identity, bias=bias[:, s : s + 1])
+
+        def bias_on_vector(out, s, bank):
+            nc.vector.tensor_scalar(out=out, in0=bank, scalar1=bias[:, s : s + 1], scalar2=None, op0=ALU.add)
+
+        def add_bias(c, offset):
+            y[c] = at(offset, [P, PACK, CHUNK], F32, f"y{c}")
+            for s in range(PACK):
+                bias_on_scalar(y[c][:, s, :], s, logits[c][s // 2][:, s % 2, :])
+            nc.sync.dma_start(out=y_rows[:, :, c * CHUNK : (c + 1) * CHUNK], in_=y[c][:])
+
+        def round_y(copy, rounded, values):
+            copy(
+                out=rounded.rearrange("p (c i s) -> p c s i", s=PACK, i=4),
+                in_=values.rearrange("p s (c i) -> p c s i", i=4),
+            )
+
+        def round_chunk(c, offset):
+            y_rounded[c] = at(offset, [P, CHUNK * PACK], BF16, f"y_rounded{c}")
+            round_y(nc.scalar.copy, y_rounded[c][:], y[c][:])
+
+        def quantize_y(rounded, first, n):
+            nc.vector.quantize_mx(
+                out=y_codes[:, first : first + n].bitcast(FP8X4), scales=y_scales[:, first : first + n], in_=rounded
+            )
+
+        def second_max(k, room):
+            bank = first_product(SECOND, k)
+            m = at(fresh(UNIT_BYTES) if room is None else behind(room, UNIT_BYTES), [P, COLUMNS], F32, f"second_max{k}")
+            nc.vector.tensor_tensor(out=by_pairs(m[:]), in0=bank, in1=by_pairs(first_maxima[k]), op=ALU.max)
+            silu_tile(k)
             nc.scalar.activation(
                 out=silus[k].rearrange("p (c i t) -> p c i t", t=PACK, i=2),
                 in_=m[:].rearrange("p (c t i) -> p c i t", t=PACK, i=2),
                 func=ACT.Silu,
             )
+            if k + COPY_AHEAD < UNITS:
+                copy_out(k + COPY_AHEAD)
+            for kind, index, size in extras.get(k, []):
+                {"wf": round_wf, "bias": add_bias, "round": round_chunk}[kind](index, behind(f"max{k}", size))
 
-        def apply_gain(engine, k, h_rounded):
-            engine.tensor_tensor(
-                out=h_rounded, in0=silus[k], in1=wide_gains[:, order[k][1]].rearrange("p j t -> p (j t)"), op=ALU.mult
+        def gain_of(k):
+            return wide_gains[:, order[k][1]].rearrange("p j t -> p (j t)")
+
+        h_rounded = {}
+
+        def pair_gain(q):
+            h_rounded[q] = at(h_offset, [P, 2, COLUMNS], BF16, f"h_pair{q}")
+            nc.gpsimd.tensor_tensor(
+                out=h_rounded[q][:], in0=pairs[q][:, : 2 * COLUMNS].rearrange("p (u c) -> p u c", u=2),
+                in1=gain_of(2 * q).unsqueeze(1).to_broadcast([P, 2, COLUMNS]), op=ALU.mult,
             )
 
-        def quantize_h(h_rounded, offset=None):
-            width = h_rounded.shape[1] // PACK
-            codes = work.tile([P, width], U32, name="h_codes", align_bytes=ALIGN)
-            if offset is None:
-                scales = work.tile([P, width], U8, name="h_scales", align_bytes=ALIGN)
-            else:
-                scales = placed.tile([P, width], U8, name="h_scales_held", align_bytes=ALIGN, offset=offset)
-            nc.vector.quantize_mx(out=codes[:].bitcast(FP8X4), scales=scales[:], in_=h_rounded)
-            return codes, scales
-
-        def second_pass(out, g, s, h_codes, h_scales, start, stop):
-            codes, scales = wf_q[(g, s // 2)]
+        def second_pass(out, g, s, h, start, stop):
+            codes, scales = wf_q[2 * g + s // 2]
             cols = slice(s % 2 * P, (s % 2 + 1) * P)
             nc.tensor.matmul_mx(
                 out=out, lhsT=codes[:, cols].bitcast(FP8X4), lhsT_scale=scales[:, cols],
-                rhs=h_codes.bitcast(FP8X4), rhs_scale=h_scales, start=start, stop=stop,
+                rhs=h[0][:].bitcast(FP8X4), rhs_scale=h[1][:], start=start, stop=stop,
             )
 
-        def bias_on_scalar(y, s, logits):
-            nc.scalar.activation(out=y[:, s, :], in_=logits, func=ACT.Identity, bias=bias[:, s : s + 1])
-
-        def bias_on_vector(y, s, logits):
-            nc.vector.tensor_scalar(out=y[:, s, :], in0=logits, scalar1=bias[:, s : s + 1], scalar2=None, op0=ALU.add)
-
-        y_scales = held.tile([P, S], U8, name="y_scales", align_bytes=ALIGN)
-        y_rows = out_0.rearrange("(p s) j -> p s j", s=PACK)
-        y_words = out_1[0].rearrange("p m t -> p (m t)").bitcast(I32)
-
-        def y_tile(width):
-            return work.tile([P, PACK, width], F32, name="y", bufs=3)
-
-        def round_y(copy, y_rounded, y):
-            copy(
-                out=y_rounded.rearrange("p (c i s) -> p c s i", s=PACK, i=4),
-                in_=y.rearrange("p s (c i) -> p c s i", i=4),
-            )
-
-        h_rounded, logits, y, y_rounded = {}, {}, {}, {}
-
-        def store_codes(stretch, gain_index):
-            cols = slice(stretch * STRETCH, (stretch + 1) * STRETCH)
-            place = behind_gain(gain_index, STRETCH * WORD)
-            codes = placed.tile([P, STRETCH], U32, name=f"y_codes{stretch}", align_bytes=ALIGN, offset=place)
-            nc.vector.quantize_mx(out=codes[:].bitcast(FP8X4), scales=y_scales[:, cols], in_=y_rounded[stretch][:])
-            nc.sync.dma_start(out=y_words[:, cols], in_=codes[:].bitcast(I32))
-
-        def second_product(stretch):
-            last = (stretch + 1) * PER_STRETCH - 1
-            if stretch == 0:
-                for g in range(GROUPS):
-                    for half in range(2):
-                        quantize_wf(g, half, behind_gain(last, PASS // 2))
-            else:
-                store_codes(stretch - 1, last)
-            codes, scales = quantize_h(h_rounded[stretch][:])
-            y[stretch] = y_tile(STRETCH)
-            logits[stretch] = []
+        def second_product(c):
+            logits[c] = []
             for b in range(2):
-                logits[stretch].append(psum.tile([P, 2, STRETCH], F32, name="logits"))
+                logits[c].append(psum.tile([P, 2, CHUNK], F32, name="logits"))
                 for e in range(2):
                     for g in range(GROUPS):
-                        cols = slice(g * STRETCH, (g + 1) * STRETCH)
-                        second_pass(
-                            logits[stretch][b][:, e, :], g, 2 * b + e, codes[:, cols], scales[:, cols],
-                            g == 0, g == GROUPS - 1,
-                        )
-
-        def y_step(stretch, step):
-            if step < 2:
-                for e in range(2):
-                    bias_on_scalar(y[stretch], 2 * step + e, logits[stretch][step][:, e, :])
-                if step == 1:
-                    nc.sync.dma_start(out=y_rows[:, :, stretch * STRETCH : (stretch + 1) * STRETCH], in_=y[stretch][:])
-            else:
-                y_rounded[stretch] = work.tile([P, STRETCH * PACK], BF16, name="y_rounded", align_bytes=ALIGN)
-                round_y(nc.scalar.copy, y_rounded[stretch][:], y[stretch][:])
+                        second_pass(logits[c][b][:, e, :], g, 2 * b + e, h_q[(c, g)], g == 0, g == GROUPS - 1)
 
         for k in range(COPY_AHEAD):
             copy_out(k)
-        for k in range(MAX_AHEAD):
-            first_max(k)
+        first_max(0, None)
+        first_max(1, None)
+        second_max(0, None)
+        gather("w", W2, CHUNK, CHUNK, copy_place[0])
+        first_max(2, None)
+        second_max(1, None)
+        for q in range(PAIRS + 1):
+            room = f"burst{q}"
+            if q == 0:
+                w1_q[1] = quantize(w1_second[:], "w1_1")
+            else:
+                for index in wf_quantisers.get(q, []):
+                    wf_q[index] = quantize(wf_rounded[index][:], f"wf{index}", behind(room, PASS // 2))
+                start, g = order[2 * q - 2]
+                h_q[(start // CHUNK, g)] = quantize(h_rounded[q - 1][:].rearrange("p u c -> p (u c)"), f"h{q - 1}", behind(room, CHUNK))
+                if g == GROUPS - 1:
+                    second_product(start // CHUNK)
+            if q < PAIRS:
+                pair_gain(q)
+            for k in burst_units[q]:
+                for kind, i, first, n in gathers.get(k, []):
+                    gather(kind, i, first, n, behind(room, n * (WORD if kind == "w" else 1)))
+                if k < UNITS:
+                    first_max(k, room)
+                second_max(k - 1, room)
 
-        last_stretch = S // STRETCH - 1
-        for k in range(UNITS):
-            stretch, place = divmod(k, PER_STRETCH)
-            if place == 0:
-                h_rounded[stretch] = h_tile(PER_STRETCH if stretch < last_stretch else 1)
-            if place == 1 and stretch > 0:
-                second_product(stretch - 1)
-            second_max_and_silu(k)
-            if k + COPY_AHEAD < UNITS and k + COPY_AHEAD not in copied:
-                copy_out(k + COPY_AHEAD)
-            if k in gathers:
-                gather_words(*gathers[k])
-            if k + MAX_AHEAD < UNITS:
-                first_max(k + MAX_AHEAD)
-            if k < 2:
-                rounded = placed.tile([P, 2 * PASS], BF16, name=f"wf_rounded{k}", align_bytes=ALIGN, offset=max_place[k])
-                round_wf(1, k, rounded[:])
-            if k <= LAST_GAIN:
-                apply_gain(nc.gpsimd, k, h_rounded[stretch][:, place * COLUMNS : (place + 1) * COLUMNS])
-            done, step = divmod(k + 1 - Y_DELAY, PER_STRETCH)
-            if done > 0 and step < 3:
-                y_step(done - 1, step)
-
-        banks = [[psum.tile([P, 2, UNIT], F32, name=f"first{i}") for b in range(2)] for i in (COPIED, FIRST)]
+        a0, a1, b0, b1 = range(2 * PAIRS, UNITS)
+        h_last, h_place = {}, {}
 
         def last_gain(k):
-            place = behind_gain(LAST_GAIN, COLUMNS * 2)
-            rounded = placed.tile([P, COLUMNS], BF16, name=f"h_last{k}", align_bytes=ALIGN, offset=place)
-            apply_gain(nc.vector, k, rounded[:])
-            return rounded[:]
+            place = behind(f"burst{PAIRS}", COLUMNS * 2 * (1 + (k == b1)))
+            h_place[k] = place
+            h_last[k] = at(place, [P, COLUMNS], BF16, f"h_last{k}")
+            nc.vector.tensor_tensor(out=h_last[k][:], in0=silus[k], in1=gain_of(k), op=ALU.mult)
 
-        def last_product(k, rounded, offset=None):
-            g = order[k][1]
-            codes, scales = quantize_h(rounded, offset)
-            for s in range(PACK):
-                second_pass(
-                    banks[k % 2][s // 2][:, s % 2, :], g, s, codes[:], scales[:],
-                    g == 0 and s % 2 == 0, g == GROUPS - 1 and s % 2 == 1,
-                )
+        def last_quantize(k):
+            h_q[k] = quantize(h_last[k][:], f"h_last{k}")
 
-        first_0, second_0, first_1, second_1 = range(LAST_GAIN, UNITS)
-        last_product(first_0, h_rounded[last_stretch][:], behind_gain(LAST_GAIN, UNIT))
-        h_first_1 = last_gain(first_1)
-        h_second_0 = last_gain(second_0)
-        last_product(first_1, h_first_1)
-        h_second_1 = last_gain(second_1)
-        last_product(second_0, h_second_0)
-        last_product(second_1, h_second_1)
-        y_step(last_stretch - 1, 2)
-        store_codes(last_stretch - 1, LAST_GAIN)
+        add_bias(2, fresh(Y_BYTES))
+        round_chunk(1, fresh(Y_BYTES // 2))
+        last_gain(a0)
+        last_gain(a1)
+        last_gain(b0)
+        last_quantize(a0)
+        last_quantize(a1)
+        bank_a = psum.tile([P, PACK, UNIT], F32, name=f"first{COPIED}")
+        for s in range(PACK):
+            for g in range(GROUPS):
+                second_pass(bank_a[:, s, :], g, s, h_q[a0 + g], g == 0, g == GROUPS - 1)
+        last_gain(b1)
+        last_quantize(b0)
+        banks_b = [psum.tile([P, 2, UNIT], F32, name=f"first{FIRST}") for b in range(2)]
+        for s in range(PACK):
+            second_pass(banks_b[s // 2][:, s % 2, :], 0, s, h_q[b0], s % 2 == 0, False)
+        last_quantize(b1)
+        for s in range(PACK):
+            second_pass(banks_b[s // 2][:, s % 2, :], 1, s, h_q[b1], False, s % 2 == 1)
+        quantize_y(y_rounded[0][:], 0, CHUNK)
+        y_rounded[2] = at(h_place[b1], [P, CHUNK * PACK], BF16, "y_rounded2")
+        nc.gpsimd.tensor_copy(
+            out=y_rounded[2][:].rearrange("p (j s) -> p j s", s=PACK), in_=y[2][:].rearrange("p s j -> p j s")
+        )
 
-        y_last_rounded = work.tile([P, STRETCH * PACK], BF16, name="y_rounded", align_bytes=ALIGN)
-        y_last_codes = work.tile([P, STRETCH], U32, name="y_codes", align_bytes=ALIGN)
-        for half in range(2):
-            first = last_stretch * STRETCH + half * UNIT
-            y_last = y_tile(UNIT)
-            for s in range(PACK):
-                add_bias = bias_on_scalar if half == 0 or s < 2 else bias_on_vector
-                add_bias(y_last, s, banks[half][s // 2][:, s % 2, :])
-            queue = nc.sync if half == 0 else nc.scalar
-            queue.dma_start(out=y_rows[:, :, first : first + UNIT], in_=y_last[:])
-            rounded = y_last_rounded[:, half * COLUMNS : (half + 1) * COLUMNS]
-            round_y(nc.vector.tensor_copy, rounded, y_last[:])
-            nc.vector.quantize_mx(
-                out=y_last_codes[:, half * UNIT : (half + 1) * UNIT].bitcast(FP8X4),
-                scales=y_scales[:, first : first + UNIT], in_=rounded,
-            )
-        nc.sync.dma_start(out=y_words[:, last_stretch * STRETCH :], in_=y_last_codes[:].bitcast(I32))
+        y_a = held.tile([P, PACK, UNIT], F32, name="y_a")
+        for s in range(PACK):
+            bias_on_scalar(y_a[:, s, :], s, bank_a[:, s, :])
+        nc.sync.dma_start(out=y_rows[:, :, c3a:c3b], in_=y_a[:])
+        y_b = held.tile([P, PACK, UNIT], F32, name="y_b")
+        last_rounded = held.tile([P, 2 * COLUMNS], BF16, name="last_rounded", align_bytes=ALIGN)
+        round_y(nc.vector.tensor_copy, last_rounded[:, :COLUMNS], y_a[:])
+        for s in range(PACK):
+            (bias_on_scalar if s < 2 else bias_on_vector)(y_b[:, s, :], s, banks_b[s // 2][:, s % 2, :])
+        nc.scalar.dma_start(out=y_rows[:, :, c3b:], in_=y_b[:])
+        quantize_y(y_rounded[1][:], CHUNK, CHUNK)
+        round_y(nc.vector.tensor_copy, last_rounded[:, COLUMNS:], y_b[:])
+        quantize_y(y_rounded[2][:], c2, CHUNK)
+        nc.sync.dma_start(out=y_words[:, :c3a], in_=y_codes[:, :c3a].bitcast(I32))
+        quantize_y(last_rounded[:], c3a, CHUNK)
+        nc.sync.dma_start(out=y_words[:, c3a:], in_=y_codes[:, c3a:].bitcast(I32))
         for q in range(QUADS):
             queue = nc.scalar if q % 2 == 0 else nc.sync
             queue.dma_start(

@@ -1,6 +1,7 @@
 from contextlib import ExitStack
 
 import concourse.mybir as mybir
+from concourse.masks import make_identity
 
 K, T, S, H, N = 512, 2048, 1024, 1024, 512
 FLOPS = 2 * S * (3 * K * H + H * N)
@@ -31,7 +32,7 @@ CHUNK = 256
 UNITS = GROUPS * S // UNIT
 W1, W2, W3 = 0, 1, 2
 COPIED, FIRST, SECOND = W3, W1, W2
-COPY_AHEAD = 4
+COPY_AHEAD = 6
 PAIRS = 6
 
 
@@ -75,13 +76,13 @@ def tile_list_opcode_trigram_families_kernel(
         extras = {
             1: [("wf", 0, HALF)], 2: [("wf", 1, HALF)], 4: [("wf", 2, HALF)], 6: [("wf", 3, HALF)],
             9: [("bias", 0, Y_BYTES)], 11: [("bias", 1, Y_BYTES)],
-            12: [("round", 0, Y_BYTES // 2)],
+            10: [("round", 0, Y_BYTES // 2)], 12: [("round", 1, Y_BYTES // 2)], 15: [("bias", 2, Y_BYTES)],
         }
         c2, c3a, c3b = 2 * CHUNK, 3 * CHUNK, 3 * CHUNK + UNIT
         gathers = {
-            4: [("w", W3, c2, CHUNK)], 5: [("s", W2, c2, CHUNK)], 6: [("w", W1, c2, CHUNK)], 7: [("w", W2, c2, CHUNK)],
-            8: [("w", W3, c3a, UNIT)], 9: [("s", W1, c3a, CHUNK)], 10: [("w", W3, c3b, UNIT), ("w", W1, c3a, UNIT)],
-            11: [("s", W2, c3a, CHUNK)], 12: [("w", W2, c3a, UNIT)], 13: [("w", W1, c3b, UNIT)], 14: [("w", W2, c3b, UNIT)],
+            3: [("w", W3, c2, CHUNK)], 5: [("s", W2, c2, CHUNK)], 6: [("w", W1, c2, CHUNK)], 7: [("w", W3, c3a, UNIT)],
+            8: [("w", W2, c2, CHUNK)], 9: [("w", W3, c3b, UNIT)],
+            11: [("s", W1, c3a, CHUNK), ("w", W1, c3a, UNIT)], 12: [("s", W2, c3a, CHUNK), ("w", W2, c3a, UNIT)], 13: [("w", W1, c3b, UNIT)], 14: [("w", W2, c3b, UNIT)],
         }
         wf_quantisers = {2: [0, 1], 3: [2, 3]}
         burst_units = [[3, 4, 5]] + [[2 * q + 4, 2 * q + 5] for q in range(1, PAIRS)] + [[UNITS]]
@@ -199,6 +200,13 @@ def tile_list_opcode_trigram_families_kernel(
         reorder_columns(nc.gpsimd.tensor_copy, w3_codes[0][:].bitcast(I32), w3_raw[0][:], 4)
         wide_gains = held.tile([P, GROUPS, UNIT, PACK], F32, name="wide_gains")
         nc.scalar.copy(out=wide_gains[:], in_=gains[:].unsqueeze(2).to_broadcast([P, GROUPS, UNIT, PACK]))
+        identity = held.tile([P, P], F32, name="identity")
+        make_identity(nc, identity[:])
+        turning = psum.tile([P, GROUPS, P], F32, name="logits")
+        for g in range(GROUPS):
+            nc.tensor.transpose(turning[:, g, :], wide_gains[:, g, : P // PACK].rearrange("p j t -> p (j t)"), identity[:])
+        turned_gains = held.tile([P, GROUPS, P], F32, name="turned_gains")
+        nc.scalar.copy(out=turned_gains[:], in_=turning[:])
         w2_codes = held.tile([P, 2 * H], U8, name="w2_codes", align_bytes=ALIGN)
         reorder_columns(nc.scalar.copy, w2_codes[:].bitcast(U16), w2_raw[:].bitcast(U16), 8)
         scales_q[W2] = held.tile([P, H], U8, name="w2_scales", align_bytes=ALIGN)
@@ -262,7 +270,6 @@ def tile_list_opcode_trigram_families_kernel(
                 silus[k] = held.tile([P, COLUMNS], F32, name=f"silu{k}")[:]
 
         y_scales = held.tile([P, S], U8, name="y_scales", align_bytes=ALIGN)
-        y_codes = held.tile([P, S], U32, name="y_codes", align_bytes=ALIGN)
         y_rows = out_0.rearrange("(p s) j -> p s j", s=PACK)
         y_words = out_1[0].rearrange("p m t -> p (m t)").bitcast(I32)
         h_q, logits, y, y_rounded = {}, {}, {}, {}
@@ -297,10 +304,14 @@ def tile_list_opcode_trigram_families_kernel(
             y_rounded[c] = at(offset, [P, CHUNK * PACK], BF16, f"y_rounded{c}")
             round_y(nc.scalar.copy, y_rounded[c][:], y[c][:])
 
-        def quantize_y(rounded, first, n):
-            nc.vector.quantize_mx(
-                out=y_codes[:, first : first + n].bitcast(FP8X4), scales=y_scales[:, first : first + n], in_=rounded
-            )
+        def quantize_y(rounded, first, codes):
+            n = codes.shape[1]
+            nc.vector.quantize_mx(out=codes.bitcast(FP8X4), scales=y_scales[:, first : first + n], in_=rounded)
+
+        def store_codes(c, offset):
+            codes = at(offset, [P, CHUNK], U32, f"y_codes{c}")
+            quantize_y(y_rounded[c][:], c * CHUNK, codes[:])
+            nc.sync.dma_start(out=y_words[:, c * CHUNK : (c + 1) * CHUNK], in_=codes[:].bitcast(I32))
 
         def second_max(k, room):
             bank = first_product(SECOND, k)
@@ -377,55 +388,62 @@ def tile_list_opcode_trigram_families_kernel(
         h_last, h_place = {}, {}
 
         def last_gain(k):
-            place = behind(f"burst{PAIRS}", COLUMNS * 2 * (1 + (k == b1)))
+            place = behind(f"burst{PAIRS}", COLUMNS * 2 * (1 + 2 * (k == b0)))
             h_place[k] = place
-            h_last[k] = at(place, [P, COLUMNS], BF16, f"h_last{k}")
-            nc.vector.tensor_tensor(out=h_last[k][:], in0=silus[k], in1=gain_of(k), op=ALU.mult)
+            h_last[k] = at(place, [P, COLUMNS * (1 + (k == b0))], BF16, f"h_last{k}")[:, :COLUMNS]
+            nc.vector.tensor_tensor(
+                out=h_last[k].rearrange("p (u c) -> p u c", c=P),
+                in0=bank_gains[:, order[k][1], :].unsqueeze(1).to_broadcast([P, PACK, P]),
+                in1=silus[k].rearrange("p (u c) -> p u c", c=P), op=ALU.mult,
+            )
 
         def last_quantize(k):
-            h_q[k] = quantize(h_last[k][:], f"h_last{k}")
+            h_q[k] = quantize(h_last[k], f"h_last{k}")
 
-        add_bias(2, fresh(Y_BYTES))
-        round_chunk(1, fresh(Y_BYTES // 2))
-        last_gain(a0)
+        bank_gains = psum.tile([P, GROUPS, P], F32, name=f"first{COPIED}")
+        for g in range(GROUPS):
+            nc.tensor.transpose(bank_gains[:, g, :], turned_gains[:, g, :], identity[:])
+        bank_a = psum.tile([P, PACK, UNIT], F32, name=f"first{COPIED}")
+        banks_b = [psum.tile([P, 2, UNIT], F32, name=f"first{FIRST}") for b in range(2)]
+        columns = [[bank_a[:, s, :] for s in range(PACK)], [banks_b[s // 2][:, s % 2, :] for s in range(PACK)]]
+
+        def last_product(k):
+            last_quantize(k)
+            half, g = divmod(k - a0, GROUPS)
+            for s in range(PACK):
+                per_bank = PACK if half == 0 else 2
+                second_pass(
+                    columns[half][s], g, s, h_q[k],
+                    g == 0 and s % per_bank == 0, g == GROUPS - 1 and s % per_bank == per_bank - 1,
+                )
+
+        h_last[a0] = at(h_offset, [P, COLUMNS], BF16, "h_last_gpsimd")[:]
+        nc.gpsimd.tensor_tensor(out=h_last[a0], in0=silus[a0], in1=gain_of(a0), op=ALU.mult)
         last_gain(a1)
         last_gain(b0)
-        last_quantize(a0)
-        last_quantize(a1)
-        bank_a = psum.tile([P, PACK, UNIT], F32, name=f"first{COPIED}")
-        for s in range(PACK):
-            for g in range(GROUPS):
-                second_pass(bank_a[:, s, :], g, s, h_q[a0 + g], g == 0, g == GROUPS - 1)
+        last_product(a0)
+        last_product(a1)
         last_gain(b1)
-        last_quantize(b0)
-        banks_b = [psum.tile([P, 2, UNIT], F32, name=f"first{FIRST}") for b in range(2)]
-        for s in range(PACK):
-            second_pass(banks_b[s // 2][:, s % 2, :], 0, s, h_q[b0], s % 2 == 0, False)
-        last_quantize(b1)
-        for s in range(PACK):
-            second_pass(banks_b[s // 2][:, s % 2, :], 1, s, h_q[b1], False, s % 2 == 1)
-        quantize_y(y_rounded[0][:], 0, CHUNK)
-        y_rounded[2] = at(h_place[b1], [P, CHUNK * PACK], BF16, "y_rounded2")
-        nc.gpsimd.tensor_copy(
-            out=y_rounded[2][:].rearrange("p (j s) -> p j s", s=PACK), in_=y[2][:].rearrange("p s j -> p j s")
-        )
+        last_product(b0)
+        store_codes(0, h_place[a1])
+        last_product(b1)
+        store_codes(1, h_place[b0])
+        y_rounded[2] = at(h_place[b0] + CHUNK * WORD, [P, CHUNK * PACK], BF16, "y_rounded2")
+        round_y(nc.vector.tensor_copy, y_rounded[2][:], y[2][:])
 
-        y_a = held.tile([P, PACK, UNIT], F32, name="y_a")
+        y_last = held.tile([P, PACK, CHUNK], F32, name="y_last")
         for s in range(PACK):
-            bias_on_scalar(y_a[:, s, :], s, bank_a[:, s, :])
-        nc.sync.dma_start(out=y_rows[:, :, c3a:c3b], in_=y_a[:])
-        y_b = held.tile([P, PACK, UNIT], F32, name="y_b")
+            bias_on_scalar(y_last[:, s, :UNIT], s, columns[0][s])
         last_rounded = held.tile([P, 2 * COLUMNS], BF16, name="last_rounded", align_bytes=ALIGN)
-        round_y(nc.vector.tensor_copy, last_rounded[:, :COLUMNS], y_a[:])
         for s in range(PACK):
-            (bias_on_scalar if s < 2 else bias_on_vector)(y_b[:, s, :], s, banks_b[s // 2][:, s % 2, :])
-        nc.scalar.dma_start(out=y_rows[:, :, c3b:], in_=y_b[:])
-        quantize_y(y_rounded[1][:], CHUNK, CHUNK)
-        round_y(nc.vector.tensor_copy, last_rounded[:, COLUMNS:], y_b[:])
-        quantize_y(y_rounded[2][:], c2, CHUNK)
-        nc.sync.dma_start(out=y_words[:, :c3a], in_=y_codes[:, :c3a].bitcast(I32))
-        quantize_y(last_rounded[:], c3a, CHUNK)
-        nc.sync.dma_start(out=y_words[:, c3a:], in_=y_codes[:, c3a:].bitcast(I32))
+            (bias_on_scalar if s < 2 else bias_on_vector)(y_last[:, s, UNIT:], s, columns[1][s])
+        round_y(nc.scalar.copy, last_rounded[:, :COLUMNS], y_last[:, :, :UNIT])
+        nc.sync.dma_start(out=y_rows[:, :, c3a:], in_=y_last[:])
+        last_codes = held.tile([P, 2 * CHUNK], U32, name="last_codes", align_bytes=ALIGN)
+        quantize_y(y_rounded[2][:], c2, last_codes[:, :CHUNK])
+        round_y(nc.vector.tensor_copy, last_rounded[:, COLUMNS:], y_last[:, :, UNIT:])
+        quantize_y(last_rounded[:], c3a, last_codes[:, CHUNK:])
+        nc.sync.dma_start(out=y_words[:, c2:], in_=last_codes[:].bitcast(I32))
         for q in range(QUADS):
             queue = nc.scalar if q % 2 == 0 else nc.sync
             queue.dma_start(

@@ -74,7 +74,7 @@ def tile_list_opcode_trigram_families_kernel(
         HALF = 2 * PASS * 2
         Y_BYTES = PACK * CHUNK * WORD
         extras = {
-            1: [("wf", 0, HALF)], 2: [("wf", 1, HALF)], 4: [("wf", 2, HALF)], 6: [("wf", 3, HALF)],
+            1: [("wf0", 1, 0)], 3: [("wf", 2, HALF)], 5: [("wf", 3, HALF)],
             9: [("bias", 0, Y_BYTES)], 11: [("bias", 1, Y_BYTES)],
             10: [("round", 0, Y_BYTES // 2)], 12: [("round", 1, Y_BYTES // 2)], 15: [("bias", 2, Y_BYTES)],
         }
@@ -84,7 +84,7 @@ def tile_list_opcode_trigram_families_kernel(
             8: [("w", W2, c2, CHUNK)], 9: [("w", W3, c3b, UNIT)],
             11: [("s", W1, c3a, CHUNK), ("w", W1, c3a, UNIT)], 12: [("s", W2, c3a, CHUNK), ("w", W2, c3a, UNIT)], 13: [("w", W1, c3b, UNIT)], 14: [("w", W2, c3b, UNIT)],
         }
-        wf_quantisers = {2: [0, 1], 3: [2, 3]}
+        wf_quantisers = {2: [0], 3: [2, 3]}
         burst_units = [[3, 4, 5]] + [[2 * q + 4, 2 * q + 5] for q in range(1, PAIRS)] + [[UNITS]]
 
         def first_max_bytes(k):
@@ -93,7 +93,7 @@ def tile_list_opcode_trigram_families_kernel(
         def burst_bytes(q):
             size = sum(first_max_bytes(k) * (k < UNITS) + UNIT_BYTES for k in burst_units[q])
             size = size + sum(n * (WORD if kind == "w" else 1) for k in burst_units[q] for kind, i, first, n in gathers.get(k, []))
-            size = size + (len(wf_quantisers.get(q, [])) + 1) * PASS // 2 + (q == PAIRS) * 3 * UNIT_BYTES
+            size = size + 3 * PASS // 2 + (q == PAIRS) * 3 * UNIT_BYTES
             return max(size, (2 + 4 * (q in wf_quantisers)) * UNIT_BYTES)
 
         table_scales = held.tile([P, T], U8, name="table_scales", align_bytes=ALIGN)
@@ -104,7 +104,8 @@ def tile_list_opcode_trigram_families_kernel(
         lists = [held.tile([P, S // PER_COLUMN], U16, name=f"list{i}") for i in range(3)]
         table_words = held.tile([P, T], I32, name="table_words", align_bytes=ALIGN)
         weight_bytes = PACK * PASS * WORD
-        w1_raw = [held.tile([P, PACK * PASS], F32, name="w1_raw0")]
+        raw_place = fresh(weight_bytes)
+        w1_raw = [at(raw_place, [P, PACK * PASS], F32, "w1_raw0")]
         size = max(burst_bytes(0), weight_bytes)
         w1_raw.append(at(open_room("burst0", size), [P, size // WORD], F32, "w1_raw1"))
         w2_raw = held.tile([P, H // 2], I32, name="w2_raw")
@@ -113,10 +114,12 @@ def tile_list_opcode_trigram_families_kernel(
         for q in range(PAIRS):
             size = burst_bytes(q + 1)
             pairs[q] = at(open_room(f"burst{q + 1}", size), [P, size // WORD], F32, f"silu_pair{q}")
-        wf_raw = [
-            pairs[1 + g][:, 2 * COLUMNS : 2 * COLUMNS + PACK * N].rearrange("p (t n) -> p t n", t=PACK)
-            for g in range(GROUPS)
-        ]
+        def wf_place(q, width):
+            return pairs[q][:, 2 * COLUMNS : 2 * COLUMNS + PACK * width].rearrange("p (t n) -> p t n", t=PACK)
+
+        early_wf = at(fresh(weight_bytes // 2), [P, PACK, N // 2], F32, "wf_raw_early")
+        h_offset = fresh(3 * HALF)
+        wf_raw = [[early_wf[:], wf_place(1, N // 2)], wf_place(2, N)]
         gains = held.tile([P, GROUPS, PACK], F32, name="gains")
         bias = held.tile([P, PACK], F32, name="bias")
 
@@ -153,7 +156,8 @@ def tile_list_opcode_trigram_families_kernel(
         load_scale_rows(raw_scales[:, H:], w2_scales[0])
         nc.sync.dma_start(out=w3_raw[1][:], in_=w3_rows[:, PASS:])
         load_w1(1)
-        nc.sync.dma_start(out=wf_raw[0], in_=wf_rows[0])
+        for half in range(2):
+            nc.sync.dma_start(out=wf_raw[0][half], in_=wf_rows[0][:, :, half * N // 2 : (half + 1) * N // 2])
         nc.sync.dma_start(out=bias[:], in_=bf.rearrange("(p s) -> p s", s=PACK))
         nc.sync.dma_start(out=wf_raw[1], in_=wf_rows[1])
 
@@ -205,7 +209,7 @@ def tile_list_opcode_trigram_families_kernel(
         turning = psum.tile([P, GROUPS, P], F32, name="logits")
         for g in range(GROUPS):
             nc.tensor.transpose(turning[:, g, :], wide_gains[:, g, : P // PACK].rearrange("p j t -> p (j t)"), identity[:])
-        turned_gains = held.tile([P, GROUPS, P], F32, name="turned_gains")
+        turned_gains = at(raw_place, [P, GROUPS, P], F32, "turned_gains")
         nc.scalar.copy(out=turned_gains[:], in_=turning[:])
         w2_codes = held.tile([P, 2 * H], U8, name="w2_codes", align_bytes=ALIGN)
         reorder_columns(nc.scalar.copy, w2_codes[:].bitcast(U16), w2_raw[:].bitcast(U16), 8)
@@ -213,7 +217,6 @@ def tile_list_opcode_trigram_families_kernel(
         reorder_columns(nc.gpsimd.tensor_copy, scales_q[W2][:], raw_scales[:, H:], 16)
         reorder_columns(nc.gpsimd.tensor_copy, w3_codes[1][:].bitcast(I32), w3_raw[1][:], 4)
 
-        h_offset = fresh(PASS * PACK * 2)
         w1_second = at(h_offset, [P, PASS * PACK], BF16, "w1_second")
         nc.gpsimd.tensor_copy(
             out=w1_second[:].rearrange("p (t m j) -> p m t j", t=PACK, j=PACK),
@@ -246,7 +249,7 @@ def tile_list_opcode_trigram_families_kernel(
         def by_pairs(values):
             return values.rearrange("p (c t i) -> p c t i", t=PACK, i=2)
 
-        copied, first_maxima, silus = {}, {}, {}
+        copied, first_maxima, silus, silu_place = {}, {}, {}, {}
         copy_place = {k: fresh(UNIT_BYTES) for k in range(COPY_AHEAD)}
 
         def copy_out(k):
@@ -267,7 +270,8 @@ def tile_list_opcode_trigram_families_kernel(
             if k < 2 * PAIRS:
                 silus[k] = pairs[k // 2][:, k % 2 * COLUMNS : (k % 2 + 1) * COLUMNS]
             else:
-                silus[k] = held.tile([P, COLUMNS], F32, name=f"silu{k}")[:]
+                silu_place[k] = fresh(2 * UNIT_BYTES)
+                silus[k] = at(silu_place[k], [P, 2 * COLUMNS], F32, f"silu{k}")[:, :COLUMNS]
 
         y_scales = held.tile([P, S], U8, name="y_scales", align_bytes=ALIGN)
         y_rows = out_0.rearrange("(p s) j -> p s j", s=PACK)
@@ -280,6 +284,13 @@ def tile_list_opcode_trigram_families_kernel(
             nc.scalar.copy(
                 out=wf_rounded[index][:].rearrange("p (s m t) -> p m t s", s=2, t=PACK),
                 in_=wf_raw[g].rearrange("p t (m s) -> p m t s", s=PACK)[:, :, :, 2 * half : 2 * half + 2],
+            )
+
+        def round_wf_columns(copy, half, walk):
+            words = wf_rounded[0][:].rearrange("p (s m t) -> p s m t", s=PACK, t=PACK)[:, :, half * P // 2 : (half + 1) * P // 2, :]
+            copy(
+                out=words.rearrange("p s m t -> " + walk),
+                in_=wf_raw[0][half].rearrange("p t (m s) -> " + walk, s=PACK),
             )
 
         def bias_on_scalar(out, s, bank):
@@ -326,7 +337,7 @@ def tile_list_opcode_trigram_families_kernel(
             if k + COPY_AHEAD < UNITS:
                 copy_out(k + COPY_AHEAD)
             for kind, index, size in extras.get(k, []):
-                {"wf": round_wf, "bias": add_bias, "round": round_chunk}[kind](index, behind(f"max{k}", size))
+                {"wf0": lambda half, offset: round_wf_columns(nc.scalar.copy, half, "p m t s"), "wf": round_wf, "bias": add_bias, "round": round_chunk}[kind](index, behind(f"max{k}", size))
 
         def gain_of(k):
             return wide_gains[:, order[k][1]].rearrange("p j t -> p (j t)")
@@ -334,15 +345,17 @@ def tile_list_opcode_trigram_families_kernel(
         h_rounded = {}
 
         def pair_gain(q):
-            h_rounded[q] = at(h_offset, [P, 2, COLUMNS], BF16, f"h_pair{q}")
+            reach = ALIGN if q == 0 else 0
+            tile = at(h_offset - reach, [P, reach // 2 + 2 * COLUMNS], BF16, f"h_pair{q}")
+            h_rounded[q] = tile[:, reach // 2 :]
             nc.gpsimd.tensor_tensor(
-                out=h_rounded[q][:], in0=pairs[q][:, : 2 * COLUMNS].rearrange("p (u c) -> p u c", u=2),
+                out=h_rounded[q].rearrange("p (u c) -> p u c", u=2), in0=pairs[q][:, : 2 * COLUMNS].rearrange("p (u c) -> p u c", u=2),
                 in1=gain_of(2 * q).unsqueeze(1).to_broadcast([P, 2, COLUMNS]), op=ALU.mult,
             )
 
         def second_pass(out, g, s, h, start, stop):
-            codes, scales = wf_q[2 * g + s // 2]
-            cols = slice(s % 2 * P, (s % 2 + 1) * P)
+            codes, scales = wf_q[0] if g == 0 else wf_q[2 + s // 2]
+            cols = slice(s * P, (s + 1) * P) if g == 0 else slice(s % 2 * P, (s % 2 + 1) * P)
             nc.tensor.matmul_mx(
                 out=out, lhsT=codes[:, cols].bitcast(FP8X4), lhsT_scale=scales[:, cols],
                 rhs=h[0][:].bitcast(FP8X4), rhs_scale=h[1][:], start=start, stop=stop,
@@ -356,6 +369,7 @@ def tile_list_opcode_trigram_families_kernel(
                     for g in range(GROUPS):
                         second_pass(logits[c][b][:, e, :], g, 2 * b + e, h_q[(c, g)], g == 0, g == GROUPS - 1)
 
+        wf_rounded[0] = at(h_offset + HALF, [P, PASS * PACK], BF16, "wf_rounded0")
         for k in range(COPY_AHEAD):
             copy_out(k)
         first_max(0, None)
@@ -368,11 +382,12 @@ def tile_list_opcode_trigram_families_kernel(
             room = f"burst{q}"
             if q == 0:
                 w1_q[1] = quantize(w1_second[:], "w1_1")
+                round_wf_columns(nc.gpsimd.tensor_copy, 0, "p m s t")
             else:
                 for index in wf_quantisers.get(q, []):
-                    wf_q[index] = quantize(wf_rounded[index][:], f"wf{index}", behind(room, PASS // 2))
+                    wf_q[index] = quantize(wf_rounded[index][:], f"wf{index}", behind(room, wf_rounded[index].shape[1] // PACK))
                 start, g = order[2 * q - 2]
-                h_q[(start // CHUNK, g)] = quantize(h_rounded[q - 1][:].rearrange("p u c -> p (u c)"), f"h{q - 1}", behind(room, CHUNK))
+                h_q[(start // CHUNK, g)] = quantize(h_rounded[q - 1], f"h{q - 1}", behind(room, CHUNK))
                 if g == GROUPS - 1:
                     second_product(start // CHUNK)
             if q < PAIRS:
@@ -398,7 +413,7 @@ def tile_list_opcode_trigram_families_kernel(
             )
 
         def last_quantize(k):
-            h_q[k] = quantize(h_last[k], f"h_last{k}")
+            h_q[k] = quantize(h_last[k], f"h_last{k}", silu_place[b0] if k == a0 else None)
 
         bank_gains = psum.tile([P, GROUPS, P], F32, name=f"first{COPIED}")
         for g in range(GROUPS):
@@ -414,21 +429,22 @@ def tile_list_opcode_trigram_families_kernel(
                 per_bank = PACK if half == 0 else 2
                 second_pass(
                     columns[half][s], g, s, h_q[k],
-                    g == 0 and s % per_bank == 0, g == GROUPS - 1 and s % per_bank == per_bank - 1,
+                    k in (a1, b0) and s % per_bank == 0, k in (a0, b1) and s % per_bank == per_bank - 1,
                 )
 
         h_last[a0] = at(h_offset, [P, COLUMNS], BF16, "h_last_gpsimd")[:]
         nc.gpsimd.tensor_tensor(out=h_last[a0], in0=silus[a0], in1=gain_of(a0), op=ALU.mult)
         last_gain(a1)
         last_gain(b0)
-        last_product(a0)
         last_product(a1)
         last_gain(b1)
-        last_product(b0)
-        store_codes(0, h_place[a1])
-        last_product(b1)
-        store_codes(1, h_place[b0])
-        y_rounded[2] = at(h_place[b0] + CHUNK * WORD, [P, CHUNK * PACK], BF16, "y_rounded2")
+        for k in (a0, b0, b1):
+            last_product(k)
+        early_codes = at(silu_place[b1], [P, 2 * CHUNK], U32, "early_codes")
+        for c in range(2):
+            quantize_y(y_rounded[c][:], c * CHUNK, early_codes[:, c * CHUNK : (c + 1) * CHUNK])
+        nc.sync.dma_start(out=y_words[:, :c2], in_=early_codes[:].bitcast(I32))
+        y_rounded[2] = at(silu_place[b1] + UNIT_BYTES, [P, CHUNK * PACK], BF16, "y_rounded2")
         round_y(nc.vector.tensor_copy, y_rounded[2][:], y[2][:])
 
         y_last = held.tile([P, PACK, CHUNK], F32, name="y_last")
@@ -437,10 +453,10 @@ def tile_list_opcode_trigram_families_kernel(
         last_rounded = held.tile([P, 2 * COLUMNS], BF16, name="last_rounded", align_bytes=ALIGN)
         for s in range(PACK):
             (bias_on_scalar if s < 2 else bias_on_vector)(y_last[:, s, UNIT:], s, columns[1][s])
-        round_y(nc.scalar.copy, last_rounded[:, :COLUMNS], y_last[:, :, :UNIT])
         nc.sync.dma_start(out=y_rows[:, :, c3a:], in_=y_last[:])
         last_codes = held.tile([P, 2 * CHUNK], U32, name="last_codes", align_bytes=ALIGN)
         quantize_y(y_rounded[2][:], c2, last_codes[:, :CHUNK])
+        round_y(nc.vector.tensor_copy, last_rounded[:, :COLUMNS], y_last[:, :, :UNIT])
         round_y(nc.vector.tensor_copy, last_rounded[:, COLUMNS:], y_last[:, :, UNIT:])
         quantize_y(last_rounded[:], c3a, last_codes[:, CHUNK:])
         nc.sync.dma_start(out=y_words[:, c2:], in_=last_codes[:].bitcast(I32))

from contextlib import ExitStack

import concourse.mybir as mybir
from concourse.masks import make_identity

K, T, S, H, N = 512, 2048, 1024, 1024, 512
FLOPS = 2 * S * (3 * K * H + H * N)

F32 = mybir.dt.float32
BF16 = mybir.dt.bfloat16
I32 = mybir.dt.int32
U32 = mybir.dt.uint32
U16 = mybir.dt.uint16
U8 = mybir.dt.uint8
FP8X4 = mybir.dt.float8_e4m3fn_x4
FP4X4 = mybir.dt.float4_e2m1fn_x4
ACT = mybir.ActivationFunctionType
ALU = mybir.AluOpType

P = 128
PACK = 4
PASS = P * PACK
GROUPS = H // PASS
QUADS = 4
PER_COLUMN = 16
WORD = 4
ALIGN = 64
UNIT = 128
COLUMNS = PACK * UNIT
UNIT_BYTES = COLUMNS * WORD
CHUNK = 256
UNITS = GROUPS * S // UNIT
W1, W2, W3 = 0, 1, 2
COPIED, FIRST, SECOND = W3, W1, W2
COPY_AHEAD = 6
PAIRS = 6


def tile_list_opcode_trigram_families_kernel(
    tc, tab_words, tab_scales, offs, offs2, offs3, w1, w2_words, w2_scales, w3_words, w3_scales, gain, wf, bf,
    out_0, out_1, out_2,
):
    nc = tc.nc
    with ExitStack() as ctx:
        held = ctx.enter_context(tc.tile_pool(name="held", bufs=1))
        placed = ctx.enter_context(tc.tile_pool(name="placed", bufs=1))
        psum = ctx.enter_context(tc.psum_pool(name="psum", bufs=2))

        top = [0]

        def fresh(size):
            top[0] = top[0] + size
            return top[0] - size

        rooms = {}

        def open_room(name, size):
            start = fresh(size)
            rooms[name] = [start, start + size]
            return start

        def behind(name, size):
            rooms[name][0] = rooms[name][0] + size
            assert rooms[name][0] <= rooms[name][1]
            return rooms[name][0] - size

        def at(offset, shape, dtype, name):
            return placed.tile(shape, dtype, name=name, align_bytes=ALIGN, offset=offset)

        order = [(c * CHUNK + j, g) for g in range(GROUPS) for c in (0, 1) for j in (0, UNIT)]
        order.extend((2 * CHUNK + j, g) for g in range(GROUPS) for j in (0, UNIT))
        order.extend((3 * CHUNK + j, g) for j in (0, UNIT) for g in range(GROUPS))

        HALF = 2 * PASS * 2
        Y_BYTES = PACK * CHUNK * WORD
        extras = {
            1: [("wf0", 1, 0)], 3: [("wf", 2, HALF)], 5: [("wf", 3, HALF)],
            9: [("bias", 0, Y_BYTES)], 11: [("bias", 1, Y_BYTES)],
            10: [("round", 0, Y_BYTES // 2)], 12: [("round", 1, Y_BYTES // 2)], 15: [("bias", 2, Y_BYTES)],
        }
        c2, c3a, c3b = 2 * CHUNK, 3 * CHUNK, 3 * CHUNK + UNIT
        gathers = {
            3: [("w", W3, c2, CHUNK)], 5: [("s", W2, c2, CHUNK)], 6: [("w", W1, c2, CHUNK)], 7: [("w", W3, c3a, UNIT)],
            8: [("w", W2, c2, CHUNK)], 9: [("w", W3, c3b, UNIT)],
            11: [("s", W1, c3a, CHUNK), ("w", W1, c3a, UNIT)], 12: [("s", W2, c3a, CHUNK), ("w", W2, c3a, UNIT)], 13: [("w", W1, c3b, UNIT)], 14: [("w", W2, c3b, UNIT)],
        }
        wf_quantisers = {2: [0], 3: [2, 3]}
        burst_units = [[3, 4, 5]] + [[2 * q + 4, 2 * q + 5] for q in range(1, PAIRS)] + [[UNITS]]

        def first_max_bytes(k):
            return UNIT_BYTES + sum(size for kind, index, size in extras.get(k, []))

        def burst_bytes(q):
            size = sum(first_max_bytes(k) * (k < UNITS) + UNIT_BYTES for k in burst_units[q])
            size = size + sum(n * (WORD if kind == "w" else 1) for k in burst_units[q] for kind, i, first, n in gathers.get(k, []))
            size = size + 3 * PASS // 2 + (q == PAIRS) * 3 * UNIT_BYTES
            return max(size, (2 + 4 * (q in wf_quantisers)) * UNIT_BYTES)

        table_scales = held.tile([P, T], U8, name="table_scales", align_bytes=ALIGN)
        nc.gpsimd.memset(table_scales[:].bitcast(I32), 0)
        raw_scales = held.tile([P, 2 * H], U8, name="raw_scales", align_bytes=ALIGN)
        nc.vector.memset(raw_scales[:].bitcast(I32), 0)

        lists = [held.tile([P, S // PER_COLUMN], U16, name=f"list{i}") for i in range(3)]
        table_words = held.tile([P, T], I32, name="table_words", align_bytes=ALIGN)
        weight_bytes = PACK * PASS * WORD
        raw_place = fresh(weight_bytes)
        w1_raw = [at(raw_place, [P, PACK * PASS], F32, "w1_raw0")]
        size = max(burst_bytes(0), weight_bytes)
        w1_raw.append(at(open_room("burst0", size), [P, size // WORD], F32, "w1_raw1"))
        w2_raw = held.tile([P, H // 2], I32, name="w2_raw")
        w3_raw = [held.tile([P, PASS], I32, name=f"w3_raw{g}") for g in range(GROUPS)]
        pairs = {}
        for q in range(PAIRS):
            size = burst_bytes(q + 1)
            pairs[q] = at(open_room(f"burst{q + 1}", size), [P, size // WORD], F32, f"silu_pair{q}")
        def wf_place(q, width):
            return pairs[q][:, 2 * COLUMNS : 2 * COLUMNS + PACK * width].rearrange("p (t n) -> p t n", t=PACK)

        early_wf = at(fresh(weight_bytes // 2), [P, PACK, N // 2], F32, "wf_raw_early")
        h_offset = fresh(3 * HALF)
        wf_raw = [[early_wf[:], wf_place(1, N // 2)], wf_place(2, N)]
        gains = held.tile([P, GROUPS, PACK], F32, name="gains")
        bias = held.tile([P, PACK], F32, name="bias")

        w1_rows = w1.rearrange("(p j) r -> p j r", j=PACK)
        wf_rows = wf.rearrange("(g p t) n -> g p t n", g=GROUPS, t=PACK)

        def load_scale_rows(dst, rows):
            for q in range(QUADS):
                nc.sync.dma_start(
                    out=dst[32 * q : 32 * q + 4, :].bitcast(I32), in_=rows[4 * q : 4 * q + 4, :].bitcast(I32)
                )

        def w1_values(g):
            return w1_raw[g][:, : PACK * PASS].rearrange("p (j r) -> p j r", j=PACK)

        def load_w1(g):
            nc.sync.dma_start(out=w1_values(g), in_=w1_rows[:, :, g * PASS : (g + 1) * PASS])

        warm = held.tile([P, 2], F32, name="warm")
        nc.gpsimd.memset(warm[:, 0:1], 0.0)
        nc.scalar.activation(out=warm[:, 1:2], in_=warm[:, 0:1], func=ACT.Silu)

        nc.sync.dma_start(lists[W3][:], offs3)
        load_scale_rows(table_scales[:], tab_scales[0])
        nc.sync.dma_start(lists[W1][:], offs)
        nc.sync.dma_start(out=gains[:], in_=gain.rearrange("(g p t) -> p g t", g=GROUPS, t=PACK))
        load_w1(0)
        nc.sync.dma_start(lists[W2][:], offs2)
        load_scale_rows(raw_scales[:, :H], w3_scales[0])
        w3_rows = w3_words[0].rearrange("p e i -> p (e i)").bitcast(I32)
        nc.sync.dma_start(out=w3_raw[0][:], in_=w3_rows[:, :PASS])
        nc.sync.dma_start(out=table_words[:], in_=tab_words[0].rearrange("p t i -> p (t i)").bitcast(I32))
        nc.sync.dma_start(out=w2_raw[:], in_=w2_words[0].bitcast(I32))
        load_scale_rows(raw_scales[:, H:], w2_scales[0])
        nc.sync.dma_start(out=w3_raw[1][:], in_=w3_rows[:, PASS:])
        load_w1(1)
        for half in range(2):
            nc.sync.dma_start(out=wf_raw[0][half], in_=wf_rows[0][:, :, half * N // 2 : (half + 1) * N // 2])
        nc.sync.dma_start(out=bias[:], in_=bf.rearrange("(p s) -> p s", s=PACK))
        nc.sync.dma_start(out=wf_raw[1], in_=wf_rows[1])

        picked = {}

        def gather(kind, i, first, n, offset=None):
            dtype, window = (U32, table_words[:].bitcast(U32)) if kind == "w" else (U8, table_scales[:])
            size = n * (WORD if kind == "w" else 1)
            tile = at(fresh(size) if offset is None else offset, [P, n], dtype, f"picked_{kind}{i}_{first}")
            entries = lists[i][:, first // PER_COLUMN : (first + n) // PER_COLUMN]
            nc.vector.tensor_copy(tile[:], window.indirect(entries))
            for j in range(0, n, UNIT):
                picked[(kind, i, first + j)] = tile[:, j : j + UNIT]

        def quantize(rounded, name, offset=None):
            width = rounded.shape[1] // PACK
            codes = held.tile([P, width], U32, name=f"{name}_codes", align_bytes=ALIGN)
            scales = at(fresh(width) if offset is None else offset, [P, width], U8, f"{name}_scales")
            nc.vector.quantize_mx(out=codes[:].bitcast(FP8X4), scales=scales[:], in_=rounded)
            return codes, scales

        def reorder_columns(copy, dst, src, per_line):
            copy(
                out=dst.rearrange("p (g t c i) -> p g c t i", c=P // per_line, t=PACK, i=per_line),
                in_=src.rearrange("p (g c i t) -> p g c t i", c=P // per_line, t=PACK, i=per_line),
            )

        w1_q, wf_q, wf_rounded = {}, {}, {}
        gather("s", W3, 0, S)
        gather("s", W1, 0, 3 * CHUNK)
        gather("s", W2, 0, 2 * CHUNK)

        w1_first = held.tile([P, PASS * PACK], BF16, name="w1_first", align_bytes=ALIGN)
        nc.scalar.copy(
            out=w1_first[:].rearrange("p (t m j) -> p m j t", t=PACK, j=PACK),
            in_=w1_values(0).rearrange("p j (m t) -> p m j t", t=PACK),
        )
        w1_q[0] = quantize(w1_first[:], "w1_0")

        scales_q = {}
        scales_q[W3] = held.tile([P, H], U8, name="w3_scales", align_bytes=ALIGN)
        reorder_columns(nc.gpsimd.tensor_copy, scales_q[W3][:], raw_scales[:, :H], 16)
        w3_codes = [held.tile([P, PASS], U32, name=f"w3_codes{g}", align_bytes=ALIGN) for g in range(GROUPS)]
        reorder_columns(nc.gpsimd.tensor_copy, w3_codes[0][:].bitcast(I32), w3_raw[0][:], 4)
        wide_gains = held.tile([P, GROUPS, UNIT, PACK], F32, name="wide_gains")
        nc.scalar.copy(out=wide_gains[:], in_=gains[:].unsqueeze(2).to_broadcast([P, GROUPS, UNIT, PACK]))
        identity = held.tile([P, P], F32, name="identity")
        make_identity(nc, identity[:])
        turning = psum.tile([P, GROUPS, P], F32, name="logits")
        for g in range(GROUPS):
            nc.tensor.transpose(turning[:, g, :], wide_gains[:, g, : P // PACK].rearrange("p j t -> p (j t)"), identity[:])
        turned_gains = at(raw_place, [P, GROUPS, P], F32, "turned_gains")
        nc.scalar.copy(out=turned_gains[:], in_=turning[:])
        w2_codes = held.tile([P, 2 * H], U8, name="w2_codes", align_bytes=ALIGN)
        reorder_columns(nc.scalar.copy, w2_codes[:].bitcast(U16), w2_raw[:].bitcast(U16), 8)
        scales_q[W2] = held.tile([P, H], U8, name="w2_scales", align_bytes=ALIGN)
        reorder_columns(nc.gpsimd.tensor_copy, scales_q[W2][:], raw_scales[:, H:], 16)
        reorder_columns(nc.gpsimd.tensor_copy, w3_codes[1][:].bitcast(I32), w3_raw[1][:], 4)

        w1_second = at(h_offset, [P, PASS * PACK], BF16, "w1_second")
        nc.gpsimd.tensor_copy(
            out=w1_second[:].rearrange("p (t m j) -> p m t j", t=PACK, j=PACK),
            in_=w1_values(1).rearrange("p j (m t) -> p m t j", t=PACK),
        )

        for i, first in ((W3, 0), (W1, 0), (W3, CHUNK), (W2, 0), (W1, CHUNK)):
            gather("w", i, first, CHUNK)

        def stationary(i, g, t):
            col = g * PASS + t * P
            if i == W1:
                return w1_q[g][0][:, t * P : (t + 1) * P].bitcast(FP8X4), w1_q[g][1][:, t * P : (t + 1) * P]
            if i == W2:
                return w2_codes[:, 2 * col : 2 * (col + P)].bitcast(FP4X4), scales_q[W2][:, col : col + P]
            return w3_codes[g][:, t * P : (t + 1) * P].bitcast(FP8X4), scales_q[W3][:, col : col + P]

        def first_product(i, k):
            start, g = order[k]
            bank = psum.tile([P, PACK, UNIT], F32, name=f"first{i}")
            for t in range(PACK):
                codes, scales = stationary(i, g, t)
                nc.tensor.matmul_mx(
                    out=bank[:, t, :], lhsT=codes, lhsT_scale=scales,
                    rhs=picked[("w", i, start)].bitcast(FP8X4), rhs_scale=picked[("s", i, start)],
                    start=True, stop=True,
                )
            return bank[:].rearrange("p t (c i) -> p c t i", i=2)

        def by_pairs(values):
            return values.rearrange("p (c t i) -> p c t i", t=PACK, i=2)

        copied, first_maxima, silus, silu_place = {}, {}, {}, {}
        copy_place = {k: fresh(UNIT_BYTES) for k in range(COPY_AHEAD)}

        def copy_out(k):
            bank = first_product(COPIED, k)
            copied[k] = at(copy_place[k], [P, COLUMNS], F32, f"copied{k}")
            nc.scalar.copy(out=by_pairs(copied[k][:]), in_=bank)

        def first_max(k, room):
            bank = first_product(FIRST, k)
            size = first_max_bytes(k)
            offset = fresh(size) if room is None else behind(room, size)
            rooms[f"max{k}"] = [offset + UNIT_BYTES, offset + size]
            copy_place[k + COPY_AHEAD] = offset
            first_maxima[k] = at(offset, [P, size // WORD], F32, f"first_max{k}")[:, :COLUMNS]
            nc.vector.tensor_tensor(out=by_pairs(first_maxima[k]), in0=bank, in1=by_pairs(copied[k][:]), op=ALU.max)

        def silu_tile(k):
            if k < 2 * PAIRS:
                silus[k] = pairs[k // 2][:, k % 2 * COLUMNS : (k % 2 + 1) * COLUMNS]
            else:
                silu_place[k] = fresh(2 * UNIT_BYTES)
                silus[k] = at(silu_place[k], [P, 2 * COLUMNS], F32, f"silu{k}")[:, :COLUMNS]

        y_scales = held.tile([P, S], U8, name="y_scales", align_bytes=ALIGN)
        y_rows = out_0.rearrange("(p s) j -> p s j", s=PACK)
        y_words = out_1[0].rearrange("p m t -> p (m t)").bitcast(I32)
        h_q, logits, y, y_rounded = {}, {}, {}, {}

        def round_wf(index, offset):
            g, half = divmod(index, 2)
            wf_rounded[index] = at(offset, [P, 2 * PASS], BF16, f"wf_rounded{index}")
            nc.scalar.copy(
                out=wf_rounded[index][:].rearrange("p (s m t) -> p m t s", s=2, t=PACK),
                in_=wf_raw[g].rearrange("p t (m s) -> p m t s", s=PACK)[:, :, :, 2 * half : 2 * half + 2],
            )

        def round_wf_columns(copy, half, walk):
            words = wf_rounded[0][:].rearrange("p (s m t) -> p s m t", s=PACK, t=PACK)[:, :, half * P // 2 : (half + 1) * P // 2, :]
            copy(
                out=words.rearrange("p s m t -> " + walk),
                in_=wf_raw[0][half].rearrange("p t (m s) -> " + walk, s=PACK),
            )

        def bias_on_scalar(out, s, bank):
            nc.scalar.activation(out=out, in_=bank, func=ACT.Identity, bias=bias[:, s : s + 1])

        def bias_on_vector(out, s, bank):
            nc.vector.tensor_scalar(out=out, in0=bank, scalar1=bias[:, s : s + 1], scalar2=None, op0=ALU.add)

        def add_bias(c, offset):
            y[c] = at(offset, [P, PACK, CHUNK], F32, f"y{c}")
            for s in range(PACK):
                bias_on_scalar(y[c][:, s, :], s, logits[c][s // 2][:, s % 2, :])
            nc.sync.dma_start(out=y_rows[:, :, c * CHUNK : (c + 1) * CHUNK], in_=y[c][:])

        def round_y(copy, rounded, values):
            copy(
                out=rounded.rearrange("p (c i s) -> p c s i", s=PACK, i=4),
                in_=values.rearrange("p s (c i) -> p c s i", i=4),
            )

        def round_chunk(c, offset):
            y_rounded[c] = at(offset, [P, CHUNK * PACK], BF16, f"y_rounded{c}")
            round_y(nc.scalar.copy, y_rounded[c][:], y[c][:])

        def quantize_y(rounded, first, codes):
            n = codes.shape[1]
            nc.vector.quantize_mx(out=codes.bitcast(FP8X4), scales=y_scales[:, first : first + n], in_=rounded)

        def store_codes(c, offset):
            codes = at(offset, [P, CHUNK], U32, f"y_codes{c}")
            quantize_y(y_rounded[c][:], c * CHUNK, codes[:])
            nc.sync.dma_start(out=y_words[:, c * CHUNK : (c + 1) * CHUNK], in_=codes[:].bitcast(I32))

        def second_max(k, room):
            bank = first_product(SECOND, k)
            m = at(fresh(UNIT_BYTES) if room is None else behind(room, UNIT_BYTES), [P, COLUMNS], F32, f"second_max{k}")
            nc.vector.tensor_tensor(out=by_pairs(m[:]), in0=bank, in1=by_pairs(first_maxima[k]), op=ALU.max)
            silu_tile(k)
            nc.scalar.activation(
                out=silus[k].rearrange("p (c i t) -> p c i t", t=PACK, i=2),
                in_=m[:].rearrange("p (c t i) -> p c i t", t=PACK, i=2),
                func=ACT.Silu,
            )
            if k + COPY_AHEAD < UNITS:
                copy_out(k + COPY_AHEAD)
            for kind, index, size in extras.get(k, []):
                {"wf0": lambda half, offset: round_wf_columns(nc.scalar.copy, half, "p m t s"), "wf": round_wf, "bias": add_bias, "round": round_chunk}[kind](index, behind(f"max{k}", size))

        def gain_of(k):
            return wide_gains[:, order[k][1]].rearrange("p j t -> p (j t)")

        h_rounded = {}

        def pair_gain(q):
            reach = ALIGN if q == 0 else 0
            tile = at(h_offset - reach, [P, reach // 2 + 2 * COLUMNS], BF16, f"h_pair{q}")
            h_rounded[q] = tile[:, reach // 2 :]
            nc.gpsimd.tensor_tensor(
                out=h_rounded[q].rearrange("p (u c) -> p u c", u=2), in0=pairs[q][:, : 2 * COLUMNS].rearrange("p (u c) -> p u c", u=2),
                in1=gain_of(2 * q).unsqueeze(1).to_broadcast([P, 2, COLUMNS]), op=ALU.mult,
            )

        def second_pass(out, g, s, h, start, stop):
            codes, scales = wf_q[0] if g == 0 else wf_q[2 + s // 2]
            cols = slice(s * P, (s + 1) * P) if g == 0 else slice(s % 2 * P, (s % 2 + 1) * P)
            nc.tensor.matmul_mx(
                out=out, lhsT=codes[:, cols].bitcast(FP8X4), lhsT_scale=scales[:, cols],
                rhs=h[0][:].bitcast(FP8X4), rhs_scale=h[1][:], start=start, stop=stop,
            )

        def second_product(c):
            logits[c] = []
            for b in range(2):
                logits[c].append(psum.tile([P, 2, CHUNK], F32, name="logits"))
                for e in range(2):
                    for g in range(GROUPS):
                        second_pass(logits[c][b][:, e, :], g, 2 * b + e, h_q[(c, g)], g == 0, g == GROUPS - 1)

        wf_rounded[0] = at(h_offset + HALF, [P, PASS * PACK], BF16, "wf_rounded0")
        for k in range(COPY_AHEAD):
            copy_out(k)
        first_max(0, None)
        first_max(1, None)
        second_max(0, None)
        gather("w", W2, CHUNK, CHUNK, copy_place[0])
        first_max(2, None)
        second_max(1, None)
        for q in range(PAIRS + 1):
            room = f"burst{q}"
            if q == 0:
                w1_q[1] = quantize(w1_second[:], "w1_1")
                round_wf_columns(nc.gpsimd.tensor_copy, 0, "p m s t")
            else:
                for index in wf_quantisers.get(q, []):
                    wf_q[index] = quantize(wf_rounded[index][:], f"wf{index}", behind(room, wf_rounded[index].shape[1] // PACK))
                start, g = order[2 * q - 2]
                h_q[(start // CHUNK, g)] = quantize(h_rounded[q - 1], f"h{q - 1}", behind(room, CHUNK))
                if g == GROUPS - 1:
                    second_product(start // CHUNK)
            if q < PAIRS:
                pair_gain(q)
            for k in burst_units[q]:
                for kind, i, first, n in gathers.get(k, []):
                    gather(kind, i, first, n, behind(room, n * (WORD if kind == "w" else 1)))
                if k < UNITS:
                    first_max(k, room)
                second_max(k - 1, room)

        a0, a1, b0, b1 = range(2 * PAIRS, UNITS)
        h_last, h_place = {}, {}

        def last_gain(k):
            place = behind(f"burst{PAIRS}", COLUMNS * 2 * (1 + 2 * (k == b0)))
            h_place[k] = place
            h_last[k] = at(place, [P, COLUMNS * (1 + (k == b0))], BF16, f"h_last{k}")[:, :COLUMNS]
            nc.vector.tensor_tensor(
                out=h_last[k].rearrange("p (u c) -> p u c", c=P),
                in0=bank_gains[:, order[k][1], :].unsqueeze(1).to_broadcast([P, PACK, P]),
                in1=silus[k].rearrange("p (u c) -> p u c", c=P), op=ALU.mult,
            )

        def last_quantize(k):
            h_q[k] = quantize(h_last[k], f"h_last{k}", silu_place[b0] if k == a0 else None)

        bank_gains = psum.tile([P, GROUPS, P], F32, name=f"first{COPIED}")
        for g in range(GROUPS):
            nc.tensor.transpose(bank_gains[:, g, :], turned_gains[:, g, :], identity[:])
        bank_a = psum.tile([P, PACK, UNIT], F32, name=f"first{COPIED}")
        banks_b = [psum.tile([P, 2, UNIT], F32, name=f"first{FIRST}") for b in range(2)]
        columns = [[bank_a[:, s, :] for s in range(PACK)], [banks_b[s // 2][:, s % 2, :] for s in range(PACK)]]

        def last_product(k):
            last_quantize(k)
            half, g = divmod(k - a0, GROUPS)
            for s in range(PACK):
                per_bank = PACK if half == 0 else 2
                second_pass(
                    columns[half][s], g, s, h_q[k],
                    k in (a1, b0) and s % per_bank == 0, k in (a0, b1) and s % per_bank == per_bank - 1,
                )

        h_last[a0] = at(h_offset, [P, COLUMNS], BF16, "h_last_gpsimd")[:]
        nc.gpsimd.tensor_tensor(out=h_last[a0], in0=silus[a0], in1=gain_of(a0), op=ALU.mult)
        last_gain(a1)
        last_gain(b0)
        last_product(a1)
        last_gain(b1)
        for k in (a0, b0, b1):
            last_product(k)
        early_codes = at(silu_place[b1], [P, 2 * CHUNK], U32, "early_codes")
        for c in range(2):
            quantize_y(y_rounded[c][:], c * CHUNK, early_codes[:, c * CHUNK : (c + 1) * CHUNK])
        nc.sync.dma_start(out=y_words[:, :c2], in_=early_codes[:].bitcast(I32))
        y_rounded[2] = at(silu_place[b1] + UNIT_BYTES, [P, CHUNK * PACK], BF16, "y_rounded2")
        round_y(nc.vector.tensor_copy, y_rounded[2][:], y[2][:])

        y_last = held.tile([P, PACK, CHUNK], F32, name="y_last")
        for s in range(PACK):
            bias_on_scalar(y_last[:, s, :UNIT], s, columns[0][s])
        last_rounded = held.tile([P, 2 * COLUMNS], BF16, name="last_rounded", align_bytes=ALIGN)
        for s in range(PACK):
            (bias_on_scalar if s < 2 else bias_on_vector)(y_last[:, s, UNIT:], s, columns[1][s])
        nc.sync.dma_start(out=y_rows[:, :, c3a:], in_=y_last[:])
        last_codes = held.tile([P, 2 * CHUNK], U32, name="last_codes", align_bytes=ALIGN)
        quantize_y(y_rounded[2][:], c2, last_codes[:, :CHUNK])
        round_y(nc.vector.tensor_copy, last_rounded[:, :COLUMNS], y_last[:, :, :UNIT])
        round_y(nc.vector.tensor_copy, last_rounded[:, COLUMNS:], y_last[:, :, UNIT:])
        quantize_y(last_rounded[:], c3a, last_codes[:, CHUNK:])
        nc.sync.dma_start(out=y_words[:, c2:], in_=last_codes[:].bitcast(I32))
        for q in range(QUADS):
            queue = nc.scalar if q % 2 == 0 else nc.sync
            queue.dma_start(
                out=out_2[0, 4 * q : 4 * q + 4, :].bitcast(I32), in_=y_scales[32 * q : 32 * q + 4, :].bitcast(I32)
            )
